import numpy as np
import ml_dtypes


def mxq(x, axis, fmt="e4m3"):
    dtype, down = {"e4m3": (ml_dtypes.float8_e4m3fn, 7), "e5m2": (ml_dtypes.float8_e5m2, 14)}[fmt]
    v = np.moveaxis(np.asarray(x, np.float32).astype(ml_dtypes.bfloat16).astype(np.float64), axis, -1)
    blocks = v.reshape(v.shape[:-1] + (-1, 32))
    amax = np.abs(blocks).max(-1, keepdims=True)
    byte = np.maximum(np.where(amax > 0, np.frexp(amax)[1] - 1 + 127, 0) - down, 1)
    scale = np.exp2(byte - 127.0)
    codes = (blocks / scale).astype(np.float32).astype(dtype).astype(np.float64)
    return np.moveaxis((codes * scale).reshape(v.shape), -1, axis)


WIDE = False


def mx_kscale(k):
    if not WIDE:
        return np.ones(k)
    levels = np.array([10, -10, 5, -5, 0])
    if k % 512:
        return np.exp2(np.random.permutation(np.resize(levels, k // 32))).repeat(32)
    a = np.empty((k // 512, 16))
    for p in range(k // 512):
        a[p, :8] = np.random.permutation(np.resize(levels, 8))
        for g in range(8):
            far = levels[np.abs(levels - a[p, g]) >= 10]
            a[p, g + 8] = far[np.random.randint(len(far))]
    return np.exp2(a.ravel()).repeat(32)


def f64(x):
    return np.asarray(x).astype(np.float64)


def striped(idx):
    return np.tile(idx.reshape(-1, 16).T, (8, 1)).astype(np.uint16)


def unstriped(offs):
    return offs[:16].T.reshape(-1).astype(np.int64)


E2M1 = np.array([0.0, 0.5, 1.0, 1.5, 2.0, 3.0, 4.0, 6.0, -0.0, -0.5, -1.0, -1.5, -2.0, -3.0, -4.0, -6.0])


def pack_weight(w, fmt):
    k, n = w.shape
    w = f64(np.asarray(w, np.float32).astype(ml_dtypes.bfloat16)).reshape(k // 32, 32, n)
    amax = np.abs(w).max(1)
    if fmt == "e4m3":
        byte = np.frexp(amax)[1] - 1 + 127 - 7
    else:
        mant, ex = np.frexp(amax / 6.0)
        byte = np.where(mant > 0.5, ex, ex - 1) + 127
    byte = np.clip(np.where(amax > 0, byte, 1), 1, 254)
    scaled = (w * np.exp2(127.0 - byte)[:, None, :]).reshape(k, n).astype(np.float32)
    by_word = np.ascontiguousarray(scaled.reshape(k // 512, 128, 4, n).transpose(0, 1, 3, 2))
    if fmt == "e4m3":
        words = by_word.astype(ml_dtypes.float8_e4m3fn).view(np.uint8)
    else:
        c = by_word.astype(ml_dtypes.float4_e2m1fn).view(np.uint8) & 0xF
        words = (c[..., 0::2] | (c[..., 1::2] << 4)).reshape(k // 512, 128, 2 * n)
    return np.ascontiguousarray(words), np.ascontiguousarray(byte.astype(np.uint8).reshape(k // 512, 16, n))


def unpack_weight(words, scales, fmt):
    g, _, n = scales.shape
    words = np.ascontiguousarray(words).reshape(g, 128, n, -1)
    if fmt == "e4m3":
        vals = words.view(ml_dtypes.float8_e4m3fn).astype(np.float64)
    else:
        nib = np.empty((g, 128, n, 4), np.uint8)
        nib[..., 0::2] = words & 0xF
        nib[..., 1::2] = words >> 4
        vals = E2M1[nib]
    vals = vals * np.repeat(np.exp2(scales.astype(np.float64) - 127.0), 8, axis=1)[..., None]
    return vals.transpose(0, 1, 3, 2).reshape(g * 512, n)


def gelu(v):
    return 0.5 * v * (1.0 + np.tanh(np.sqrt(2.0 / np.pi) * (v + 0.044715 * v**3)))


K, T, S, H, N = 1024, 2048, 1024, 512, 384

def setup_inputs():
    n = np.random.standard_normal
    s = mx_kscale(K)[:, None]
    u = mx_kscale(H)[:, None]
    tab_words, tab_scales = pack_weight(n((K, T)) * s, "e4m3")
    we_words, we_scales = pack_weight(n((K, H)) / np.sqrt(K) / s * u.T, "e4m3")
    wb_words, wb_scales = pack_weight(0.7 * n((K, H)) / np.sqrt(K) / s * u.T, "e2m1")
    return {
        "tab_words": tab_words, "tab_scales": tab_scales,
        "offs": striped(np.random.permutation(T)[:S]),
        "wr": (0.5 * n((K, H)) / np.sqrt(K) / s).astype(np.float32),
        "we_words": we_words, "we_scales": we_scales,
        "wb_words": wb_words, "wb_scales": wb_scales,
        "wo": (n((H, N)) / np.sqrt(H) / u).astype(np.float32),
        "bo": (0.5 * n(N)).astype(np.float32),
    }

def reference(tab_words, tab_scales, offs, wr, we_words, we_scales, wb_words, wb_scales, wo, bo):
    v = unpack_weight(tab_words, tab_scales, "e4m3")[:, unstriped(offs)]
    we = unpack_weight(we_words, we_scales, "e4m3")
    wb = unpack_weight(wb_words, wb_scales, "e2m1")
    rate = mxq(f64(wr), 0, "e4m3").T @ v
    expo = we.T @ v
    back = wb.T @ v
    h = np.exp(rate) * expo - back
    y = mxq(f64(wo), 0, "e4m3").T @ mxq(h, 0, "e4m3")
    return y + f64(bo)[:, None]

@@ -1,0 +1,254 @@
+from contextlib import ExitStack
+
+import concourse.mybir as mybir
+
+K, T, S, H, N = 1024, 2048, 1024, 512, 384
+FLOPS = 3 * 2 * K * H * S + 2 * H * N * S
+
+F32 = mybir.dt.float32
+BF16 = mybir.dt.bfloat16
+I32 = mybir.dt.int32
+U32 = mybir.dt.uint32
+U16 = mybir.dt.uint16
+U8 = mybir.dt.uint8
+FP8X4 = mybir.dt.float8_e4m3fn_x4
+FP4X4 = mybir.dt.float4_e2m1fn_x4
+ALU = mybir.AluOpType
+ACT = mybir.ActivationFunctionType
+
+P = 128
+PASSES = 2
+SLOTS = 4
+RUN = 8
+HALF = 512
+CHUNK = 256
+BANK = 512
+
+
+def tile_list_kmer_locus_enrichment_kernel(
+    tc, tab_words, tab_scales, offs, wr, we_words, we_scales, wb_words, wb_scales, wo, bo, out
+):
+    nc = tc.nc
+    with ExitStack() as ctx:
+        keep = ctx.enter_context(tc.tile_pool(name="keep", bufs=1))
+        ring = ctx.enter_context(tc.tile_pool(name="ring", bufs=2))
+        psum = ctx.enter_context(tc.psum_pool(name="psum", bufs=8))
+
+        def bank():
+            return psum.tile([P, BANK], F32, name="bank", tag="bank")
+
+        offsets = keep.tile([P, S // 16], U16, name="offsets")
+        nc.sync.dma_start(offsets[:], offs)
+
+        ts_win = keep.tile([P, T // 4], I32, name="ts_win", align_bytes=64)
+        tw_win = [keep.tile([P, T], I32, name=f"tw_win{a}", tag=f"table{a}", align_bytes=64) for a in range(PASSES)]
+        v_codes = [keep.tile([P, S], U32, name=f"v_codes{a}", align_bytes=64) for a in range(PASSES)]
+        v_scales = keep.tile([P, S], U8, name="v_scales", align_bytes=64)
+        v_scales1 = keep.tile([P, S // 4], I32, name="v_scales1", align_bytes=64)
+        wr_raw = [keep.tile([P, 4 * H], F32, name=f"wr_raw{a}", tag=f"stage{a}", align_bytes=64) for a in range(PASSES)]
+        wr_bf = [keep.tile([P, 4 * H], BF16, name=f"wr_bf{a}", align_bytes=64) for a in range(PASSES)]
+        wr_codes = [keep.tile([P, H], U32, name=f"wr_codes{a}", align_bytes=64) for a in range(PASSES)]
+        wr_scales = [keep.tile([P, H], U8, name=f"wr_scales{a}", align_bytes=64) for a in range(PASSES)]
+        ws_raw = keep.tile([P, 2, PASSES, H // 4], I32, name="ws_raw", align_bytes=64)
+        we_codes = keep.tile([P, PASSES * H], I32, name="we_codes", align_bytes=64)
+        wb_codes = keep.tile([P, PASSES * H // 2], I32, name="wb_codes", align_bytes=64)
+        wo_bf = keep.tile([P, N * SLOTS], BF16, name="wo_bf", align_bytes=64)
+        wo_codes = keep.tile([P, N], U32, name="wo_codes", align_bytes=64)
+        wo_scales = keep.tile([P, N], U8, name="wo_scales", align_bytes=64)
+        growth = keep.tile([P, SLOTS, S], F32, name="growth", align_bytes=64)
+        warm = keep.tile([P, 2], F32, name="warm", tag="small")
+
+        nc.vector.memset(ts_win[:], 0)
+        nc.vector.memset(warm[:, 0:1], 0.0)
+        nc.gpsimd.memset(ws_raw[:], 0)
+        nc.gpsimd.memset(v_scales1[:], 0)
+        for q in range(4):
+            nc.scalar.dma_start(
+                out=ts_win[32 * q : 32 * q + 8, :],
+                in_=tab_scales[:, 4 * q : 4 * q + 4, :].bitcast(I32),
+            )
+        nc.scalar.activation(warm[:, 1:2], warm[:, 0:1], ACT.Exp)
+        for a in range(PASSES):
+            nc.sync.dma_start(
+                out=wr_raw[a][:], in_=wr[512 * a : 512 * (a + 1), :].rearrange("(p i) c -> p (i c)", i=4)
+            )
+            nc.sync.dma_start(out=tw_win[a][:], in_=tab_words[a].rearrange("p t i -> p (t i)").bitcast(I32))
+        for w, scales in enumerate((we_scales, wb_scales)):
+            for q in range(4):
+                nc.gpsimd.dma_start(
+                    out=ws_raw[32 * q : 32 * q + 4, w, :, :],
+                    in_=scales[:, 4 * q : 4 * q + 4, :].rearrange("a r c -> r a c").bitcast(I32),
+                )
+        bias = keep.tile([P, N // P], F32, name="bias", tag="small")
+        with nc.allow_non_contiguous_dma(reason="one bias value a partition"):
+            nc.scalar.dma_start(out=bias[:], in_=bo.rearrange("(b p) -> p b", p=P))
+
+        def gather_scales():
+            nc.vector.tensor_copy(v_scales[:], ts_win[:].bitcast(U8).indirect(offsets[:]))
+            for q in range(4):
+                nc.gpsimd.dma_start(
+                    out=v_scales1[32 * q : 32 * q + 4, :], in_=v_scales[32 * q + 4 : 32 * q + 8, :].bitcast(I32)
+                )
+
+        def gather_words(a, lo, hi):
+            nc.vector.tensor_copy(
+                v_codes[a][:, lo:hi], tw_win[a][:].bitcast(U32).indirect(offsets[:, lo // 16 : hi // 16])
+            )
+
+        def cast_wr(a, t, engine_copy):
+            engine_copy(
+                wr_bf[a][:, 512 * t : 512 * (t + 1)].rearrange("p (g e i) -> p g e i", e=RUN, i=4),
+                wr_raw[a][:].rearrange("p (i g t e) -> p t g e i", i=4, t=SLOTS, e=RUN)[:, t],
+            )
+
+        def quantise_wr(a, t0, t1):
+            nc.vector.quantize_mx(
+                out=wr_codes[a][:, P * t0 : P * t1].bitcast(FP8X4),
+                scales=wr_scales[a][:, P * t0 : P * t1],
+                in_=wr_bf[a][:, 512 * t0 : 512 * t1],
+            )
+
+        def reorder(dst, src, run):
+            nc.vector.tensor_copy(
+                dst.rearrange("p (t x e) -> p t x e", t=SLOTS, e=run),
+                src.rearrange("p (x t e) -> p t x e", t=SLOTS, e=run),
+            )
+
+        def product(dst, codes, scales, a, lo, hi, unpacked=False):
+            if unpacked and a == 1:
+                plane = v_scales1[:, lo // 4 : hi // 4].bitcast(U8)
+            else:
+                plane = v_scales[4 * a : P, lo:hi]
+            nc.tensor.matmul_mx(
+                out=dst, lhsT=codes, lhsT_scale=scales,
+                rhs=v_codes[a][:, lo:hi].bitcast(FP8X4), rhs_scale=plane,
+                start=(a == 0), stop=(a == PASSES - 1),
+            )
+
+        def w_scale(w, a, t):
+            at = 128 * t + 32 * (2 * w + a)
+            return ws[:, at : at + 32].bitcast(U8)
+
+        gather_scales()
+        for t in range(SLOTS):
+            cast_wr(0, t, nc.scalar.copy)
+        w_raw = keep.tile([P, PASSES * (H + H // 2)], I32, name="w_raw", tag="stage0", align_bytes=64)
+        we_raw = w_raw[:, 0 : PASSES * H]
+        wb_raw = w_raw[:, PASSES * H :]
+        nc.sync.dma_start(out=we_raw.rearrange("p (a c) -> p a c", a=PASSES), in_=we_words.rearrange("a p c i -> p a (c i)").bitcast(I32))
+        nc.sync.dma_start(out=wb_raw.rearrange("p (a c) -> p a c", a=PASSES), in_=wb_words.rearrange("a p c -> p a c").bitcast(I32))
+        quantise_wr(0, 0, 4)
+        gather_words(0, 0, HALF)
+        gather_words(0, HALF, S)
+        rate = [[bank() for t in range(SLOTS)] for half in range(2)]
+
+        def rate_pass(a, half, t):
+            cols = slice(P * t, P * (t + 1))
+            product(rate[half][t][:], wr_codes[a][:, cols].bitcast(FP8X4), wr_scales[a][:, cols], a, HALF * half, HALF * (half + 1))
+
+        for half in range(2):
+            for t in range(SLOTS):
+                rate_pass(0, half, t)
+
+        cast_wr(1, 0, nc.scalar.copy)
+        cast_wr(1, 1, nc.scalar.copy)
+        cast_wr(1, 2, nc.scalar.copy)
+        cast_wr(1, 3, nc.vector.tensor_copy)
+        wo_raw = keep.tile([P, SLOTS, N], F32, name="wo_raw", tag="stage1", align_bytes=64)
+        for t in range(SLOTS):
+            nc.sync.dma_start(out=wo_raw[:, t, :], in_=wo.rearrange("(g t e) n -> t g e n", t=SLOTS, e=RUN)[t])
+        ws = keep.tile([P, 2 * PASSES * H // 4], I32, name="ws", tag="table0", align_bytes=64)
+        reorder(ws[:], ws_raw[:].rearrange("p w a c -> p (w a c)"), RUN // 4)
+        quantise_wr(1, 0, 4)
+        for half in range(2):
+            gather_words(1, HALF * half, HALF * (half + 1))
+            for t in range(SLOTS):
+                rate_pass(1, half, t)
+                nc.scalar.activation(growth[:, t, HALF * half : HALF * (half + 1)], rate[half][t][:], ACT.Exp)
+            if half == 0:
+                reorder(we_codes[:], we_raw, RUN)
+            else:
+                reorder(wb_codes[:], wb_raw, RUN // 2)
+
+        for b in range(N // P):
+            nc.scalar.copy(
+                wo_bf[:, 512 * b : 512 * (b + 1)].rearrange("p (n t) -> p n t", t=SLOTS),
+                wo_raw[:, :, P * b : P * (b + 1)].rearrange("p t n -> p n t"),
+            )
+
+        chunks = S // CHUNK
+        signal = {}
+        h_bf = {}
+        h_mx = {}
+
+        def exposure(c):
+            lo = CHUNK * c
+            signal[c] = ring.tile([P, 2, CHUNK, 2], F32, name="signal", align_bytes=64)
+            for u in range(2):
+                acc = bank()
+                for s in range(2):
+                    t = 2 * u + s
+                    for a in range(PASSES):
+                        at = 256 * t + 128 * a
+                        product(acc[:, CHUNK * s : CHUNK * (s + 1)], we_codes[:, at : at + 128].bitcast(FP8X4), w_scale(0, a, t), a, lo, lo + CHUNK)
+                nc.vector.tensor_tensor(
+                    signal[c][:, u, :, :],
+                    acc[:].rearrange("p (s n) -> p n s", s=2),
+                    growth[:, 2 * u : 2 * u + 2, lo : lo + CHUNK].rearrange("p s n -> p n s"),
+                    ALU.mult,
+                )
+
+        def background(c):
+            h_bf[c] = ring.tile([P, CHUNK * SLOTS], BF16, name="h_bf", align_bytes=64)
+            for j in range(2):
+                lo = CHUNK * c + P * j
+                acc = bank()
+                for t in range(SLOTS):
+                    for a in range(PASSES):
+                        at = 128 * t + 64 * a
+                        product(acc[:, P * t : P * (t + 1)], wb_codes[:, at : at + 64].bitcast(FP4X4), w_scale(1, a, t), a, lo, lo + P, unpacked=True)
+                nc.vector.tensor_tensor(
+                    h_bf[c][:, 512 * j : 512 * (j + 1)].rearrange("p (n u s) -> p n u s", u=2, s=2),
+                    signal[c][:, :, P * j : P * (j + 1), :].rearrange("p u n s -> p n u s"),
+                    acc[:].rearrange("p (u s n) -> p n u s", u=2, s=2),
+                    ALU.subtract,
+                )
+
+        def quantise_h(c):
+            codes = ring.tile([P, CHUNK], U32, name="h_codes", align_bytes=64)
+            scales = ring.tile([P, CHUNK], U8, name="h_scales", align_bytes=64)
+            nc.vector.quantize_mx(out=codes[:].bitcast(FP8X4), scales=scales[:], in_=h_bf[c][:])
+            h_mx[c] = (codes, scales)
+
+        def readout(c):
+            codes, scales = h_mx[c]
+            staged = ring.tile([P, N // P, CHUNK], F32, name="staged", align_bytes=64)
+            accs = [bank(), bank()]
+            last = c == chunks - 1
+            out_view = out[:, CHUNK * c : CHUNK * (c + 1)].rearrange("(b p) j -> p b j", p=P)
+            for b in range(N // P):
+                dst = accs[b // 2][:, CHUNK * (b % 2) : CHUNK * (b % 2 + 1)]
+                nc.tensor.matmul_mx(
+                    out=dst, lhsT=wo_codes[:, P * b : P * (b + 1)].bitcast(FP8X4), lhsT_scale=wo_scales[:, P * b : P * (b + 1)],
+                    rhs=codes[:].bitcast(FP8X4), rhs_scale=scales[:], start=True, stop=True,
+                )
+            for b in range(N // P):
+                src = accs[b // 2][:, CHUNK * (b % 2) : CHUNK * (b % 2 + 1)]
+                if last and b == 2:
+                    nc.vector.tensor_scalar(staged[:, b, :], src, bias[:, b : b + 1], None, ALU.add)
+                else:
+                    nc.scalar.activation(staged[:, b, :], src, ACT.Identity, bias=bias[:, b : b + 1])
+            nc.sync.dma_start(out=out_view, in_=staged[:])
+
+        for c in range(chunks):
+            exposure(c)
+            if c == 0:
+                nc.vector.quantize_mx(out=wo_codes[:, 0:256].bitcast(FP8X4), scales=wo_scales[:, 0:256], in_=wo_bf[:, 0:1024])
+                nc.vector.quantize_mx(out=wo_codes[:, 256:384].bitcast(FP8X4), scales=wo_scales[:, 256:384], in_=wo_bf[:, 1024:1536])
+            else:
+                quantise_h(c - 1)
+            background(c)
+            if c > 0:
+                readout(c - 1)
+        quantise_h(chunks - 1)
+        readout(chunks - 1)

@@ -31,7 +31,8 @@ def tile_list_kmer_locus_enrichment_kernel(
     nc = tc.nc
     with ExitStack() as ctx:
         keep = ctx.enter_context(tc.tile_pool(name="keep", bufs=1))
-        ring = ctx.enter_context(tc.tile_pool(name="ring", bufs=2))
+        ring = ctx.enter_context(tc.tile_pool(name="ring", bufs=5))
+        placed = ctx.enter_context(tc.tile_pool(name="placed", bufs=1))
         psum = ctx.enter_context(tc.psum_pool(name="psum", bufs=8))
 
         def bank():
@@ -40,55 +41,62 @@ def tile_list_kmer_locus_enrichment_kernel(
         offsets = keep.tile([P, S // 16], U16, name="offsets")
         nc.sync.dma_start(offsets[:], offs)
 
-        ts_win = keep.tile([P, T // 4], I32, name="ts_win", align_bytes=64)
-        tw_win = [keep.tile([P, T], I32, name=f"tw_win{a}", tag=f"table{a}", align_bytes=64) for a in range(PASSES)]
+        TAB0, WR, TAB1, TS, BF1 = 0, 8192, 24576, 32768, 38912
+        ts_win = placed.tile([P, T // 4], I32, name="ts_win", offset=TS, align_bytes=64)
         v_codes = [keep.tile([P, S], U32, name=f"v_codes{a}", align_bytes=64) for a in range(PASSES)]
         v_scales = keep.tile([P, S], U8, name="v_scales", align_bytes=64)
         v_scales1 = keep.tile([P, S // 4], I32, name="v_scales1", align_bytes=64)
-        wr_raw = [keep.tile([P, 4 * H], F32, name=f"wr_raw{a}", tag=f"stage{a}", align_bytes=64) for a in range(PASSES)]
-        wr_bf = [keep.tile([P, 4 * H], BF16, name=f"wr_bf{a}", align_bytes=64) for a in range(PASSES)]
+        wr_bf = [
+            keep.tile([P, 4 * H], BF16, name="wr_bf0", align_bytes=64),
+            placed.tile([P, 4 * H], BF16, name="wr_bf1", offset=BF1, align_bytes=64),
+        ]
         wr_codes = [keep.tile([P, H], U32, name=f"wr_codes{a}", align_bytes=64) for a in range(PASSES)]
         wr_scales = [keep.tile([P, H], U8, name=f"wr_scales{a}", align_bytes=64) for a in range(PASSES)]
         ws_raw = keep.tile([P, 2, PASSES, H // 4], I32, name="ws_raw", align_bytes=64)
-        we_codes = keep.tile([P, PASSES * H], I32, name="we_codes", align_bytes=64)
-        wb_codes = keep.tile([P, PASSES * H // 2], I32, name="wb_codes", align_bytes=64)
         wo_bf = keep.tile([P, N * SLOTS], BF16, name="wo_bf", align_bytes=64)
         wo_codes = keep.tile([P, N], U32, name="wo_codes", align_bytes=64)
         wo_scales = keep.tile([P, N], U8, name="wo_scales", align_bytes=64)
         growth = keep.tile([P, SLOTS, S], F32, name="growth", align_bytes=64)
-        warm = keep.tile([P, 2], F32, name="warm", tag="small")
+        warm = keep.tile([P, 2], F32, name="warm")
+        bias = keep.tile([P, N // P], F32, name="bias")
 
+        def load_table(a):
+            nc.sync.dma_start(out=tw_win[a][:], in_=tab_words[a].rearrange("p t i -> p (t i)").bitcast(I32))
+
+        def load_wr(a):
+            nc.sync.dma_start(out=wr_raw[:, a, :], in_=wr[512 * a : 512 * (a + 1), :].rearrange("(p i) c -> p (i c)", i=4))
+
+        tw_win = [placed.tile([P, T], I32, name="tw_win0", offset=TAB0, align_bytes=64)]
+        load_table(0)
         nc.vector.memset(ts_win[:], 0)
-        nc.vector.memset(warm[:, 0:1], 0.0)
+        nc.gpsimd.memset(warm[:, 0:1], 0.0)
         nc.gpsimd.memset(ws_raw[:], 0)
-        nc.gpsimd.memset(v_scales1[:], 0)
+        zeros = placed.tile([P, S // 4], I32, name="zeros", offset=TAB1 - 512, align_bytes=64)
+        nc.vector.memset(zeros[:], 0)
+        nc.vector.tensor_copy(v_scales1[:], zeros[:])
         for q in range(4):
-            nc.scalar.dma_start(
+            nc.sync.dma_start(
                 out=ts_win[32 * q : 32 * q + 8, :],
                 in_=tab_scales[:, 4 * q : 4 * q + 4, :].bitcast(I32),
             )
         nc.scalar.activation(warm[:, 1:2], warm[:, 0:1], ACT.Exp)
-        for a in range(PASSES):
-            nc.sync.dma_start(
-                out=wr_raw[a][:], in_=wr[512 * a : 512 * (a + 1), :].rearrange("(p i) c -> p (i c)", i=4)
-            )
-            nc.sync.dma_start(out=tw_win[a][:], in_=tab_words[a].rearrange("p t i -> p (t i)").bitcast(I32))
+        wr_raw = placed.tile([P, PASSES, 4 * H], F32, name="wr_raw", offset=WR, align_bytes=64)
+        tw_win.append(placed.tile([P, T], I32, name="tw_win1", offset=TAB1, align_bytes=64))
+        load_wr(0)
+        load_table(1)
+        load_wr(1)
         for w, scales in enumerate((we_scales, wb_scales)):
             for q in range(4):
                 nc.gpsimd.dma_start(
                     out=ws_raw[32 * q : 32 * q + 4, w, :, :],
                     in_=scales[:, 4 * q : 4 * q + 4, :].rearrange("a r c -> r a c").bitcast(I32),
                 )
-        bias = keep.tile([P, N // P], F32, name="bias", tag="small")
         with nc.allow_non_contiguous_dma(reason="one bias value a partition"):
-            nc.scalar.dma_start(out=bias[:], in_=bo.rearrange("(b p) -> p b", p=P))
+            nc.gpsimd.dma_start(out=bias[:], in_=bo.rearrange("(b p) -> p b", p=P))
 
-        def gather_scales():
-            nc.vector.tensor_copy(v_scales[:], ts_win[:].bitcast(U8).indirect(offsets[:]))
-            for q in range(4):
-                nc.gpsimd.dma_start(
-                    out=v_scales1[32 * q : 32 * q + 4, :], in_=v_scales[32 * q + 4 : 32 * q + 8, :].bitcast(I32)
-                )
+        def gather_scales(lo, hi):
+            nc.vector.tensor_copy(v_scales[:, lo:hi], ts_win[:].bitcast(U8).indirect(offsets[:, lo // 16 : hi // 16]))
+
 
         def gather_words(a, lo, hi):
             nc.vector.tensor_copy(
@@ -98,7 +106,7 @@ def tile_list_kmer_locus_enrichment_kernel(
         def cast_wr(a, t, engine_copy):
             engine_copy(
                 wr_bf[a][:, 512 * t : 512 * (t + 1)].rearrange("p (g e i) -> p g e i", e=RUN, i=4),
-                wr_raw[a][:].rearrange("p (i g t e) -> p t g e i", i=4, t=SLOTS, e=RUN)[:, t],
+                wr_raw[:, a, :].rearrange("p (i g t e) -> p t g e i", i=4, t=SLOTS, e=RUN)[:, t],
             )
 
         def quantise_wr(a, t0, t1):
@@ -126,55 +134,61 @@ def tile_list_kmer_locus_enrichment_kernel(
             )
 
         def w_scale(w, a, t):
-            at = 128 * t + 32 * (2 * w + a)
-            return ws[:, at : at + 32].bitcast(U8)
+            at = 64 * t + 32 * a
+            return ws[w][:, at : at + 32].bitcast(U8)
 
-        gather_scales()
-        for t in range(SLOTS):
-            cast_wr(0, t, nc.scalar.copy)
-        w_raw = keep.tile([P, PASSES * (H + H // 2)], I32, name="w_raw", tag="stage0", align_bytes=64)
+        gather_words(0, 0, S)
+        w_raw = placed.tile([P, PASSES * (H + H // 2)], I32, name="w_raw", offset=TAB0, align_bytes=64)
         we_raw = w_raw[:, 0 : PASSES * H]
         wb_raw = w_raw[:, PASSES * H :]
         nc.sync.dma_start(out=we_raw.rearrange("p (a c) -> p a c", a=PASSES), in_=we_words.rearrange("a p c i -> p a (c i)").bitcast(I32))
         nc.sync.dma_start(out=wb_raw.rearrange("p (a c) -> p a c", a=PASSES), in_=wb_words.rearrange("a p c -> p a c").bitcast(I32))
-        quantise_wr(0, 0, 4)
-        gather_words(0, 0, HALF)
-        gather_words(0, HALF, S)
-        rate = [[bank() for t in range(SLOTS)] for half in range(2)]
-
-        def rate_pass(a, half, t):
-            cols = slice(P * t, P * (t + 1))
-            product(rate[half][t][:], wr_codes[a][:, cols].bitcast(FP8X4), wr_scales[a][:, cols], a, HALF * half, HALF * (half + 1))
-
-        for half in range(2):
-            for t in range(SLOTS):
-                rate_pass(0, half, t)
-
-        cast_wr(1, 0, nc.scalar.copy)
-        cast_wr(1, 1, nc.scalar.copy)
-        cast_wr(1, 2, nc.scalar.copy)
-        cast_wr(1, 3, nc.vector.tensor_copy)
-        wo_raw = keep.tile([P, SLOTS, N], F32, name="wo_raw", tag="stage1", align_bytes=64)
+        gather_scales(0, S)
+        for dst, src, rows in ((0, 4, 64), (64, 68, 32), (96, 100, 4)):
+            nc.sync.dma_start(out=v_scales1[dst : dst + rows, :], in_=v_scales[src : src + rows, :].bitcast(I32))
+        wo_raw = placed.tile([P, SLOTS, N], F32, name="wo_raw", offset=TS, align_bytes=64)
         for t in range(SLOTS):
             nc.sync.dma_start(out=wo_raw[:, t, :], in_=wo.rearrange("(g t e) n -> t g e n", t=SLOTS, e=RUN)[t])
-        ws = keep.tile([P, 2 * PASSES * H // 4], I32, name="ws", tag="table0", align_bytes=64)
-        reorder(ws[:], ws_raw[:].rearrange("p w a c -> p (w a c)"), RUN // 4)
-        quantise_wr(1, 0, 4)
-        for half in range(2):
-            gather_words(1, HALF * half, HALF * (half + 1))
-            for t in range(SLOTS):
-                rate_pass(1, half, t)
-                nc.scalar.activation(growth[:, t, HALF * half : HALF * (half + 1)], rate[half][t][:], ACT.Exp)
-            if half == 0:
-                reorder(we_codes[:], we_raw, RUN)
-            else:
-                reorder(wb_codes[:], wb_raw, RUN // 2)
 
-        for b in range(N // P):
-            nc.scalar.copy(
-                wo_bf[:, 512 * b : 512 * (b + 1)].rearrange("p (n t) -> p n t", t=SLOTS),
-                wo_raw[:, :, P * b : P * (b + 1)].rearrange("p t n -> p n t"),
-            )
+        def prepare_wr(a):
+            cast_wr(a, 0, nc.vector.tensor_copy)
+            cast_wr(a, 1, nc.vector.tensor_copy)
+            cast_wr(a, 2, nc.scalar.copy)
+            cast_wr(a, 3, nc.scalar.copy)
+            quantise_wr(a, 0, 2)
+            quantise_wr(a, 2, 4)
+
+        rate = [[bank() for t in range(SLOTS)] for half in range(2)]
+
+        def rate_pass(a, half, slots):
+            for t in slots:
+                cols = slice(P * t, P * (t + 1))
+                product(rate[half][t][:], wr_codes[a][:, cols].bitcast(FP8X4), wr_scales[a][:, cols], a, HALF * half, HALF * (half + 1))
+                if a == PASSES - 1:
+                    nc.scalar.activation(growth[:, t, HALF * half : HALF * (half + 1)], rate[half][t][:], ACT.Exp)
+
+        prepare_wr(0)
+        for slots in ((0, 1), (2, 3)):
+            for half in range(2):
+                rate_pass(0, half, slots)
+        gather_words(1, 0, S)
+        ws = [placed.tile([P, PASSES * H // 4], I32, name=f"ws{w}", offset=at, align_bytes=64) for w, at in enumerate((TAB1, WR))]
+        prepare_wr(1)
+        reorder(ws[0][:], ws_raw[:, 0, :, :].rearrange("p a c -> p (a c)"), RUN // 4)
+        we_codes = placed.tile([P, PASSES * H], I32, name="we_codes", offset=BF1, align_bytes=64)
+        wb_codes = placed.tile([P, PASSES * H // 2], I32, name="wb_codes", offset=WR + 1024, align_bytes=64)
+        reorder(we_codes[:], we_raw, RUN)
+        reorder(wb_codes[:], wb_raw, RUN // 2)
+        reorder(ws[1][:], ws_raw[:, 1, :, :].rearrange("p a c -> p (a c)"), RUN // 4)
+        rate_pass(1, 0, range(SLOTS))
+        rate_pass(1, 1, (0, 1))
+
+        def cast_wo():
+            for b in range(N // P):
+                nc.scalar.copy(
+                    wo_bf[:, 512 * b : 512 * (b + 1)].rearrange("p (n t) -> p n t", t=SLOTS),
+                    wo_raw[:, :, P * b : P * (b + 1)].rearrange("p t n -> p n t"),
+                )
 
         chunks = S // CHUNK
         signal = {}
@@ -198,57 +212,69 @@ def tile_list_kmer_locus_enrichment_kernel(
                     ALU.mult,
                 )
 
-        def background(c):
-            h_bf[c] = ring.tile([P, CHUNK * SLOTS], BF16, name="h_bf", align_bytes=64)
-            for j in range(2):
-                lo = CHUNK * c + P * j
-                acc = bank()
-                for t in range(SLOTS):
-                    for a in range(PASSES):
-                        at = 128 * t + 64 * a
-                        product(acc[:, P * t : P * (t + 1)], wb_codes[:, at : at + 64].bitcast(FP4X4), w_scale(1, a, t), a, lo, lo + P, unpacked=True)
-                nc.vector.tensor_tensor(
-                    h_bf[c][:, 512 * j : 512 * (j + 1)].rearrange("p (n u s) -> p n u s", u=2, s=2),
-                    signal[c][:, :, P * j : P * (j + 1), :].rearrange("p u n s -> p n u s"),
-                    acc[:].rearrange("p (u s n) -> p n u s", u=2, s=2),
-                    ALU.subtract,
-                )
+        def background(c, j):
+            if j == 0:
+                h_bf[c] = ring.tile([P, CHUNK * SLOTS], BF16, name="h_bf", align_bytes=64)
+            lo = CHUNK * c + P * j
+            acc = bank()
+            for t in range(SLOTS):
+                for a in range(PASSES):
+                    at = 128 * t + 64 * a
+                    product(acc[:, P * t : P * (t + 1)], wb_codes[:, at : at + 64].bitcast(FP4X4), w_scale(1, a, t), a, lo, lo + P, unpacked=True)
+            nc.vector.tensor_tensor(
+                h_bf[c][:, 512 * j : 512 * (j + 1)].rearrange("p (n u s) -> p n u s", u=2, s=2),
+                signal[c][:, :, P * j : P * (j + 1), :].rearrange("p u n s -> p n u s"),
+                acc[:].rearrange("p (u s n) -> p n u s", u=2, s=2),
+                ALU.subtract,
+            )
 
-        def quantise_h(c):
-            codes = ring.tile([P, CHUNK], U32, name="h_codes", align_bytes=64)
-            scales = ring.tile([P, CHUNK], U8, name="h_scales", align_bytes=64)
-            nc.vector.quantize_mx(out=codes[:].bitcast(FP8X4), scales=scales[:], in_=h_bf[c][:])
-            h_mx[c] = (codes, scales)
+        def quantise_h(c, lo, width):
+            codes = ring.tile([P, width], U32, name="h_codes", align_bytes=64)
+            scales = ring.tile([P, width], U8, name="h_scales", align_bytes=64)
+            nc.vector.quantize_mx(out=codes[:].bitcast(FP8X4), scales=scales[:], in_=h_bf[c][:, 4 * lo : 4 * (lo + width)])
+            h_mx[c, lo] = (codes, scales)
 
-        def readout(c):
-            codes, scales = h_mx[c]
-            staged = ring.tile([P, N // P, CHUNK], F32, name="staged", align_bytes=64)
-            accs = [bank(), bank()]
-            last = c == chunks - 1
-            out_view = out[:, CHUNK * c : CHUNK * (c + 1)].rearrange("(b p) j -> p b j", p=P)
-            for b in range(N // P):
-                dst = accs[b // 2][:, CHUNK * (b % 2) : CHUNK * (b % 2 + 1)]
+        def readout(c, lo, width, on_vector=False):
+            codes, scales = h_mx[c, lo]
+            blocks = N // P
+            staged = ring.tile([P, blocks, width], F32, name="staged", align_bytes=64)
+            per_bank = min(blocks, BANK // width)
+            accs = [bank() for first in range(0, blocks, per_bank)]
+            sums = [accs[b // per_bank][:, width * (b % per_bank) : width * (b % per_bank + 1)] for b in range(blocks)]
+            for b in range(blocks):
                 nc.tensor.matmul_mx(
-                    out=dst, lhsT=wo_codes[:, P * b : P * (b + 1)].bitcast(FP8X4), lhsT_scale=wo_scales[:, P * b : P * (b + 1)],
+                    out=sums[b], lhsT=wo_codes[:, P * b : P * (b + 1)].bitcast(FP8X4), lhsT_scale=wo_scales[:, P * b : P * (b + 1)],
                     rhs=codes[:].bitcast(FP8X4), rhs_scale=scales[:], start=True, stop=True,
                 )
-            for b in range(N // P):
-                src = accs[b // 2][:, CHUNK * (b % 2) : CHUNK * (b % 2 + 1)]
-                if last and b == 2:
-                    nc.vector.tensor_scalar(staged[:, b, :], src, bias[:, b : b + 1], None, ALU.add)
-                else:
-                    nc.scalar.activation(staged[:, b, :], src, ACT.Identity, bias=bias[:, b : b + 1])
-            nc.sync.dma_start(out=out_view, in_=staged[:])
+            if on_vector:
+                nc.vector.tensor_tensor(
+                    staged[:],
+                    accs[0][:, 0 : blocks * width].rearrange("p (b j) -> p b j", b=blocks),
+                    bias[:].unsqueeze(2).to_broadcast([P, blocks, width]),
+                    ALU.add,
+                )
+            else:
+                for b in range(blocks):
+                    nc.scalar.activation(staged[:, b, :], sums[b], ACT.Identity, bias=bias[:, b : b + 1])
+            first = CHUNK * c + lo
+            nc.sync.dma_start(out=out[:, first : first + width].rearrange("(b p) j -> p b j", p=P), in_=staged[:])
 
+        last = chunks - 1
         for c in range(chunks):
             exposure(c)
             if c == 0:
+                rate_pass(1, 1, (2, 3))
+                cast_wo()
+            if c > 0:
+                quantise_h(c - 1, 0, CHUNK)
+            if c == 2:
                 nc.vector.quantize_mx(out=wo_codes[:, 0:256].bitcast(FP8X4), scales=wo_scales[:, 0:256], in_=wo_bf[:, 0:1024])
                 nc.vector.quantize_mx(out=wo_codes[:, 256:384].bitcast(FP8X4), scales=wo_scales[:, 256:384], in_=wo_bf[:, 1024:1536])
-            else:
-                quantise_h(c - 1)
-            background(c)
-            if c > 0:
-                readout(c - 1)
-        quantise_h(chunks - 1)
-        readout(chunks - 1)
+            if c > 1:
+                readout(c - 2, 0, CHUNK)
+            background(c, 0)
+            background(c, 1)
+        readout(last - 1, 0, CHUNK)
+        for j in range(2):
+            quantise_h(last, P * j, P)
+            readout(last, P * j, P, on_vector=(j == 1))

@@ -39,7 +39,6 @@ def tile_list_kmer_locus_enrichment_kernel(
             return psum.tile([P, BANK], F32, name="bank", tag="bank")
 
         offsets = keep.tile([P, S // 16], U16, name="offsets")
-        nc.sync.dma_start(offsets[:], offs)
 
         TAB0, WR, TAB1, TS, BF1 = 0, 8192, 24576, 32768, 38912
         ts_win = placed.tile([P, T // 4], I32, name="ts_win", offset=TS, align_bytes=64)
@@ -50,7 +49,7 @@ def tile_list_kmer_locus_enrichment_kernel(
             keep.tile([P, 4 * H], BF16, name="wr_bf0", align_bytes=64),
             placed.tile([P, 4 * H], BF16, name="wr_bf1", offset=BF1, align_bytes=64),
         ]
-        wr_codes = [keep.tile([P, H], U32, name=f"wr_codes{a}", align_bytes=64) for a in range(PASSES)]
+        wr_codes = {}
         wr_scales = [keep.tile([P, H], U8, name=f"wr_scales{a}", align_bytes=64) for a in range(PASSES)]
         ws_raw = keep.tile([P, 2, PASSES, H // 4], I32, name="ws_raw", align_bytes=64)
         wo_bf = keep.tile([P, N * SLOTS], BF16, name="wo_bf", align_bytes=64)
@@ -68,6 +67,7 @@ def tile_list_kmer_locus_enrichment_kernel(
 
         tw_win = [placed.tile([P, T], I32, name="tw_win0", offset=TAB0, align_bytes=64)]
         load_table(0)
+        nc.sync.dma_start(offsets[:], offs)
         nc.vector.memset(ts_win[:], 0)
         nc.gpsimd.memset(warm[:, 0:1], 0.0)
         nc.gpsimd.memset(ws_raw[:], 0)
@@ -83,8 +83,8 @@ def tile_list_kmer_locus_enrichment_kernel(
         wr_raw = placed.tile([P, PASSES, 4 * H], F32, name="wr_raw", offset=WR, align_bytes=64)
         tw_win.append(placed.tile([P, T], I32, name="tw_win1", offset=TAB1, align_bytes=64))
         load_wr(0)
-        load_table(1)
         load_wr(1)
+        load_table(1)
         for w, scales in enumerate((we_scales, wb_scales)):
             for q in range(4):
                 nc.gpsimd.dma_start(
@@ -92,7 +92,7 @@ def tile_list_kmer_locus_enrichment_kernel(
                     in_=scales[:, 4 * q : 4 * q + 4, :].rearrange("a r c -> r a c").bitcast(I32),
                 )
         with nc.allow_non_contiguous_dma(reason="one bias value a partition"):
-            nc.gpsimd.dma_start(out=bias[:], in_=bo.rearrange("(b p) -> p b", p=P))
+            nc.scalar.dma_start(out=bias[:], in_=bo.rearrange("(b p) -> p b", p=P))
 
         def gather_scales(lo, hi):
             nc.vector.tensor_copy(v_scales[:, lo:hi], ts_win[:].bitcast(U8).indirect(offsets[:, lo // 16 : hi // 16]))
@@ -109,11 +109,12 @@ def tile_list_kmer_locus_enrichment_kernel(
                 wr_raw[:, a, :].rearrange("p (i g t e) -> p t g e i", i=4, t=SLOTS, e=RUN)[:, t],
             )
 
-        def quantise_wr(a, t0, t1):
+        def quantise_wr(a, u, codes):
+            wr_codes[a, u] = codes
             nc.vector.quantize_mx(
-                out=wr_codes[a][:, P * t0 : P * t1].bitcast(FP8X4),
-                scales=wr_scales[a][:, P * t0 : P * t1],
-                in_=wr_bf[a][:, 512 * t0 : 512 * t1],
+                out=codes[:].bitcast(FP8X4),
+                scales=wr_scales[a][:, 256 * u : 256 * (u + 1)],
+                in_=wr_bf[a][:, 1024 * u : 1024 * (u + 1)],
             )
 
         def reorder(dst, src, run):
@@ -155,33 +156,36 @@ def tile_list_kmer_locus_enrichment_kernel(
             cast_wr(a, 1, nc.vector.tensor_copy)
             cast_wr(a, 2, nc.scalar.copy)
             cast_wr(a, 3, nc.scalar.copy)
-            quantise_wr(a, 0, 2)
-            quantise_wr(a, 2, 4)
 
         rate = [[bank() for t in range(SLOTS)] for half in range(2)]
 
         def rate_pass(a, half, slots):
             for t in slots:
                 cols = slice(P * t, P * (t + 1))
-                product(rate[half][t][:], wr_codes[a][:, cols].bitcast(FP8X4), wr_scales[a][:, cols], a, HALF * half, HALF * (half + 1))
+                product(rate[half][t][:], wr_codes[a, t // 2][:, P * (t % 2) : P * (t % 2 + 1)].bitcast(FP8X4), wr_scales[a][:, cols], a, HALF * half, HALF * (half + 1))
                 if a == PASSES - 1:
                     nc.scalar.activation(growth[:, t, HALF * half : HALF * (half + 1)], rate[half][t][:], ACT.Exp)
 
         prepare_wr(0)
-        for slots in ((0, 1), (2, 3)):
-            for half in range(2):
-                rate_pass(0, half, slots)
-        gather_words(1, 0, S)
-        ws = [placed.tile([P, PASSES * H // 4], I32, name=f"ws{w}", offset=at, align_bytes=64) for w, at in enumerate((TAB1, WR))]
+        quantise_wr(0, 0, keep.tile([P, 256], U32, name="wr_codes00", align_bytes=64))
+        for half in range(2):
+            rate_pass(0, half, (0, 1))
         prepare_wr(1)
+        quantise_wr(1, 0, keep.tile([P, 256], U32, name="wr_codes10", align_bytes=64))
+        quantise_wr(0, 1, placed.tile([P, 256], U32, name="wr_codes01", offset=WR + 1024, align_bytes=64))
+        for half in range(2):
+            rate_pass(0, half, (2, 3))
+        quantise_wr(1, 1, keep.tile([P, 256], U32, name="wr_codes11", align_bytes=64))
+        ws = [placed.tile([P, PASSES * H // 4], I32, name=f"ws{w}", offset=at, align_bytes=64) for w, at in enumerate((WR, TAB1))]
         reorder(ws[0][:], ws_raw[:, 0, :, :].rearrange("p a c -> p (a c)"), RUN // 4)
+        gather_words(1, 0, HALF)
+        rate_pass(1, 0, range(SLOTS))
         we_codes = placed.tile([P, PASSES * H], I32, name="we_codes", offset=BF1, align_bytes=64)
-        wb_codes = placed.tile([P, PASSES * H // 2], I32, name="wb_codes", offset=WR + 1024, align_bytes=64)
         reorder(we_codes[:], we_raw, RUN)
+        gather_words(1, HALF, S)
+        wb_codes = placed.tile([P, PASSES * H // 2], I32, name="wb_codes", offset=TAB1 + 1024, align_bytes=64)
         reorder(wb_codes[:], wb_raw, RUN // 2)
         reorder(ws[1][:], ws_raw[:, 1, :, :].rearrange("p a c -> p (a c)"), RUN // 4)
-        rate_pass(1, 0, range(SLOTS))
-        rate_pass(1, 1, (0, 1))
 
         def cast_wo():
             for b in range(N // P):
@@ -261,8 +265,10 @@ def tile_list_kmer_locus_enrichment_kernel(
 
         last = chunks - 1
         for c in range(chunks):
+            if c == 1:
+                rate_pass(1, 1, (0, 1))
             exposure(c)
-            if c == 0:
+            if c == 1:
                 rate_pass(1, 1, (2, 3))
                 cast_wo()
             if c > 0:

@@ -20,9 +20,9 @@ P = 128
 PASSES = 2
 SLOTS = 4
 RUN = 8
-HALF = 512
 CHUNK = 256
 BANK = 512
+CHUNKS = S // CHUNK
 
 
 def tile_list_kmer_locus_enrichment_kernel(
@@ -39,80 +39,67 @@ def tile_list_kmer_locus_enrichment_kernel(
             return psum.tile([P, BANK], F32, name="bank", tag="bank")
 
         offsets = keep.tile([P, S // 16], U16, name="offsets")
-
-        TAB0, WR, TAB1, TS, BF1 = 0, 8192, 24576, 32768, 38912
-        ts_win = placed.tile([P, T // 4], I32, name="ts_win", offset=TS, align_bytes=64)
-        v_codes = [keep.tile([P, S], U32, name=f"v_codes{a}", align_bytes=64) for a in range(PASSES)]
         v_scales = keep.tile([P, S], U8, name="v_scales", align_bytes=64)
         v_scales1 = keep.tile([P, S // 4], I32, name="v_scales1", align_bytes=64)
-        wr_bf = [
-            keep.tile([P, 4 * H], BF16, name="wr_bf0", align_bytes=64),
-            placed.tile([P, 4 * H], BF16, name="wr_bf1", offset=BF1, align_bytes=64),
-        ]
-        wr_codes = {}
+        wr_codes = [keep.tile([P, H], U32, name=f"wr_codes{a}", align_bytes=64) for a in range(PASSES)]
         wr_scales = [keep.tile([P, H], U8, name=f"wr_scales{a}", align_bytes=64) for a in range(PASSES)]
-        ws_raw = keep.tile([P, 2, PASSES, H // 4], I32, name="ws_raw", align_bytes=64)
-        wo_bf = keep.tile([P, N * SLOTS], BF16, name="wo_bf", align_bytes=64)
+        ws_raw = [keep.tile([P, PASSES * H // 4], I32, name=f"ws_raw{w}", align_bytes=64) for w in range(2)]
+        ws = {}
+        wr_bf = {}
         wo_codes = keep.tile([P, N], U32, name="wo_codes", align_bytes=64)
         wo_scales = keep.tile([P, N], U8, name="wo_scales", align_bytes=64)
-        growth = keep.tile([P, SLOTS, S], F32, name="growth", align_bytes=64)
-        warm = keep.tile([P, 2], F32, name="warm")
-        bias = keep.tile([P, N // P], F32, name="bias")
+        back = keep.tile([P, SLOTS * S], F32, name="back", align_bytes=64)
 
-        def load_table(a):
-            nc.sync.dma_start(out=tw_win[a][:], in_=tab_words[a].rearrange("p t i -> p (t i)").bitcast(I32))
-
-        def load_wr(a):
-            nc.sync.dma_start(out=wr_raw[:, a, :], in_=wr[512 * a : 512 * (a + 1), :].rearrange("(p i) c -> p (i c)", i=4))
-
-        tw_win = [placed.tile([P, T], I32, name="tw_win0", offset=TAB0, align_bytes=64)]
-        load_table(0)
         nc.sync.dma_start(offsets[:], offs)
-        nc.vector.memset(ts_win[:], 0)
-        nc.gpsimd.memset(warm[:, 0:1], 0.0)
-        nc.gpsimd.memset(ws_raw[:], 0)
-        zeros = placed.tile([P, S // 4], I32, name="zeros", offset=TAB1 - 512, align_bytes=64)
-        nc.vector.memset(zeros[:], 0)
-        nc.vector.tensor_copy(v_scales1[:], zeros[:])
+        WB, TAB0, WO, TAB1, GROWTH, TS = 0, 2048, 10240, 16320, 28672, 45056
+        BF, BIAS, WE = TAB1 + 64, TAB1 + 4160, TAB1 + 4224
+        WR0, WR1, WBC, WS1, VC0, END = TS, TS + 8192, TS + 16384, TS + 18432, TS + 19456, TS + 23552
+        zeros = placed.tile([P, (TAB1 + 8192) // 4], I32, name="zeros", offset=0, align_bytes=64)
+        ts_tile = placed.tile([P, (END - TS) // 4], I32, name="ts_tile", offset=TS, align_bytes=64)
+        ts_win = ts_tile[:, 0 : T // 4]
+        nc.vector.memset(ts_win, 0)
+        nc.gpsimd.memset(ws_raw[1][:], 0)
+        nc.vector.memset(zeros[:, 0 : S // 4], 0)
+        nc.vector.tensor_copy(v_scales1[:], zeros[:, 0 : S // 4])
+        nc.vector.memset(ws_raw[0][:], 0)
         for q in range(4):
             nc.sync.dma_start(
-                out=ts_win[32 * q : 32 * q + 8, :],
+                out=ts_tile[32 * q : 32 * q + 8, 0 : T // 4],
                 in_=tab_scales[:, 4 * q : 4 * q + 4, :].bitcast(I32),
             )
-        nc.scalar.activation(warm[:, 1:2], warm[:, 0:1], ACT.Exp)
-        wr_raw = placed.tile([P, PASSES, 4 * H], F32, name="wr_raw", offset=WR, align_bytes=64)
-        tw_win.append(placed.tile([P, T], I32, name="tw_win1", offset=TAB1, align_bytes=64))
-        load_wr(0)
-        load_wr(1)
-        load_table(1)
-        for w, scales in enumerate((we_scales, wb_scales)):
-            for q in range(4):
-                nc.gpsimd.dma_start(
-                    out=ws_raw[32 * q : 32 * q + 4, w, :, :],
-                    in_=scales[:, 4 * q : 4 * q + 4, :].rearrange("a r c -> r a c").bitcast(I32),
-                )
-        with nc.allow_non_contiguous_dma(reason="one bias value a partition"):
-            nc.scalar.dma_start(out=bias[:], in_=bo.rearrange("(b p) -> p b", p=P))
 
-        def gather_scales(lo, hi):
-            nc.vector.tensor_copy(v_scales[:, lo:hi], ts_win[:].bitcast(U8).indirect(offsets[:, lo // 16 : hi // 16]))
+        def load_scales(w, scales, q, queue):
+            queue.dma_start(
+                out=ws_raw[w][32 * q : 32 * q + 4, :].rearrange("p (a c) -> p a c", a=PASSES),
+                in_=scales[:, 4 * q : 4 * q + 4, :].rearrange("a r c -> r a c").bitcast(I32),
+            )
 
+        load_scales(1, wb_scales, 0, nc.sync)
+        wb_raw = placed.tile([P, PASSES * H // 2], I32, name="wb_raw", offset=WB, align_bytes=64)
+        tw_win = [placed.tile([P, T], I32, name=f"tw_win{a}", offset=at, align_bytes=64) for a, at in enumerate((TAB0, TAB1))]
+        nc.sync.dma_start(out=wb_raw[:].rearrange("p (a c) -> p a c", a=PASSES), in_=wb_words.rearrange("a p c -> p a c").bitcast(I32))
+        for a in range(PASSES):
+            nc.sync.dma_start(out=tw_win[a][:], in_=tab_words[a].rearrange("p t i -> p (t i)").bitcast(I32))
+        for q in range(1, 4):
+            load_scales(1, wb_scales, q, nc.gpsimd)
+        for q in range(4):
+            load_scales(0, we_scales, q, nc.gpsimd)
 
-        def gather_words(a, lo, hi):
+        def gather_words(a, c):
+            lo, hi = CHUNK * c, CHUNK * (c + 1)
             nc.vector.tensor_copy(
                 v_codes[a][:, lo:hi], tw_win[a][:].bitcast(U32).indirect(offsets[:, lo // 16 : hi // 16])
             )
 
-        def cast_wr(a, t, engine_copy):
+        def cast_wr(a, t0, t1, engine_copy):
             engine_copy(
-                wr_bf[a][:, 512 * t : 512 * (t + 1)].rearrange("p (g e i) -> p g e i", e=RUN, i=4),
-                wr_raw[:, a, :].rearrange("p (i g t e) -> p t g e i", i=4, t=SLOTS, e=RUN)[:, t],
+                wr_bf[a][:, 512 * t0 : 512 * t1].rearrange("p (t g e i) -> p t g e i", t=t1 - t0, e=RUN, i=4),
+                wr_raw[a][:].rearrange("p (i g t e) -> p t g e i", i=4, t=SLOTS, e=RUN)[:, t0:t1],
             )
 
-        def quantise_wr(a, u, codes):
-            wr_codes[a, u] = codes
+        def quantise_wr(a, u):
             nc.vector.quantize_mx(
-                out=codes[:].bitcast(FP8X4),
+                out=wr_codes[a][:, 256 * u : 256 * (u + 1)].bitcast(FP8X4),
                 scales=wr_scales[a][:, 256 * u : 256 * (u + 1)],
                 in_=wr_bf[a][:, 1024 * u : 1024 * (u + 1)],
             )
@@ -123,7 +110,7 @@ def tile_list_kmer_locus_enrichment_kernel(
                 src.rearrange("p (x t e) -> p t x e", t=SLOTS, e=run),
             )
 
-        def product(dst, codes, scales, a, lo, hi, unpacked=False):
+        def product(dst, codes, scales, a, lo, hi, start, stop, unpacked=False):
             if unpacked and a == 1:
                 plane = v_scales1[:, lo // 4 : hi // 4].bitcast(U8)
             else:
@@ -131,111 +118,131 @@ def tile_list_kmer_locus_enrichment_kernel(
             nc.tensor.matmul_mx(
                 out=dst, lhsT=codes, lhsT_scale=scales,
                 rhs=v_codes[a][:, lo:hi].bitcast(FP8X4), rhs_scale=plane,
-                start=(a == 0), stop=(a == PASSES - 1),
+                start=start, stop=stop,
             )
 
         def w_scale(w, a, t):
             at = 64 * t + 32 * a
             return ws[w][:, at : at + 32].bitcast(U8)
 
-        gather_words(0, 0, S)
-        w_raw = placed.tile([P, PASSES * (H + H // 2)], I32, name="w_raw", offset=TAB0, align_bytes=64)
-        we_raw = w_raw[:, 0 : PASSES * H]
-        wb_raw = w_raw[:, PASSES * H :]
-        nc.sync.dma_start(out=we_raw.rearrange("p (a c) -> p a c", a=PASSES), in_=we_words.rearrange("a p c i -> p a (c i)").bitcast(I32))
-        nc.sync.dma_start(out=wb_raw.rearrange("p (a c) -> p a c", a=PASSES), in_=wb_words.rearrange("a p c -> p a c").bitcast(I32))
-        gather_scales(0, S)
-        for dst, src, rows in ((0, 4, 64), (64, 68, 32), (96, 100, 4)):
-            nc.sync.dma_start(out=v_scales1[dst : dst + rows, :], in_=v_scales[src : src + rows, :].bitcast(I32))
-        wo_raw = placed.tile([P, SLOTS, N], F32, name="wo_raw", offset=TS, align_bytes=64)
-        for t in range(SLOTS):
-            nc.sync.dma_start(out=wo_raw[:, t, :], in_=wo.rearrange("(g t e) n -> t g e n", t=SLOTS, e=RUN)[t])
+        nc.vector.tensor_copy(v_scales[:], ts_win.bitcast(U8).indirect(offsets[:]))
+        nc.sync.dma_start(out=v_scales1[0:100, :], in_=v_scales[4:104, :].bitcast(I32))
+        wr_raw = [placed.tile([P, 4 * H], F32, name=f"wr_raw{a}", offset=at, align_bytes=64) for a, at in enumerate((WR0, WR1))]
+        for a in range(PASSES):
+            nc.sync.dma_start(out=wr_raw[a][:], in_=wr[512 * a : 512 * (a + 1), :].rearrange("(p i) c -> p (i c)", i=4))
+        wb_codes = placed.tile([P, PASSES * H // 2], I32, name="wb_codes", offset=WBC, align_bytes=64)
+        ws[1] = placed.tile([P, PASSES * H // 4], I32, name="ws1", offset=WS1, align_bytes=64)
+        v_codes = [
+            placed.tile([P, S], U32, name="v_codes0", offset=VC0, align_bytes=64),
+            keep.tile([P, S], U32, name="v_codes1", align_bytes=64),
+        ]
+        reorder(wb_codes[:], wb_raw[:], RUN // 2)
+        reorder(ws[1][:], ws_raw[1][:], RUN // 4)
 
-        def prepare_wr(a):
-            cast_wr(a, 0, nc.vector.tensor_copy)
-            cast_wr(a, 1, nc.vector.tensor_copy)
-            cast_wr(a, 2, nc.scalar.copy)
-            cast_wr(a, 3, nc.scalar.copy)
+        back_acc = [bank() for j in range(S // P)]
 
-        rate = [[bank() for t in range(SLOTS)] for half in range(2)]
-
-        def rate_pass(a, half, slots):
-            for t in slots:
-                cols = slice(P * t, P * (t + 1))
-                product(rate[half][t][:], wr_codes[a, t // 2][:, P * (t % 2) : P * (t % 2 + 1)].bitcast(FP8X4), wr_scales[a][:, cols], a, HALF * half, HALF * (half + 1))
-                if a == PASSES - 1:
-                    nc.scalar.activation(growth[:, t, HALF * half : HALF * (half + 1)], rate[half][t][:], ACT.Exp)
-
-        prepare_wr(0)
-        quantise_wr(0, 0, keep.tile([P, 256], U32, name="wr_codes00", align_bytes=64))
-        for half in range(2):
-            rate_pass(0, half, (0, 1))
-        prepare_wr(1)
-        quantise_wr(1, 0, keep.tile([P, 256], U32, name="wr_codes10", align_bytes=64))
-        quantise_wr(0, 1, placed.tile([P, 256], U32, name="wr_codes01", offset=WR + 1024, align_bytes=64))
-        for half in range(2):
-            rate_pass(0, half, (2, 3))
-        quantise_wr(1, 1, keep.tile([P, 256], U32, name="wr_codes11", align_bytes=64))
-        ws = [placed.tile([P, PASSES * H // 4], I32, name=f"ws{w}", offset=at, align_bytes=64) for w, at in enumerate((WR, TAB1))]
-        reorder(ws[0][:], ws_raw[:, 0, :, :].rearrange("p a c -> p (a c)"), RUN // 4)
-        gather_words(1, 0, HALF)
-        rate_pass(1, 0, range(SLOTS))
-        we_codes = placed.tile([P, PASSES * H], I32, name="we_codes", offset=BF1, align_bytes=64)
-        reorder(we_codes[:], we_raw, RUN)
-        gather_words(1, HALF, S)
-        wb_codes = placed.tile([P, PASSES * H // 2], I32, name="wb_codes", offset=TAB1 + 1024, align_bytes=64)
-        reorder(wb_codes[:], wb_raw, RUN // 2)
-        reorder(ws[1][:], ws_raw[:, 1, :, :].rearrange("p a c -> p (a c)"), RUN // 4)
-
-        def cast_wo():
-            for b in range(N // P):
+        def background(a, j):
+            for t in range(SLOTS):
+                at = 128 * t + 64 * a
+                product(back_acc[j][:, P * t : P * (t + 1)], wb_codes[:, at : at + 64].bitcast(FP4X4), w_scale(1, a, t), a, P * j, P * (j + 1),
+                        start=(a == 0 and t == 0), stop=(a == PASSES - 1 and t == SLOTS - 1), unpacked=True)
+            if a == PASSES - 1:
                 nc.scalar.copy(
-                    wo_bf[:, 512 * b : 512 * (b + 1)].rearrange("p (n t) -> p n t", t=SLOTS),
-                    wo_raw[:, :, P * b : P * (b + 1)].rearrange("p t n -> p n t"),
+                    back[:, BANK * j : BANK * (j + 1)].rearrange("p (n t) -> p n t", t=SLOTS),
+                    back_acc[j][:].rearrange("p (t n) -> p n t", t=SLOTS),
                 )
 
-        chunks = S // CHUNK
+        for a in range(PASSES):
+            for c in range(CHUNKS):
+                gather_words(a, c)
+                background(a, 2 * c)
+                background(a, 2 * c + 1)
+
+        we_raw = placed.tile([P, PASSES * H], I32, name="we_raw", offset=WE, align_bytes=64)
+        wo_raw = placed.tile([P, SLOTS, N], F32, name="wo_raw", offset=WO, align_bytes=64)
+        bias = placed.tile([P, N // P], F32, name="bias", offset=BIAS, align_bytes=64)
+        nc.sync.dma_start(out=we_raw[:].rearrange("p (a c) -> p a c", a=PASSES), in_=we_words.rearrange("a p c i -> p a (c i)").bitcast(I32))
+        for t in range(SLOTS):
+            nc.sync.dma_start(out=wo_raw[:, t, :], in_=wo.rearrange("(g t e) n -> t g e n", t=SLOTS, e=RUN)[t])
+        with nc.allow_non_contiguous_dma(reason="one bias value a partition"):
+            nc.sync.dma_start(out=bias[:], in_=bo.rearrange("(b p) -> p b", p=P))
+
+        rate = {}
+        growth = {}
+
+        def rate_pass(a, c, u):
+            if a == 0:
+                rate[c, u] = bank()
+            lo = CHUNK * c
+            for s in range(2):
+                cols = slice(P * (2 * u + s), P * (2 * u + s + 1))
+                product(rate[c, u][:, CHUNK * s : CHUNK * (s + 1)], wr_codes[a][:, cols].bitcast(FP8X4), wr_scales[a][:, cols], a, lo, lo + CHUNK,
+                        start=(a == 0 and s == 0), stop=(a == PASSES - 1 and s == 1))
+            if a == PASSES - 1:
+                growth[c, u] = placed.tile([P, CHUNK, 2], F32, name=f"growth{c}{u}", offset=GROWTH + 2048 * (2 * c + u), align_bytes=64)
+                nc.scalar.activation(growth[c, u][:], rate[c, u][:].rearrange("p (s n) -> p n s", s=2), ACT.Exp)
+
+        wr_bf[0] = placed.tile([P, 4 * H], BF16, name="wr_bf0", offset=BF, align_bytes=64)
+        cast_wr(0, 0, 2, nc.vector.tensor_copy)
+        cast_wr(0, 2, 4, nc.vector.tensor_copy)
+        quantise_wr(0, 0)
+        quantise_wr(0, 1)
+        for c in range(2):
+            for u in range(2):
+                rate_pass(0, c, u)
+        ws[0] = placed.tile([P, PASSES * H // 4], I32, name="ws0", offset=WR0, align_bytes=64)
+        reorder(ws[0][:], ws_raw[0][:], RUN // 4)
+        wr_bf[1] = placed.tile([P, 4 * H], BF16, name="wr_bf1", offset=BF, align_bytes=64)
+        cast_wr(1, 0, 2, nc.vector.tensor_copy)
+        cast_wr(1, 2, 3, nc.scalar.copy)
+        cast_wr(1, 3, 4, nc.vector.tensor_copy)
+        quantise_wr(1, 0)
+        quantise_wr(1, 1)
+        we_codes = placed.tile([P, PASSES * H], I32, name="we_codes", offset=BF, align_bytes=64)
+        reorder(we_codes[:], we_raw[:], RUN)
+
+        def cast_wo(wo_bf, b):
+            nc.scalar.copy(
+                wo_bf[:, 512 * b : 512 * (b + 1)].rearrange("p (n t) -> p n t", t=SLOTS),
+                wo_raw[:, :, P * b : P * (b + 1)].rearrange("p t n -> p n t"),
+            )
+
         signal = {}
         h_bf = {}
         h_mx = {}
 
-        def exposure(c):
+        def exposure(c, u):
             lo = CHUNK * c
-            signal[c] = ring.tile([P, 2, CHUNK, 2], F32, name="signal", align_bytes=64)
-            for u in range(2):
-                acc = bank()
-                for s in range(2):
-                    t = 2 * u + s
-                    for a in range(PASSES):
-                        at = 256 * t + 128 * a
-                        product(acc[:, CHUNK * s : CHUNK * (s + 1)], we_codes[:, at : at + 128].bitcast(FP8X4), w_scale(0, a, t), a, lo, lo + CHUNK)
-                nc.vector.tensor_tensor(
-                    signal[c][:, u, :, :],
-                    acc[:].rearrange("p (s n) -> p n s", s=2),
-                    growth[:, 2 * u : 2 * u + 2, lo : lo + CHUNK].rearrange("p s n -> p n s"),
-                    ALU.mult,
-                )
-
-        def background(c, j):
-            if j == 0:
-                h_bf[c] = ring.tile([P, CHUNK * SLOTS], BF16, name="h_bf", align_bytes=64)
-            lo = CHUNK * c + P * j
+            if u == 0:
+                signal[c] = ring.tile([P, 2, CHUNK, 2], F32, name="signal", align_bytes=64)
             acc = bank()
-            for t in range(SLOTS):
+            for s in range(2):
+                t = 2 * u + s
                 for a in range(PASSES):
-                    at = 128 * t + 64 * a
-                    product(acc[:, P * t : P * (t + 1)], wb_codes[:, at : at + 64].bitcast(FP4X4), w_scale(1, a, t), a, lo, lo + P, unpacked=True)
+                    at = 256 * t + 128 * a
+                    product(acc[:, CHUNK * s : CHUNK * (s + 1)], we_codes[:, at : at + 128].bitcast(FP8X4), w_scale(0, a, t), a, lo, lo + CHUNK,
+                            start=(a == 0), stop=(a == PASSES - 1))
             nc.vector.tensor_tensor(
-                h_bf[c][:, 512 * j : 512 * (j + 1)].rearrange("p (n u s) -> p n u s", u=2, s=2),
-                signal[c][:, :, P * j : P * (j + 1), :].rearrange("p u n s -> p n u s"),
-                acc[:].rearrange("p (u s n) -> p n u s", u=2, s=2),
+                signal[c][:, u, :, :],
+                acc[:].rearrange("p (s n) -> p n s", s=2),
+                growth[c, u][:],
+                ALU.mult,
+            )
+
+        def correct(c, lo, width):
+            h_bf[c, lo] = ring.tile([P, width * SLOTS], BF16, name="h_bf", align_bytes=64)
+            first = CHUNK * c + lo
+            nc.vector.tensor_tensor(
+                h_bf[c, lo][:].rearrange("p (n u s) -> p n u s", u=2, s=2),
+                signal[c][:, :, lo : lo + width, :].rearrange("p u n s -> p n u s"),
+                back[:, SLOTS * first : SLOTS * (first + width)].rearrange("p (n u s) -> p n u s", u=2, s=2),
                 ALU.subtract,
             )
 
         def quantise_h(c, lo, width):
             codes = ring.tile([P, width], U32, name="h_codes", align_bytes=64)
             scales = ring.tile([P, width], U8, name="h_scales", align_bytes=64)
-            nc.vector.quantize_mx(out=codes[:].bitcast(FP8X4), scales=scales[:], in_=h_bf[c][:, 4 * lo : 4 * (lo + width)])
+            nc.vector.quantize_mx(out=codes[:].bitcast(FP8X4), scales=scales[:], in_=h_bf[c, lo][:])
             h_mx[c, lo] = (codes, scales)
 
         def readout(c, lo, width, on_vector=False):
@@ -263,24 +270,32 @@ def tile_list_kmer_locus_enrichment_kernel(
             first = CHUNK * c + lo
             nc.sync.dma_start(out=out[:, first : first + width].rearrange("(b p) j -> p b j", p=P), in_=staged[:])
 
-        last = chunks - 1
-        for c in range(chunks):
-            if c == 1:
-                rate_pass(1, 1, (0, 1))
-            exposure(c)
-            if c == 1:
-                rate_pass(1, 1, (2, 3))
-                cast_wo()
+        last = CHUNKS - 1
+        for u in range(2):
+            rate_pass(1, 0, u)
+        for c in range(CHUNKS):
+            exposure(c, 0)
             if c > 0:
                 quantise_h(c - 1, 0, CHUNK)
-            if c == 2:
+            if c < last:
+                for u in range(2):
+                    if c > 0:
+                        rate_pass(0, c + 1, u)
+                    rate_pass(1, c + 1, u)
+            exposure(c, 1)
+            if c == 0:
+                wo_bf = placed.tile([P, N * SLOTS], BF16, name="wo_bf", offset=GROWTH, align_bytes=64)
+                for b in range(N // P):
+                    cast_wo(wo_bf, b)
+            if c == 1:
                 nc.vector.quantize_mx(out=wo_codes[:, 0:256].bitcast(FP8X4), scales=wo_scales[:, 0:256], in_=wo_bf[:, 0:1024])
                 nc.vector.quantize_mx(out=wo_codes[:, 256:384].bitcast(FP8X4), scales=wo_scales[:, 256:384], in_=wo_bf[:, 1024:1536])
-            if c > 1:
-                readout(c - 2, 0, CHUNK)
-            background(c, 0)
-            background(c, 1)
-        readout(last - 1, 0, CHUNK)
+            if c > 0:
+                readout(c - 1, 0, CHUNK)
+            if c < last:
+                correct(c, 0, CHUNK)
+        for j in range(2):
+            correct(last, P * j, P)
         for j in range(2):
             quantise_h(last, P * j, P)
             readout(last, P * j, P, on_vector=(j == 1))

@@ -23,6 +23,10 @@ RUN = 8
 CHUNK = 256
 BANK = 512
 CHUNKS = S // CHUNK
+EARLY = 4
+BACK_BANK = (0, 1, 2, 3, 0, 1, 0, 1)
+RATE_BANK = (6, 4, 4, 4)
+EXPO_BANK = (2, 6, 2, 2)
 
 
 def tile_list_kmer_locus_enrichment_kernel(
@@ -33,79 +37,81 @@ def tile_list_kmer_locus_enrichment_kernel(
         keep = ctx.enter_context(tc.tile_pool(name="keep", bufs=1))
         ring = ctx.enter_context(tc.tile_pool(name="ring", bufs=5))
         placed = ctx.enter_context(tc.tile_pool(name="placed", bufs=1))
-        psum = ctx.enter_context(tc.psum_pool(name="psum", bufs=8))
+        psum = ctx.enter_context(tc.psum_pool(name="psum", bufs=1))
 
-        def bank():
-            return psum.tile([P, BANK], F32, name="bank", tag="bank")
+        def bank(name, index):
+            return psum.tile([P, BANK], F32, name=name, offset=4 * BANK * index)
+
+        def kept(name, shape, dtype):
+            return keep.tile(shape, dtype, name=name, align_bytes=64)
+
+        def at(name, offset, shape, dtype):
+            return placed.tile(shape, dtype, name=name, offset=offset, align_bytes=64)
 
         offsets = keep.tile([P, S // 16], U16, name="offsets")
-        v_scales = keep.tile([P, S], U8, name="v_scales", align_bytes=64)
-        v_scales1 = keep.tile([P, S // 4], I32, name="v_scales1", align_bytes=64)
-        wr_codes = [keep.tile([P, H], U32, name=f"wr_codes{a}", align_bytes=64) for a in range(PASSES)]
-        wr_scales = [keep.tile([P, H], U8, name=f"wr_scales{a}", align_bytes=64) for a in range(PASSES)]
-        ws_raw = [keep.tile([P, PASSES * H // 4], I32, name=f"ws_raw{w}", align_bytes=64) for w in range(2)]
-        ws = {}
-        wr_bf = {}
-        wo_codes = keep.tile([P, N], U32, name="wo_codes", align_bytes=64)
-        wo_scales = keep.tile([P, N], U8, name="wo_scales", align_bytes=64)
-        back = keep.tile([P, SLOTS * S], F32, name="back", align_bytes=64)
-
         nc.sync.dma_start(offsets[:], offs)
-        WB, TAB0, WO, TAB1, GROWTH, TS = 0, 2048, 10240, 16320, 28672, 45056
-        BF, BIAS, WE = TAB1 + 64, TAB1 + 4160, TAB1 + 4224
-        WR0, WR1, WBC, WS1, VC0, END = TS, TS + 8192, TS + 16384, TS + 18432, TS + 19456, TS + 23552
-        zeros = placed.tile([P, (TAB1 + 8192) // 4], I32, name="zeros", offset=0, align_bytes=64)
-        ts_tile = placed.tile([P, (END - TS) // 4], I32, name="ts_tile", offset=TS, align_bytes=64)
+
+        WB, WO, TAB0, TAB1, GROWTH, TS, LATE = 0, 2048, 8128, 16320, 32768, 49152, 81920
+        BIAS, WE, WES = TAB0 + 64, TAB0 + 128, TAB0 + 4224
+        WRC, BF = TAB1, TAB1 + 2048
+        WR1, VC0, WR0, END = TS, TS + 8192, TS + 12288, TS + 20480
+
+        v_scales = kept("v_scales", [P, S], U8)
+        v_scales1 = kept("v_scales1", [P, S // 4], I32)
+        zeros = at("zeros", 0, [P, (TAB1 + 8192) // 4], I32)
+        ts_tile = at("ts_tile", TS, [P, (END - TS) // 4], I32)
         ts_win = ts_tile[:, 0 : T // 4]
-        nc.vector.memset(ts_win, 0)
-        nc.gpsimd.memset(ws_raw[1][:], 0)
+        ws_raw = [kept("wes_raw", [P, PASSES * H // 4], I32), at("wbs_raw", LATE, [P, PASSES * H // 4], I32)]
+        nc.gpsimd.memset(ts_win, 0)
         nc.vector.memset(zeros[:, 0 : S // 4], 0)
         nc.vector.tensor_copy(v_scales1[:], zeros[:, 0 : S // 4])
-        nc.vector.memset(ws_raw[0][:], 0)
+        nc.gpsimd.memset(ws_raw[1][:], 0)
+        nc.gpsimd.memset(ws_raw[0][:], 0)
         for q in range(4):
             nc.sync.dma_start(
                 out=ts_tile[32 * q : 32 * q + 8, 0 : T // 4],
                 in_=tab_scales[:, 4 * q : 4 * q + 4, :].bitcast(I32),
             )
 
-        def load_scales(w, scales, q, queue):
-            queue.dma_start(
-                out=ws_raw[w][32 * q : 32 * q + 4, :].rearrange("p (a c) -> p a c", a=PASSES),
-                in_=scales[:, 4 * q : 4 * q + 4, :].rearrange("a r c -> r a c").bitcast(I32),
-            )
+        def load_scales(w, scales, queue):
+            for q in range(4):
+                queue.dma_start(
+                    out=ws_raw[w][32 * q : 32 * q + 4, :],
+                    in_=scales[:, 4 * q : 4 * q + 4, :].rearrange("a r c -> r a c").bitcast(I32),
+                )
 
-        load_scales(1, wb_scales, 0, nc.sync)
-        wb_raw = placed.tile([P, PASSES * H // 2], I32, name="wb_raw", offset=WB, align_bytes=64)
-        tw_win = [placed.tile([P, T], I32, name=f"tw_win{a}", offset=at, align_bytes=64) for a, at in enumerate((TAB0, TAB1))]
-        nc.sync.dma_start(out=wb_raw[:].rearrange("p (a c) -> p a c", a=PASSES), in_=wb_words.rearrange("a p c -> p a c").bitcast(I32))
-        for a in range(PASSES):
+        wb_raw = at("wb_raw", WB, [P, PASSES * H // 2], I32)
+        tw_win = [at("tw_win0", TAB0, [P, T], I32), at("tw_win1", TAB1, [P, T], I32)]
+
+        def load_table(a):
             nc.sync.dma_start(out=tw_win[a][:], in_=tab_words[a].rearrange("p t i -> p (t i)").bitcast(I32))
-        for q in range(1, 4):
-            load_scales(1, wb_scales, q, nc.gpsimd)
-        for q in range(4):
-            load_scales(0, we_scales, q, nc.gpsimd)
 
-        def gather_words(a, c):
-            lo, hi = CHUNK * c, CHUNK * (c + 1)
+        load_table(0)
+        nc.sync.dma_start(out=wb_raw[:].rearrange("p (a c) -> p a c", a=PASSES), in_=wb_words.rearrange("a p c -> p a c").bitcast(I32))
+        load_scales(1, wb_scales, nc.sync)
+        load_table(1)
+        load_scales(0, we_scales, nc.gpsimd)
+
+        def gather_words(a, lo, hi):
             nc.vector.tensor_copy(
                 v_codes[a][:, lo:hi], tw_win[a][:].bitcast(U32).indirect(offsets[:, lo // 16 : hi // 16])
             )
 
-        def cast_wr(a, t0, t1, engine_copy):
+        def cast_wr(a, u, engine_copy):
             engine_copy(
-                wr_bf[a][:, 512 * t0 : 512 * t1].rearrange("p (t g e i) -> p t g e i", t=t1 - t0, e=RUN, i=4),
-                wr_raw[a][:].rearrange("p (i g t e) -> p t g e i", i=4, t=SLOTS, e=RUN)[:, t0:t1],
+                wr_bf[a, u][:].rearrange("p (t g e i) -> p t g e i", t=2, e=RUN, i=4),
+                wr_raw[a][:].rearrange("p (i g t e) -> p t g e i", i=4, t=SLOTS, e=RUN)[:, 2 * u : 2 * u + 2],
             )
 
         def quantise_wr(a, u):
             nc.vector.quantize_mx(
-                out=wr_codes[a][:, 256 * u : 256 * (u + 1)].bitcast(FP8X4),
+                out=wr_codes[a, u][:].bitcast(FP8X4),
                 scales=wr_scales[a][:, 256 * u : 256 * (u + 1)],
-                in_=wr_bf[a][:, 1024 * u : 1024 * (u + 1)],
+                in_=wr_bf[a, u][:],
             )
 
-        def reorder(dst, src, run):
-            nc.vector.tensor_copy(
+        def reorder(engine, dst, src, run):
+            engine.tensor_copy(
                 dst.rearrange("p (t x e) -> p t x e", t=SLOTS, e=run),
                 src.rearrange("p (x t e) -> p t x e", t=SLOTS, e=run),
             )
@@ -122,90 +128,81 @@ def tile_list_kmer_locus_enrichment_kernel(
             )
 
         def w_scale(w, a, t):
-            at = 64 * t + 32 * a
-            return ws[w][:, at : at + 32].bitcast(U8)
+            first = 64 * t + 32 * a
+            return ws[w][:, first : first + 32].bitcast(U8)
 
         nc.vector.tensor_copy(v_scales[:], ts_win.bitcast(U8).indirect(offsets[:]))
-        nc.sync.dma_start(out=v_scales1[0:100, :], in_=v_scales[4:104, :].bitcast(I32))
-        wr_raw = [placed.tile([P, 4 * H], F32, name=f"wr_raw{a}", offset=at, align_bytes=64) for a, at in enumerate((WR0, WR1))]
+        for dst, rows in ((0, 64), (64, 32), (96, 4)):
+            nc.sync.dma_start(out=v_scales1[dst : dst + rows, :], in_=v_scales[dst + 4 : dst + 4 + rows, :].bitcast(I32))
+        wr_raw = [at("wr_raw0", WR0, [P, 4 * H], F32), at("wr_raw1", WR1, [P, 4 * H], F32)]
         for a in range(PASSES):
             nc.sync.dma_start(out=wr_raw[a][:], in_=wr[512 * a : 512 * (a + 1), :].rearrange("(p i) c -> p (i c)", i=4))
-        wb_codes = placed.tile([P, PASSES * H // 2], I32, name="wb_codes", offset=WBC, align_bytes=64)
-        ws[1] = placed.tile([P, PASSES * H // 4], I32, name="ws1", offset=WS1, align_bytes=64)
-        v_codes = [
-            placed.tile([P, S], U32, name="v_codes0", offset=VC0, align_bytes=64),
-            keep.tile([P, S], U32, name="v_codes1", align_bytes=64),
-        ]
-        reorder(wb_codes[:], wb_raw[:], RUN // 2)
-        reorder(ws[1][:], ws_raw[1][:], RUN // 4)
+        v_codes = [at("v_codes0", VC0, [P, S], U32)]
+        ws = {}
+        wb_codes = kept("wb_codes", [P, PASSES * H // 2], I32)
+        ws[1] = kept("ws1", [P, PASSES * H // 4], I32)
+        reorder(nc.gpsimd, wb_codes[:], wb_raw[:], RUN // 2)
+        reorder(nc.gpsimd, ws[1][:], ws_raw[1][:], RUN // 4)
+        for lo, hi in [[0,256],[256,512],[512,1024]]:
+            gather_words(0, lo, hi)
+        v_codes.append(kept("v_codes1", [P, S], U32))
 
-        back_acc = [bank() for j in range(S // P)]
-
-        def background(a, j):
-            for t in range(SLOTS):
-                at = 128 * t + 64 * a
-                product(back_acc[j][:, P * t : P * (t + 1)], wb_codes[:, at : at + 64].bitcast(FP4X4), w_scale(1, a, t), a, P * j, P * (j + 1),
-                        start=(a == 0 and t == 0), stop=(a == PASSES - 1 and t == SLOTS - 1), unpacked=True)
-            if a == PASSES - 1:
-                nc.scalar.copy(
-                    back[:, BANK * j : BANK * (j + 1)].rearrange("p (n t) -> p n t", t=SLOTS),
-                    back_acc[j][:].rearrange("p (t n) -> p n t", t=SLOTS),
-                )
-
-        for a in range(PASSES):
-            for c in range(CHUNKS):
-                gather_words(a, c)
-                background(a, 2 * c)
-                background(a, 2 * c + 1)
-
-        we_raw = placed.tile([P, PASSES * H], I32, name="we_raw", offset=WE, align_bytes=64)
-        wo_raw = placed.tile([P, SLOTS, N], F32, name="wo_raw", offset=WO, align_bytes=64)
-        bias = placed.tile([P, N // P], F32, name="bias", offset=BIAS, align_bytes=64)
+        we_raw = at("we_raw", WE, [P, PASSES * H], I32)
+        wo_raw = at("wo_raw", WO, [P, SLOTS, N], F32)
+        bias = at("bias", BIAS, [P, N // P], F32)
         nc.sync.dma_start(out=we_raw[:].rearrange("p (a c) -> p a c", a=PASSES), in_=we_words.rearrange("a p c i -> p a (c i)").bitcast(I32))
         for t in range(SLOTS):
             nc.sync.dma_start(out=wo_raw[:, t, :], in_=wo.rearrange("(g t e) n -> t g e n", t=SLOTS, e=RUN)[t])
         with nc.allow_non_contiguous_dma(reason="one bias value a partition"):
             nc.sync.dma_start(out=bias[:], in_=bo.rearrange("(b p) -> p b", p=P))
 
+        back_acc = {}
+        back = {}
+
+        def background(a, j):
+            if a == 0:
+                back_acc[j] = bank(f"back_acc{j}", BACK_BANK[j])
+            for t in range(SLOTS):
+                first = 128 * t + 64 * a
+                product(back_acc[j][:, P * t : P * (t + 1)], wb_codes[:, first : first + 64].bitcast(FP4X4), w_scale(1, a, t), a, P * j, P * (j + 1),
+                        start=(a == 0 and t == 0), stop=(a == PASSES - 1 and t == SLOTS - 1), unpacked=True)
+
+        def keep_background(j):
+            nc.scalar.copy(
+                back[j // 2][:, BANK * (j % 2) : BANK * (j % 2 + 1)].rearrange("p (n t) -> p n t", t=SLOTS),
+                back_acc[j][:].rearrange("p (t n) -> p n t", t=SLOTS),
+            )
+
         rate = {}
         growth = {}
 
         def rate_pass(a, c, u):
             if a == 0:
-                rate[c, u] = bank()
+                rate[c, u] = bank(f"rate{c}{u}", RATE_BANK[c] + u)
             lo = CHUNK * c
             for s in range(2):
                 cols = slice(P * (2 * u + s), P * (2 * u + s + 1))
-                product(rate[c, u][:, CHUNK * s : CHUNK * (s + 1)], wr_codes[a][:, cols].bitcast(FP8X4), wr_scales[a][:, cols], a, lo, lo + CHUNK,
+                product(rate[c, u][:, CHUNK * s : CHUNK * (s + 1)], wr_codes[a, u][:, P * s : P * (s + 1)].bitcast(FP8X4), wr_scales[a][:, cols], a, lo, lo + CHUNK,
                         start=(a == 0 and s == 0), stop=(a == PASSES - 1 and s == 1))
             if a == PASSES - 1:
-                growth[c, u] = placed.tile([P, CHUNK, 2], F32, name=f"growth{c}{u}", offset=GROWTH + 2048 * (2 * c + u), align_bytes=64)
+                growth[c, u] = at(f"growth{c}{u}", GROWTH + 2048 * (2 * c + u), [P, CHUNK, 2], F32)
                 nc.scalar.activation(growth[c, u][:], rate[c, u][:].rearrange("p (s n) -> p n s", s=2), ACT.Exp)
 
-        wr_bf[0] = placed.tile([P, 4 * H], BF16, name="wr_bf0", offset=BF, align_bytes=64)
-        cast_wr(0, 0, 2, nc.vector.tensor_copy)
-        cast_wr(0, 2, 4, nc.vector.tensor_copy)
-        quantise_wr(0, 0)
-        quantise_wr(0, 1)
-        for c in range(2):
-            for u in range(2):
-                rate_pass(0, c, u)
-        ws[0] = placed.tile([P, PASSES * H // 4], I32, name="ws0", offset=WR0, align_bytes=64)
-        reorder(ws[0][:], ws_raw[0][:], RUN // 4)
-        wr_bf[1] = placed.tile([P, 4 * H], BF16, name="wr_bf1", offset=BF, align_bytes=64)
-        cast_wr(1, 0, 2, nc.vector.tensor_copy)
-        cast_wr(1, 2, 3, nc.scalar.copy)
-        cast_wr(1, 3, 4, nc.vector.tensor_copy)
-        quantise_wr(1, 0)
-        quantise_wr(1, 1)
-        we_codes = placed.tile([P, PASSES * H], I32, name="we_codes", offset=BF, align_bytes=64)
-        reorder(we_codes[:], we_raw[:], RUN)
+        wr_bf = {(1, 1): kept("wr_bf11", [P, 2 * H], BF16)}
+        wr_scales = [kept(f"wr_scales{a}", [P, H], U8) for a in range(PASSES)]
+        wo_codes = kept("wo_codes", [P, N], U32)
+        wo_scales = kept("wo_scales", [P, N], U8)
 
-        def cast_wo(wo_bf, b):
-            nc.scalar.copy(
+        def cast_wo(b):
+            nc.gpsimd.tensor_scalar(
                 wo_bf[:, 512 * b : 512 * (b + 1)].rearrange("p (n t) -> p n t", t=SLOTS),
                 wo_raw[:, :, P * b : P * (b + 1)].rearrange("p t n -> p n t"),
+                1.0, 0.0, ALU.mult, ALU.add,
             )
+
+        def quantise_wo():
+            nc.vector.quantize_mx(out=wo_codes[:, 0:256].bitcast(FP8X4), scales=wo_scales[:, 0:256], in_=wo_bf[:, 0:1024])
+            nc.vector.quantize_mx(out=wo_codes[:, 256:384].bitcast(FP8X4), scales=wo_scales[:, 256:384], in_=wo_bf[:, 1024:1536])
 
         signal = {}
         h_bf = {}
@@ -215,12 +212,12 @@ def tile_list_kmer_locus_enrichment_kernel(
             lo = CHUNK * c
             if u == 0:
                 signal[c] = ring.tile([P, 2, CHUNK, 2], F32, name="signal", align_bytes=64)
-            acc = bank()
+            acc = bank(f"expo{c}{u}", EXPO_BANK[c] + u)
             for s in range(2):
                 t = 2 * u + s
                 for a in range(PASSES):
-                    at = 256 * t + 128 * a
-                    product(acc[:, CHUNK * s : CHUNK * (s + 1)], we_codes[:, at : at + 128].bitcast(FP8X4), w_scale(0, a, t), a, lo, lo + CHUNK,
+                    first = 256 * t + 128 * a
+                    product(acc[:, CHUNK * s : CHUNK * (s + 1)], we_codes[:, first : first + 128].bitcast(FP8X4), w_scale(0, a, t), a, lo, lo + CHUNK,
                             start=(a == 0), stop=(a == PASSES - 1))
             nc.vector.tensor_tensor(
                 signal[c][:, u, :, :],
@@ -229,28 +226,32 @@ def tile_list_kmer_locus_enrichment_kernel(
                 ALU.mult,
             )
 
-        def correct(c, lo, width):
-            h_bf[c, lo] = ring.tile([P, width * SLOTS], BF16, name="h_bf", align_bytes=64)
-            first = CHUNK * c + lo
-            nc.vector.tensor_tensor(
-                h_bf[c, lo][:].rearrange("p (n u s) -> p n u s", u=2, s=2),
+        def correct(c, lo, width, engine):
+            if lo == 0:
+                h_bf[c] = ring.tile([P, CHUNK * SLOTS], BF16, name="h_bf", align_bytes=64)
+            if c in back:
+                taken = back[c][:, SLOTS * lo : SLOTS * (lo + width)].rearrange("p (n u s) -> p n u s", u=2, s=2)
+            else:
+                taken = back_acc[2 * c + lo // P][:].rearrange("p (u s n) -> p n u s", u=2, s=2)
+            engine.tensor_tensor(
+                h_bf[c][:, SLOTS * lo : SLOTS * (lo + width)].rearrange("p (n u s) -> p n u s", u=2, s=2),
                 signal[c][:, :, lo : lo + width, :].rearrange("p u n s -> p n u s"),
-                back[:, SLOTS * first : SLOTS * (first + width)].rearrange("p (n u s) -> p n u s", u=2, s=2),
+                taken,
                 ALU.subtract,
             )
 
         def quantise_h(c, lo, width):
             codes = ring.tile([P, width], U32, name="h_codes", align_bytes=64)
             scales = ring.tile([P, width], U8, name="h_scales", align_bytes=64)
-            nc.vector.quantize_mx(out=codes[:].bitcast(FP8X4), scales=scales[:], in_=h_bf[c, lo][:])
+            nc.vector.quantize_mx(out=codes[:].bitcast(FP8X4), scales=scales[:], in_=h_bf[c][:, SLOTS * lo : SLOTS * (lo + width)])
             h_mx[c, lo] = (codes, scales)
 
-        def readout(c, lo, width, on_vector=False):
+        def readout(c, lo, width, first_bank, on_vector=False):
             codes, scales = h_mx[c, lo]
             blocks = N // P
             staged = ring.tile([P, blocks, width], F32, name="staged", align_bytes=64)
             per_bank = min(blocks, BANK // width)
-            accs = [bank() for first in range(0, blocks, per_bank)]
+            accs = [bank(f"sum{c}{lo}{first}", first_bank + first // per_bank) for first in range(0, blocks, per_bank)]
             sums = [accs[b // per_bank][:, width * (b % per_bank) : width * (b % per_bank + 1)] for b in range(blocks)]
             for b in range(blocks):
                 nc.tensor.matmul_mx(
@@ -270,32 +271,72 @@ def tile_list_kmer_locus_enrichment_kernel(
             first = CHUNK * c + lo
             nc.sync.dma_start(out=out[:, first : first + width].rearrange("(b p) j -> p b j", p=P), in_=staged[:])
 
-        last = CHUNKS - 1
-        for u in range(2):
-            rate_pass(1, 0, u)
-        for c in range(CHUNKS):
-            exposure(c, 0)
-            if c > 0:
-                quantise_h(c - 1, 0, CHUNK)
-            if c < last:
-                for u in range(2):
-                    if c > 0:
-                        rate_pass(0, c + 1, u)
-                    rate_pass(1, c + 1, u)
-            exposure(c, 1)
+        ws[0] = at("ws0", LATE, [P, PASSES * H // 4], I32)
+        reorder(nc.gpsimd, ws[0][:], ws_raw[0][:], RUN // 4)
+        for j in range(EARLY):
+            background(0, j)
+        for lo, hi in ((0, 256), (256, 512), (512, S)):
+            gather_words(1, lo, hi)
+        wr_bf[0, 0] = at("wr_bf00", BF + 2048, [P, 2 * H], BF16)
+        wr_bf[0, 1] = at("wr_bf01", BF, [P, 2 * H], BF16)
+        cast_wr(0, 0, nc.vector.tensor_copy)
+        cast_wr(0, 1, nc.vector.tensor_copy)
+        back[0] = kept("back0", [P, 2 * BANK], F32)
+        back[1] = kept("back1", [P, 2 * BANK], F32)
+        for j in range(EARLY):
+            background(1, j)
+            keep_background(j)
+        for j in range(EARLY, 6):
+            background(0, j)
+            background(1, j)
+        wr_codes = {(0, 0): kept("wr_codes00", [P, 256], U32), (0, 1): kept("wr_codes01", [P, 256], U32), (1, 0): kept("wr_codes10", [P, 256], U32)}
+        quantise_wr(0, 0)
+        quantise_wr(0, 1)
+        wr_bf[1, 0] = at("wr_bf10", BF + 2048, [P, 2 * H], BF16)
+        cast_wr(1, 0, nc.vector.tensor_copy)
+        cast_wr(1, 1, nc.scalar.copy)
+        for c in range(2):
+            for u in range(2):
+                rate_pass(0, c, u)
+        quantise_wr(1, 0)
+        we_codes = at("we_codes", BF + 2048, [P, PASSES * H], I32)
+        reorder(nc.vector, we_codes[:], we_raw[:], RUN)
+        wr_codes[1, 1] = at("wr_codes11", WE, [P, 256], U32)
+        quantise_wr(1, 1)
+        wo_bf = kept("wo_bf", [P, N * SLOTS], BF16)
+        for b in range(N // P):
+            cast_wo(b)
+        for c in range(2):
+            for u in range(2):
+                rate_pass(1, c, u)
+                exposure(c, u)
             if c == 0:
-                wo_bf = placed.tile([P, N * SLOTS], BF16, name="wo_bf", offset=GROWTH, align_bytes=64)
-                for b in range(N // P):
-                    cast_wo(wo_bf, b)
-            if c == 1:
-                nc.vector.quantize_mx(out=wo_codes[:, 0:256].bitcast(FP8X4), scales=wo_scales[:, 0:256], in_=wo_bf[:, 0:1024])
-                nc.vector.quantize_mx(out=wo_codes[:, 256:384].bitcast(FP8X4), scales=wo_scales[:, 256:384], in_=wo_bf[:, 1024:1536])
-            if c > 0:
-                readout(c - 1, 0, CHUNK)
-            if c < last:
-                correct(c, 0, CHUNK)
+                quantise_wo()
+            correct(c, 0, P, nc.gpsimd)
+            correct(c, P, P, nc.gpsimd)
+        for u in range(2):
+            rate_pass(0, 2, u)
+            rate_pass(1, 2, u)
+        for u in range(2):
+            exposure(2, u)
+        quantise_h(0, 0, CHUNK)
+        readout(0, 0, CHUNK, 6)
+        for u in range(2):
+            rate_pass(0, 3, u)
+            rate_pass(1, 3, u)
+        correct(2, 0, P, nc.vector)
+        correct(2, P, P, nc.vector)
+        exposure(3, 0)
+        quantise_h(2, 0, CHUNK)
+        exposure(3, 1)
+        readout(2, 0, CHUNK, 4)
+        quantise_h(1, 0, CHUNK)
+        readout(1, 0, CHUNK, 6)
         for j in range(2):
-            correct(last, P * j, P)
+            background(0, 6 + j)
+            background(1, 6 + j)
         for j in range(2):
-            quantise_h(last, P * j, P)
-            readout(last, P * j, P, on_vector=(j == 1))
+            correct(3, P * j, P, nc.vector)
+        for j in range(2):
+            quantise_h(3, P * j, P)
+            readout(3, P * j, P, 2 + j, on_vector=(j == 1))

@@ -23,10 +23,10 @@ RUN = 8
 CHUNK = 256
 BANK = 512
 CHUNKS = S // CHUNK
-EARLY = 4
-BACK_BANK = (0, 1, 2, 3, 0, 1, 0, 1)
-RATE_BANK = (6, 4, 4, 4)
-EXPO_BANK = (2, 6, 2, 2)
+EARLY = 2
+BACK_BANK = (0, 1, 2, 3, 6, 7, 6, 7)
+RATE_BANK = (4, 4, 4, 4)
+EXPO_BANK = (0, 0, 0, 0)
 
 
 def tile_list_kmer_locus_enrichment_kernel(
@@ -56,22 +56,17 @@ def tile_list_kmer_locus_enrichment_kernel(
         WRC, BF = TAB1, TAB1 + 2048
         WR1, VC0, WR0, END = TS, TS + 8192, TS + 12288, TS + 20480
 
-        v_scales = kept("v_scales", [P, S], U8)
-        v_scales1 = kept("v_scales1", [P, S // 4], I32)
-        zeros = at("zeros", 0, [P, (TAB1 + 8192) // 4], I32)
+        v_rows = kept("v_rows", [P, S], U8)
+        v_scales = kept("v_scales", [P, PASSES * S // 4], I32)
         ts_tile = at("ts_tile", TS, [P, (END - TS) // 4], I32)
         ts_win = ts_tile[:, 0 : T // 4]
-        ws_raw = [kept("wes_raw", [P, PASSES * H // 4], I32), at("wbs_raw", LATE, [P, PASSES * H // 4], I32)]
-        nc.gpsimd.memset(ts_win, 0)
-        nc.vector.memset(zeros[:, 0 : S // 4], 0)
-        nc.vector.tensor_copy(v_scales1[:], zeros[:, 0 : S // 4])
+        ws_raw = [kept("wes_raw", [P, PASSES * H // 4], I32), kept("wbs_raw", [P, PASSES * H // 4], I32)]
+        nc.sync.dma_start(out=ts_tile[0:32, 0 : T // 4], in_=tab_scales.rearrange("a r t -> r a t").bitcast(I32))
         nc.gpsimd.memset(ws_raw[1][:], 0)
         nc.gpsimd.memset(ws_raw[0][:], 0)
-        for q in range(4):
-            nc.sync.dma_start(
-                out=ts_tile[32 * q : 32 * q + 8, 0 : T // 4],
-                in_=tab_scales[:, 4 * q : 4 * q + 4, :].bitcast(I32),
-            )
+        nc.vector.memset(ts_tile[32:64, 0 : T // 4], 0)
+        nc.vector.memset(ts_tile[64:128, 0 : T // 4], 0)
+        nc.vector.memset(v_scales[:], 0)
 
         def load_scales(w, scales, queue):
             for q in range(4):
@@ -116,11 +111,8 @@ def tile_list_kmer_locus_enrichment_kernel(
                 src.rearrange("p (x t e) -> p t x e", t=SLOTS, e=run),
             )
 
-        def product(dst, codes, scales, a, lo, hi, start, stop, unpacked=False):
-            if unpacked and a == 1:
-                plane = v_scales1[:, lo // 4 : hi // 4].bitcast(U8)
-            else:
-                plane = v_scales[4 * a : P, lo:hi]
+        def product(dst, codes, scales, a, lo, hi, start, stop):
+            plane = v_scales[:, (S * a + lo) // 4 : (S * a + hi) // 4].bitcast(U8)
             nc.tensor.matmul_mx(
                 out=dst, lhsT=codes, lhsT_scale=scales,
                 rhs=v_codes[a][:, lo:hi].bitcast(FP8X4), rhs_scale=plane,
@@ -131,20 +123,20 @@ def tile_list_kmer_locus_enrichment_kernel(
             first = 64 * t + 32 * a
             return ws[w][:, first : first + 32].bitcast(U8)
 
-        nc.vector.tensor_copy(v_scales[:], ts_win.bitcast(U8).indirect(offsets[:]))
-        for dst, rows in ((0, 64), (64, 32), (96, 4)):
-            nc.sync.dma_start(out=v_scales1[dst : dst + rows, :], in_=v_scales[dst + 4 : dst + 4 + rows, :].bitcast(I32))
+        nc.vector.tensor_copy(v_rows[:], ts_win.bitcast(U8).indirect(offsets[:]))
+        for q in range(4):
+            nc.sync.dma_start(out=v_scales[32 * q : 32 * q + 4, :], in_=v_rows[8 * q : 8 * q + 8, :].bitcast(I32))
         wr_raw = [at("wr_raw0", WR0, [P, 4 * H], F32), at("wr_raw1", WR1, [P, 4 * H], F32)]
         for a in range(PASSES):
             nc.sync.dma_start(out=wr_raw[a][:], in_=wr[512 * a : 512 * (a + 1), :].rearrange("(p i) c -> p (i c)", i=4))
-        v_codes = [at("v_codes0", VC0, [P, S], U32)]
+        v_codes = [kept("v_codes0", [P, S], U32)]
         ws = {}
+        for lo, hi in [[0,1024]]:
+            gather_words(0, lo, hi)
         wb_codes = kept("wb_codes", [P, PASSES * H // 2], I32)
         ws[1] = kept("ws1", [P, PASSES * H // 4], I32)
-        reorder(nc.gpsimd, wb_codes[:], wb_raw[:], RUN // 2)
-        reorder(nc.gpsimd, ws[1][:], ws_raw[1][:], RUN // 4)
-        for lo, hi in [[0,256],[256,512],[512,1024]]:
-            gather_words(0, lo, hi)
+        reorder(nc.vector, wb_codes[:], wb_raw[:], RUN // 2)
+        reorder(nc.vector, ws[1][:], ws_raw[1][:], RUN // 4)
         v_codes.append(kept("v_codes1", [P, S], U32))
 
         we_raw = at("we_raw", WE, [P, PASSES * H], I32)
@@ -165,7 +157,7 @@ def tile_list_kmer_locus_enrichment_kernel(
             for t in range(SLOTS):
                 first = 128 * t + 64 * a
                 product(back_acc[j][:, P * t : P * (t + 1)], wb_codes[:, first : first + 64].bitcast(FP4X4), w_scale(1, a, t), a, P * j, P * (j + 1),
-                        start=(a == 0 and t == 0), stop=(a == PASSES - 1 and t == SLOTS - 1), unpacked=True)
+                        start=(a == 0 and t == 0), stop=(a == PASSES - 1 and t == SLOTS - 1))
 
         def keep_background(j):
             nc.scalar.copy(
@@ -194,10 +186,9 @@ def tile_list_kmer_locus_enrichment_kernel(
         wo_scales = kept("wo_scales", [P, N], U8)
 
         def cast_wo(b):
-            nc.gpsimd.tensor_scalar(
+            nc.scalar.copy(
                 wo_bf[:, 512 * b : 512 * (b + 1)].rearrange("p (n t) -> p n t", t=SLOTS),
                 wo_raw[:, :, P * b : P * (b + 1)].rearrange("p t n -> p n t"),
-                1.0, 0.0, ALU.mult, ALU.add,
             )
 
         def quantise_wo():
@@ -271,72 +262,79 @@ def tile_list_kmer_locus_enrichment_kernel(
             first = CHUNK * c + lo
             nc.sync.dma_start(out=out[:, first : first + width].rearrange("(b p) j -> p b j", p=P), in_=staged[:])
 
-        ws[0] = at("ws0", LATE, [P, PASSES * H // 4], I32)
-        reorder(nc.gpsimd, ws[0][:], ws_raw[0][:], RUN // 4)
-        for j in range(EARLY):
+        for j in range(4):
             background(0, j)
         for lo, hi in ((0, 256), (256, 512), (512, S)):
             gather_words(1, lo, hi)
-        wr_bf[0, 0] = at("wr_bf00", BF + 2048, [P, 2 * H], BF16)
-        wr_bf[0, 1] = at("wr_bf01", BF, [P, 2 * H], BF16)
-        cast_wr(0, 0, nc.vector.tensor_copy)
+        wr_bf[0, 0] = kept("wr_bf00", [P, 2 * H], BF16)
+        wr_bf[0, 1] = at("wr_bf01", LATE + 8192, [P, 2 * H], BF16)
+        wr_bf[1, 0] = at("wr_bf10", LATE + 12288, [P, 2 * H], BF16)
         cast_wr(0, 1, nc.vector.tensor_copy)
+        cast_wr(0, 0, nc.vector.tensor_copy)
         back[0] = kept("back0", [P, 2 * BANK], F32)
-        back[1] = kept("back1", [P, 2 * BANK], F32)
-        for j in range(EARLY):
+        for j in range(4):
             background(1, j)
-            keep_background(j)
-        for j in range(EARLY, 6):
+            if j < EARLY:
+                keep_background(j)
+        for j in (4, 5):
             background(0, j)
             background(1, j)
-        wr_codes = {(0, 0): kept("wr_codes00", [P, 256], U32), (0, 1): kept("wr_codes01", [P, 256], U32), (1, 0): kept("wr_codes10", [P, 256], U32)}
-        quantise_wr(0, 0)
+        wr_codes = {(a, u): kept(f"wr_codes{a}{u}", [P, 256], U32) for a in range(PASSES) for u in range(2)}
         quantise_wr(0, 1)
-        wr_bf[1, 0] = at("wr_bf10", BF + 2048, [P, 2 * H], BF16)
+        quantise_wr(0, 0)
+        ws[0] = at("ws0", LATE + 8192, [P, PASSES * H // 4], I32)
+        reorder(nc.vector, ws[0][:], ws_raw[0][:], RUN // 4)
         cast_wr(1, 0, nc.vector.tensor_copy)
         cast_wr(1, 1, nc.scalar.copy)
-        for c in range(2):
-            for u in range(2):
-                rate_pass(0, c, u)
+        for u in range(2):
+            rate_pass(0, 0, u)
         quantise_wr(1, 0)
-        we_codes = at("we_codes", BF + 2048, [P, PASSES * H], I32)
-        reorder(nc.vector, we_codes[:], we_raw[:], RUN)
-        wr_codes[1, 1] = at("wr_codes11", WE, [P, 256], U32)
         quantise_wr(1, 1)
-        wo_bf = kept("wo_bf", [P, N * SLOTS], BF16)
+        we_codes = at("we_codes", LATE + 12288, [P, PASSES * H], I32)
+        for u in range(2):
+            nc.vector.tensor_copy(
+                we_codes[:, H * u : H * (u + 1)].rearrange("p (t x e) -> p t x e", t=2, e=RUN),
+                we_raw[:].rearrange("p (x t e) -> p t x e", t=SLOTS, e=RUN)[:, 2 * u : 2 * u + 2],
+            )
+        for u in range(2):
+            rate_pass(1, 0, u)
+        for u in range(2):
+            exposure(0, u)
+        for u in range(2):
+            rate_pass(0, 1, u)
+            rate_pass(1, 1, u)
+        wo_bf = at("wo_bf", GROWTH - 3072 + 64, [P, N * SLOTS], BF16)
         for b in range(N // P):
             cast_wo(b)
-        for c in range(2):
-            for u in range(2):
-                rate_pass(1, c, u)
-                exposure(c, u)
-            if c == 0:
-                quantise_wo()
-            correct(c, 0, P, nc.gpsimd)
-            correct(c, P, P, nc.gpsimd)
+        correct(0, 0, CHUNK, nc.vector)
+        exposure(1, 0)
+        quantise_h(0, 0, CHUNK)
+        exposure(1, 1)
         for u in range(2):
             rate_pass(0, 2, u)
             rate_pass(1, 2, u)
-        for u in range(2):
-            exposure(2, u)
-        quantise_h(0, 0, CHUNK)
-        readout(0, 0, CHUNK, 6)
+        quantise_wo()
+        correct(1, 0, P, nc.vector)
+        correct(1, P, P, nc.vector)
+        exposure(2, 0)
+        quantise_h(1, 0, CHUNK)
+        readout(0, 0, CHUNK, 2)
+        exposure(2, 1)
         for u in range(2):
             rate_pass(0, 3, u)
             rate_pass(1, 3, u)
+        readout(1, 0, CHUNK, 2)
+        exposure(3, 0)
         correct(2, 0, P, nc.vector)
         correct(2, P, P, nc.vector)
-        exposure(3, 0)
-        quantise_h(2, 0, CHUNK)
         exposure(3, 1)
-        readout(2, 0, CHUNK, 4)
-        quantise_h(1, 0, CHUNK)
-        readout(1, 0, CHUNK, 6)
+        quantise_h(2, 0, CHUNK)
         for j in range(2):
             background(0, 6 + j)
             background(1, 6 + j)
+        readout(2, 0, CHUNK, 2)
         for j in range(2):
             correct(3, P * j, P, nc.vector)
         for j in range(2):
             quantise_h(3, P * j, P)
-            readout(3, P * j, P, 2 + j, on_vector=(j == 1))
+            readout(3, P * j, P, 4 + j, on_vector=(j == 1))

@@ -68,8 +68,8 @@ def tile_list_kmer_locus_enrichment_kernel(
         nc.vector.memset(ts_tile[64:128, 0 : T // 4], 0)
         nc.vector.memset(v_scales[:], 0)
 
-        def load_scales(w, scales, queue):
-            for q in range(4):
+        def load_scales(w, scales, queue, quadrants):
+            for q in quadrants:
                 queue.dma_start(
                     out=ws_raw[w][32 * q : 32 * q + 4, :],
                     in_=scales[:, 4 * q : 4 * q + 4, :].rearrange("a r c -> r a c").bitcast(I32),
@@ -83,9 +83,10 @@ def tile_list_kmer_locus_enrichment_kernel(
 
         load_table(0)
         nc.sync.dma_start(out=wb_raw[:].rearrange("p (a c) -> p a c", a=PASSES), in_=wb_words.rearrange("a p c -> p a c").bitcast(I32))
-        load_scales(1, wb_scales, nc.sync)
+        load_scales(1, wb_scales, nc.sync, range(4))
         load_table(1)
-        load_scales(0, we_scales, nc.gpsimd)
+        load_scales(0, we_scales, nc.sync, (0, 1))
+        load_scales(0, we_scales, nc.gpsimd, (2, 3))
 
         def gather_words(a, lo, hi):
             nc.vector.tensor_copy(
@@ -96,6 +97,12 @@ def tile_list_kmer_locus_enrichment_kernel(
             engine_copy(
                 wr_bf[a, u][:].rearrange("p (t g e i) -> p t g e i", t=2, e=RUN, i=4),
                 wr_raw[a][:].rearrange("p (i g t e) -> p t g e i", i=4, t=SLOTS, e=RUN)[:, 2 * u : 2 * u + 2],
+            )
+
+        def cast_slot(a, t, engine_copy):
+            engine_copy(
+                wr_bf[a, t // 2][:, H * (t % 2) : H * (t % 2 + 1)].rearrange("p (g e i) -> p g e i", e=RUN, i=4),
+                wr_raw[a][:].rearrange("p (i g t e) -> p t g e i", i=4, t=SLOTS, e=RUN)[:, t],
             )
 
         def quantise_wr(a, u):
@@ -196,10 +203,11 @@ def tile_list_kmer_locus_enrichment_kernel(
             nc.vector.quantize_mx(out=wo_codes[:, 256:384].bitcast(FP8X4), scales=wo_scales[:, 256:384], in_=wo_bf[:, 1024:1536])
 
         signal = {}
+        expo = {}
         h_bf = {}
         h_mx = {}
 
-        def exposure(c, u):
+        def exposure(c, u, pieces=((0, CHUNK),)):
             lo = CHUNK * c
             if u == 0:
                 signal[c] = ring.tile([P, 2, CHUNK, 2], F32, name="signal", align_bytes=64)
@@ -210,10 +218,15 @@ def tile_list_kmer_locus_enrichment_kernel(
                     first = 256 * t + 128 * a
                     product(acc[:, CHUNK * s : CHUNK * (s + 1)], we_codes[:, first : first + 128].bitcast(FP8X4), w_scale(0, a, t), a, lo, lo + CHUNK,
                             start=(a == 0), stop=(a == PASSES - 1))
+            expo[c, u] = acc
+            for first, width in pieces:
+                grow(c, u, first, width)
+
+        def grow(c, u, first, width):
             nc.vector.tensor_tensor(
-                signal[c][:, u, :, :],
-                acc[:].rearrange("p (s n) -> p n s", s=2),
-                growth[c, u][:],
+                signal[c][:, u, first : first + width, :],
+                expo[c, u][:].rearrange("p (s n) -> p n s", s=2)[:, first : first + width],
+                growth[c, u][:, first : first + width],
                 ALU.mult,
             )
 
@@ -223,7 +236,7 @@ def tile_list_kmer_locus_enrichment_kernel(
             if c in back:
                 taken = back[c][:, SLOTS * lo : SLOTS * (lo + width)].rearrange("p (n u s) -> p n u s", u=2, s=2)
             else:
-                taken = back_acc[2 * c + lo // P][:].rearrange("p (u s n) -> p n u s", u=2, s=2)
+                taken = back_acc[2 * c + lo // P][:].rearrange("p (u s n) -> p n u s", u=2, s=2)[:, lo % P : lo % P + width]
             engine.tensor_tensor(
                 h_bf[c][:, SLOTS * lo : SLOTS * (lo + width)].rearrange("p (n u s) -> p n u s", u=2, s=2),
                 signal[c][:, :, lo : lo + width, :].rearrange("p u n s -> p n u s"),
@@ -266,9 +279,11 @@ def tile_list_kmer_locus_enrichment_kernel(
             background(0, j)
         for lo, hi in ((0, 256), (256, 512), (512, S)):
             gather_words(1, lo, hi)
+        ws[0] = kept("ws0", [P, PASSES * H // 4], I32)
+        reorder(nc.vector, ws[0][:], ws_raw[0][:], RUN // 4)
         wr_bf[0, 0] = kept("wr_bf00", [P, 2 * H], BF16)
-        wr_bf[0, 1] = at("wr_bf01", LATE + 8192, [P, 2 * H], BF16)
-        wr_bf[1, 0] = at("wr_bf10", LATE + 12288, [P, 2 * H], BF16)
+        wr_bf[0, 1] = kept("wr_bf01", [P, 2 * H], BF16)
+        wr_bf[1, 0] = kept("wr_bf10", [P, 2 * H], BF16)
         cast_wr(0, 1, nc.vector.tensor_copy)
         cast_wr(0, 0, nc.vector.tensor_copy)
         back[0] = kept("back0", [P, 2 * BANK], F32)
@@ -282,15 +297,15 @@ def tile_list_kmer_locus_enrichment_kernel(
         wr_codes = {(a, u): kept(f"wr_codes{a}{u}", [P, 256], U32) for a in range(PASSES) for u in range(2)}
         quantise_wr(0, 1)
         quantise_wr(0, 0)
-        ws[0] = at("ws0", LATE + 8192, [P, PASSES * H // 4], I32)
-        reorder(nc.vector, ws[0][:], ws_raw[0][:], RUN // 4)
-        cast_wr(1, 0, nc.vector.tensor_copy)
-        cast_wr(1, 1, nc.scalar.copy)
+        cast_slot(1, 0, nc.vector.tensor_copy)
+        cast_slot(1, 1, nc.scalar.copy)
+        cast_slot(1, 2, nc.vector.tensor_copy)
+        cast_slot(1, 3, nc.scalar.copy)
         for u in range(2):
             rate_pass(0, 0, u)
         quantise_wr(1, 0)
         quantise_wr(1, 1)
-        we_codes = at("we_codes", LATE + 12288, [P, PASSES * H], I32)
+        we_codes = kept("we_codes", [P, PASSES * H], I32)
         for u in range(2):
             nc.vector.tensor_copy(
                 we_codes[:, H * u : H * (u + 1)].rearrange("p (t x e) -> p t x e", t=2, e=RUN),
@@ -316,25 +331,31 @@ def tile_list_kmer_locus_enrichment_kernel(
         quantise_wo()
         correct(1, 0, P, nc.vector)
         correct(1, P, P, nc.vector)
-        exposure(2, 0)
-        quantise_h(1, 0, CHUNK)
         readout(0, 0, CHUNK, 2)
+        exposure(2, 0)
         exposure(2, 1)
+        quantise_h(1, 0, CHUNK)
         for u in range(2):
             rate_pass(0, 3, u)
             rate_pass(1, 3, u)
         readout(1, 0, CHUNK, 2)
-        exposure(3, 0)
         correct(2, 0, P, nc.vector)
         correct(2, P, P, nc.vector)
-        exposure(3, 1)
+        exposure(3, 0, ((0, P),))
         quantise_h(2, 0, CHUNK)
+        exposure(3, 1, ((0, P),))
+        readout(2, 0, CHUNK, 2)
         for j in range(2):
             background(0, 6 + j)
             background(1, 6 + j)
-        readout(2, 0, CHUNK, 2)
-        for j in range(2):
-            correct(3, P * j, P, nc.vector)
-        for j in range(2):
-            quantise_h(3, P * j, P)
-            readout(3, P * j, P, 4 + j, on_vector=(j == 1))
+        grow(3, 0, P, P)
+        correct(3, 0, P, nc.vector)
+        grow(3, 1, P, P)
+        quantise_h(3, 0, P)
+        readout(3, 0, P, 4)
+        correct(3, P, 64, nc.vector)
+        correct(3, P + 64, 64, nc.vector)
+        quantise_h(3, P, 64)
+        readout(3, P, 64, 5)
+        quantise_h(3, P + 64, 64)
+        readout(3, P + 64, 64, 0, on_vector=True)

@@ -86,7 +86,6 @@ def tile_list_kmer_locus_enrichment_kernel(
         load_scales(1, wb_scales, nc.sync, range(4))
         load_table(1)
         load_scales(0, we_scales, nc.sync, (0, 1))
-        load_scales(0, we_scales, nc.gpsimd, (2, 3))
 
         def gather_words(a, lo, hi):
             nc.vector.tensor_copy(
@@ -136,6 +135,8 @@ def tile_list_kmer_locus_enrichment_kernel(
         wr_raw = [at("wr_raw0", WR0, [P, 4 * H], F32), at("wr_raw1", WR1, [P, 4 * H], F32)]
         for a in range(PASSES):
             nc.sync.dma_start(out=wr_raw[a][:], in_=wr[512 * a : 512 * (a + 1), :].rearrange("(p i) c -> p (i c)", i=4))
+            if a == 0:
+                load_scales(0, we_scales, nc.sync, (2, 3))
         v_codes = [kept("v_codes0", [P, S], U32)]
         ws = {}
         for lo, hi in [[0,1024]]:

@@ -23,10 +23,10 @@ RUN = 8
 CHUNK = 256
 BANK = 512
 CHUNKS = S // CHUNK
-EARLY = 2
-BACK_BANK = (0, 1, 2, 3, 6, 7, 6, 7)
+BACK_BANK = (4, 2, 5, 3, 0, 6, 1, 7)
 RATE_BANK = (4, 4, 4, 4)
 EXPO_BANK = (0, 0, 0, 0)
+WARMUP = 4
 
 
 def tile_list_kmer_locus_enrichment_kernel(
@@ -56,6 +56,16 @@ def tile_list_kmer_locus_enrichment_kernel(
         WRC, BF = TAB1, TAB1 + 2048
         WR1, VC0, WR0, END = TS, TS + 8192, TS + 12288, TS + 20480
 
+        G00 = GROWTH
+        WO_HEAD = G00 + 2048 - 64
+        H2 = WO_HEAD + 2048 - 64
+        H4 = H2 + 1024 - 64
+        WO_TAIL = H4 + 1024 - 64
+        G11 = WO_TAIL + 1024 - 64
+        FREE = LATE
+        H_AT = (H2 + 64, FREE + 8192, H2, FREE + 9216, H4, FREE + 10240)
+        GROWTH_AT = (G00, FREE, FREE + 2048, G11, FREE + 4096, FREE + 6144, FREE + 12288, FREE + 14336)
+        CODES_AT = (GROWTH_AT[2], GROWTH_AT[4], GROWTH_AT[6])
         v_rows = kept("v_rows", [P, S], U8)
         v_scales = kept("v_scales", [P, PASSES * S // 4], I32)
         ts_tile = at("ts_tile", TS, [P, (END - TS) // 4], I32)
@@ -168,8 +178,9 @@ def tile_list_kmer_locus_enrichment_kernel(
                         start=(a == 0 and t == 0), stop=(a == PASSES - 1 and t == SLOTS - 1))
 
         def keep_background(j):
+            back[j] = kept(f"back{j}", [P, BANK], F32)
             nc.scalar.copy(
-                back[j // 2][:, BANK * (j % 2) : BANK * (j % 2 + 1)].rearrange("p (n t) -> p n t", t=SLOTS),
+                back[j][:].rearrange("p (n t) -> p n t", t=SLOTS),
                 back_acc[j][:].rearrange("p (t n) -> p n t", t=SLOTS),
             )
 
@@ -185,7 +196,7 @@ def tile_list_kmer_locus_enrichment_kernel(
                 product(rate[c, u][:, CHUNK * s : CHUNK * (s + 1)], wr_codes[a, u][:, P * s : P * (s + 1)].bitcast(FP8X4), wr_scales[a][:, cols], a, lo, lo + CHUNK,
                         start=(a == 0 and s == 0), stop=(a == PASSES - 1 and s == 1))
             if a == PASSES - 1:
-                growth[c, u] = at(f"growth{c}{u}", GROWTH + 2048 * (2 * c + u), [P, CHUNK, 2], F32)
+                growth[c, u] = at(f"growth{c}{u}", GROWTH_AT[2 * c + u], [P, CHUNK, 2], F32)
                 nc.scalar.activation(growth[c, u][:], rate[c, u][:].rearrange("p (s n) -> p n s", s=2), ACT.Exp)
 
         wr_bf = {(1, 1): kept("wr_bf11", [P, 2 * H], BF16)}
@@ -195,13 +206,13 @@ def tile_list_kmer_locus_enrichment_kernel(
 
         def cast_wo(b):
             nc.scalar.copy(
-                wo_bf[:, 512 * b : 512 * (b + 1)].rearrange("p (n t) -> p n t", t=SLOTS),
+                wo_bf[b].rearrange("p (n t) -> p n t", t=SLOTS),
                 wo_raw[:, :, P * b : P * (b + 1)].rearrange("p t n -> p n t"),
             )
 
-        def quantise_wo():
-            nc.vector.quantize_mx(out=wo_codes[:, 0:256].bitcast(FP8X4), scales=wo_scales[:, 0:256], in_=wo_bf[:, 0:1024])
-            nc.vector.quantize_mx(out=wo_codes[:, 256:384].bitcast(FP8X4), scales=wo_scales[:, 256:384], in_=wo_bf[:, 1024:1536])
+        def quantise_wo(part):
+            cols = (slice(0, 256), slice(256, 384))[part]
+            nc.vector.quantize_mx(out=wo_codes[:, cols].bitcast(FP8X4), scales=wo_scales[:, cols], in_=(wo_head, wo_tail)[part][:])
 
         signal = {}
         expo = {}
@@ -232,24 +243,69 @@ def tile_list_kmer_locus_enrichment_kernel(
             )
 
         def correct(c, lo, width, engine):
-            if lo == 0:
-                h_bf[c] = ring.tile([P, CHUNK * SLOTS], BF16, name="h_bf", align_bytes=64)
-            if c in back:
-                taken = back[c][:, SLOTS * lo : SLOTS * (lo + width)].rearrange("p (n u s) -> p n u s", u=2, s=2)
+            j = 2 * c + lo // P
+            h_bf[j] = at(f"h_bf{j}", H_AT[j], [P, P * SLOTS], BF16)
+            if j in back:
+                taken = back[j][:, SLOTS * (lo % P) : SLOTS * (lo % P + width)].rearrange("p (n u s) -> p n u s", u=2, s=2)
             else:
-                taken = back_acc[2 * c + lo // P][:].rearrange("p (u s n) -> p n u s", u=2, s=2)[:, lo % P : lo % P + width]
+                taken = back_acc[j][:].rearrange("p (u s n) -> p n u s", u=2, s=2)[:, lo % P : lo % P + width]
             engine.tensor_tensor(
-                h_bf[c][:, SLOTS * lo : SLOTS * (lo + width)].rearrange("p (n u s) -> p n u s", u=2, s=2),
+                h_bf[j][:].rearrange("p (n u s) -> p n u s", u=2, s=2),
                 signal[c][:, :, lo : lo + width, :].rearrange("p u n s -> p n u s"),
                 taken,
                 ALU.subtract,
             )
 
         def quantise_h(c, lo, width):
+            codes = at(f"h_codes{c}", CODES_AT[c], [P, width], U32)
+            scales = ring.tile([P, width], U8, name="h_scales", align_bytes=64)
+            for half in (1, 0):
+                cols = slice(P * half, P * (half + 1))
+                nc.vector.quantize_mx(out=codes[:, cols].bitcast(FP8X4), scales=scales[:, cols], in_=h_bf[2 * c + half][:])
+            h_mx[c, lo] = (codes, scales)
+
+        def rate_tile(j):
+            acc = bank(f"rate_tile{j}", 4 + j % 2)
+            for a in range(PASSES):
+                for t in range(SLOTS):
+                    product(acc[:, P * t : P * (t + 1)], wr_codes[a, t // 2][:, P * (t % 2) : P * (t % 2 + 1)].bitcast(FP8X4), wr_scales[a][:, P * t : P * (t + 1)],
+                            a, P * j, P * (j + 1), start=(a == 0 and t == 0), stop=(a == PASSES - 1 and t == SLOTS - 1))
+            growth[j] = at(f"growth{j}", GROWTH_AT[j], [P, P, SLOTS], F32)
+            nc.scalar.activation(growth[j][:], acc[:].rearrange("p (t n) -> p n t", t=SLOTS), ACT.Exp)
+
+        def exposure_tile(j):
+            expo[j] = bank(f"expo_tile{j}", j % 2)
+            for a in range(PASSES):
+                for t in range(SLOTS):
+                    first = 256 * t + 128 * a
+                    product(expo[j][:, P * t : P * (t + 1)], we_codes[:, first : first + 128].bitcast(FP8X4), w_scale(0, a, t),
+                            a, P * j, P * (j + 1), start=(a == 0 and t == 0), stop=(a == PASSES - 1 and t == SLOTS - 1))
+
+        piece_signal = {}
+        piece_bf = {}
+
+        def grow_piece(j, lo, width):
+            piece_signal[j, lo] = kept(f"signal{j}{lo}", [P, width, SLOTS], F32)
+            nc.vector.tensor_tensor(
+                piece_signal[j, lo][:],
+                expo[j][:].rearrange("p (t n) -> p n t", t=SLOTS)[:, lo : lo + width],
+                growth[j][:, lo : lo + width],
+                ALU.mult,
+            )
+
+        def correct_piece(j, lo, width, engine):
+            piece_bf[j, lo] = kept(f"h_bf{j}{lo}", [P, width * SLOTS], BF16)
+            if j in back:
+                taken = back[j][:, SLOTS * lo : SLOTS * (lo + width)].rearrange("p (n t) -> p n t", t=SLOTS)
+            else:
+                taken = back_acc[j][:].rearrange("p (t n) -> p n t", t=SLOTS)[:, lo : lo + width]
+            engine.tensor_tensor(piece_bf[j, lo][:].rearrange("p (n t) -> p n t", t=SLOTS), piece_signal[j, lo][:], taken, ALU.subtract)
+
+        def quantise_piece(j, lo, width):
             codes = ring.tile([P, width], U32, name="h_codes", align_bytes=64)
             scales = ring.tile([P, width], U8, name="h_scales", align_bytes=64)
-            nc.vector.quantize_mx(out=codes[:].bitcast(FP8X4), scales=scales[:], in_=h_bf[c][:, SLOTS * lo : SLOTS * (lo + width)])
-            h_mx[c, lo] = (codes, scales)
+            nc.vector.quantize_mx(out=codes[:].bitcast(FP8X4), scales=scales[:], in_=piece_bf[j, lo][:])
+            h_mx[j // 2, P * (j % 2) + lo] = (codes, scales)
 
         def readout(c, lo, width, first_bank, on_vector=False):
             codes, scales = h_mx[c, lo]
@@ -274,11 +330,19 @@ def tile_list_kmer_locus_enrichment_kernel(
                 for b in range(blocks):
                     nc.scalar.activation(staged[:, b, :], sums[b], ACT.Identity, bias=bias[:, b : b + 1])
             first = CHUNK * c + lo
-            nc.sync.dma_start(out=out[:, first : first + width].rearrange("(b p) j -> p b j", p=P), in_=staged[:])
+            if width == CHUNK:
+                for b in range(blocks):
+                    nc.sync.dma_start(out=out[P * b : P * (b + 1), first : first + width], in_=staged[:, b, :])
+            else:
+                nc.sync.dma_start(out=out[:, first : first + width].rearrange("(b p) j -> p b j", p=P), in_=staged[:])
 
-        for j in range(4):
-            background(0, j)
-        for lo, hi in ((0, 256), (256, 512), (512, S)):
+        warm = bank("warm", 7)
+        for i in range(WARMUP):
+            nc.tensor.matmul_mx(
+                out=warm[:], lhsT=wb_raw[:, 0:64].bitcast(FP4X4), lhsT_scale=ws_raw[1][:, 0:32].bitcast(U8),
+                rhs=tw_win[0][:, 0:BANK].bitcast(FP8X4), rhs_scale=ws_raw[1][:, 0:128].bitcast(U8), start=True, stop=True,
+            )
+        for lo, hi in ((0, 256), (256, 512), (512, 768), (768, S)):
             gather_words(1, lo, hi)
         ws[0] = kept("ws0", [P, PASSES * H // 4], I32)
         reorder(nc.vector, ws[0][:], ws_raw[0][:], RUN // 4)
@@ -287,14 +351,26 @@ def tile_list_kmer_locus_enrichment_kernel(
         wr_bf[1, 0] = kept("wr_bf10", [P, 2 * H], BF16)
         cast_wr(0, 1, nc.vector.tensor_copy)
         cast_wr(0, 0, nc.vector.tensor_copy)
-        back[0] = kept("back0", [P, 2 * BANK], F32)
-        for j in range(4):
-            background(1, j)
-            if j < EARLY:
-                keep_background(j)
-        for j in (4, 5):
-            background(0, j)
-            background(1, j)
+        background(0,0)
+        background(0,2)
+        background(1,0)
+        keep_background(0)
+        background(0,4)
+        background(1,2)
+        keep_background(2)
+        background(0,6)
+        background(1,4)
+        keep_background(4)
+        background(1,6)
+        keep_background(6)
+        background(0,1)
+        background(1,1)
+        background(0,3)
+        background(1,3)
+        background(0,5)
+        background(1,5)
+        background(0,7)
+        background(1,7)
         wr_codes = {(a, u): kept(f"wr_codes{a}{u}", [P, 256], U32) for a in range(PASSES) for u in range(2)}
         quantise_wr(0, 1)
         quantise_wr(0, 0)
@@ -319,44 +395,48 @@ def tile_list_kmer_locus_enrichment_kernel(
         for u in range(2):
             rate_pass(0, 1, u)
             rate_pass(1, 1, u)
-        wo_bf = at("wo_bf", GROWTH - 3072 + 64, [P, N * SLOTS], BF16)
-        for b in range(N // P):
+        wo_head = at("wo_head", WO_HEAD, [P, 2 * P * SLOTS], BF16)
+        wo_bf = {0: wo_head[:, 0:512], 1: wo_head[:, 512:1024]}
+        for b in range(2):
             cast_wo(b)
-        correct(0, 0, CHUNK, nc.vector)
+        correct(0, 0, P, nc.gpsimd)
+        correct(0, P, P, nc.vector)
         exposure(1, 0)
-        quantise_h(0, 0, CHUNK)
         exposure(1, 1)
-        for u in range(2):
-            rate_pass(0, 2, u)
-            rate_pass(1, 2, u)
-        quantise_wo()
-        correct(1, 0, P, nc.vector)
+        quantise_h(0, 0, CHUNK)
+        rate_pass(0,2,0)
+        rate_pass(1,2,0)
+        rate_pass(0,2,1)
+        rate_pass(1,2,1)
+        wo_tail = at("wo_tail", WO_TAIL, [P, P * SLOTS], BF16)
+        wo_bf[2] = wo_tail[:]
+        cast_wo(2)
+        quantise_wo(0)
+        correct(1, 0, P, nc.gpsimd)
         correct(1, P, P, nc.vector)
-        readout(0, 0, CHUNK, 2)
         exposure(2, 0)
         exposure(2, 1)
         quantise_h(1, 0, CHUNK)
-        for u in range(2):
-            rate_pass(0, 3, u)
-            rate_pass(1, 3, u)
-        readout(1, 0, CHUNK, 2)
-        correct(2, 0, P, nc.vector)
+        quantise_wo(1)
+        rate_tile(6)
+        rate_tile(7)
+        readout(0, 0, CHUNK, 2)
+        correct(2, 0, P, nc.gpsimd)
         correct(2, P, P, nc.vector)
-        exposure(3, 0, ((0, P),))
+        exposure_tile(6)
+        exposure_tile(7)
+        readout(1, 0, CHUNK, 4)
+        grow_piece(6, 0, P)
         quantise_h(2, 0, CHUNK)
-        exposure(3, 1, ((0, P),))
         readout(2, 0, CHUNK, 2)
-        for j in range(2):
-            background(0, 6 + j)
-            background(1, 6 + j)
-        grow(3, 0, P, P)
-        correct(3, 0, P, nc.vector)
-        grow(3, 1, P, P)
-        quantise_h(3, 0, P)
-        readout(3, 0, P, 4)
-        correct(3, P, 64, nc.vector)
-        correct(3, P + 64, 64, nc.vector)
-        quantise_h(3, P, 64)
-        readout(3, P, 64, 5)
-        quantise_h(3, P + 64, 64)
-        readout(3, P + 64, 64, 0, on_vector=True)
+        grow_piece(7, 0, 64)
+        correct_piece(6, 0, P, nc.vector)
+        grow_piece(7, 64, 64)
+        quantise_piece(6, 0, P)
+        readout(3, 0, P, 6)
+        correct_piece(7, 0, 64, nc.vector)
+        correct_piece(7, 64, 64, nc.vector)
+        quantise_piece(7, 0, 64)
+        readout(3, P, 64, 0, on_vector=True)
+        quantise_piece(7, 64, 64)
+        readout(3, P + 64, 64, 4, on_vector=True)

@@ -26,7 +26,6 @@ CHUNKS = S // CHUNK
 BACK_BANK = (4, 2, 5, 3, 0, 6, 1, 7)
 RATE_BANK = (4, 4, 4, 4)
 EXPO_BANK = (0, 0, 0, 0)
-WARMUP = 4
 
 
 def tile_list_kmer_locus_enrichment_kernel(
@@ -336,12 +335,6 @@ def tile_list_kmer_locus_enrichment_kernel(
             else:
                 nc.sync.dma_start(out=out[:, first : first + width].rearrange("(b p) j -> p b j", p=P), in_=staged[:])
 
-        warm = bank("warm", 7)
-        for i in range(WARMUP):
-            nc.tensor.matmul_mx(
-                out=warm[:], lhsT=wb_raw[:, 0:64].bitcast(FP4X4), lhsT_scale=ws_raw[1][:, 0:32].bitcast(U8),
-                rhs=tw_win[0][:, 0:BANK].bitcast(FP8X4), rhs_scale=ws_raw[1][:, 0:128].bitcast(U8), start=True, stop=True,
-            )
         for lo, hi in ((0, 256), (256, 512), (512, 768), (768, S)):
             gather_words(1, lo, hi)
         ws[0] = kept("ws0", [P, PASSES * H // 4], I32)

@@ -80,7 +80,7 @@ def tile_list_kmer_locus_enrichment_kernel(
         def load_scales(w, scales, queue, quadrants):
             for q in quadrants:
                 queue.dma_start(
-                    out=ws_raw[w][32 * q : 32 * q + 4, :],
+                    out=ws_raw[w][32 * q + 4 * (1 - w) : 32 * q + 4 * (1 - w) + 4, :],
                     in_=scales[:, 4 * q : 4 * q + 4, :].rearrange("a r c -> r a c").bitcast(I32),
                 )
 
@@ -92,9 +92,9 @@ def tile_list_kmer_locus_enrichment_kernel(
 
         load_table(0)
         nc.sync.dma_start(out=wb_raw[:].rearrange("p (a c) -> p a c", a=PASSES), in_=wb_words.rearrange("a p c -> p a c").bitcast(I32))
-        load_scales(1, wb_scales, nc.sync, range(4))
+        load_scales(1, wb_scales, nc.sync, (0, 2, 1, 3))
         load_table(1)
-        load_scales(0, we_scales, nc.sync, (0, 1))
+        load_scales(0, we_scales, nc.sync, (0, 2))
 
         def gather_words(a, lo, hi):
             nc.vector.tensor_copy(
@@ -136,16 +136,16 @@ def tile_list_kmer_locus_enrichment_kernel(
 
         def w_scale(w, a, t):
             first = 64 * t + 32 * a
-            return ws[w][:, first : first + 32].bitcast(U8)
+            return ws[w][4 * (1 - w) :, first : first + 32].bitcast(U8)
 
         nc.vector.tensor_copy(v_rows[:], ts_win.bitcast(U8).indirect(offsets[:]))
-        for q in range(4):
+        for q in (0, 2, 1, 3):
             nc.sync.dma_start(out=v_scales[32 * q : 32 * q + 4, :], in_=v_rows[8 * q : 8 * q + 8, :].bitcast(I32))
         wr_raw = [at("wr_raw0", WR0, [P, 4 * H], F32), at("wr_raw1", WR1, [P, 4 * H], F32)]
         for a in range(PASSES):
             nc.sync.dma_start(out=wr_raw[a][:], in_=wr[512 * a : 512 * (a + 1), :].rearrange("(p i) c -> p (i c)", i=4))
             if a == 0:
-                load_scales(0, we_scales, nc.sync, (2, 3))
+                load_scales(0, we_scales, nc.sync, (1, 3))
         v_codes = [kept("v_codes0", [P, S], U32)]
         ws = {}
         for lo, hi in [[0,1024]]:

@@ -22,10 +22,10 @@ SLOTS = 4
 RUN = 8
 CHUNK = 256
 BANK = 512
-CHUNKS = S // CHUNK
-BACK_BANK = (4, 2, 5, 3, 0, 6, 1, 7)
-RATE_BANK = (4, 4, 4, 4)
-EXPO_BANK = (0, 0, 0, 0)
+BLOCKS = N // P
+LINK = 64
+COPIED = (0, 2, 4, 7)
+WAITING = (1, 3, 5, 6)
 
 
 def tile_list_kmer_locus_enrichment_kernel(
@@ -34,7 +34,6 @@ def tile_list_kmer_locus_enrichment_kernel(
     nc = tc.nc
     with ExitStack() as ctx:
         keep = ctx.enter_context(tc.tile_pool(name="keep", bufs=1))
-        ring = ctx.enter_context(tc.tile_pool(name="ring", bufs=5))
         placed = ctx.enter_context(tc.tile_pool(name="placed", bufs=1))
         psum = ctx.enter_context(tc.psum_pool(name="psum", bufs=1))
 
@@ -50,61 +49,141 @@ def tile_list_kmer_locus_enrichment_kernel(
         offsets = keep.tile([P, S // 16], U16, name="offsets")
         nc.sync.dma_start(offsets[:], offs)
 
-        WB, WO, TAB0, TAB1, GROWTH, TS, LATE = 0, 2048, 8128, 16320, 32768, 49152, 81920
-        BIAS, WE, WES = TAB0 + 64, TAB0 + 128, TAB0 + 4224
-        WRC, BF = TAB1, TAB1 + 2048
-        WR1, VC0, WR0, END = TS, TS + 8192, TS + 12288, TS + 20480
+        SLOT = 8192
+        GROWTH_AT = {(c, u): SLOT * (1 + 2 * c + u) for c in range(4) for u in range(2)}
+        FIRST = ((0, 0), (1, 1), (2, 0), (3, 0))
+        CODES_AT = [GROWTH_AT[FIRST[1]] - 4 * CHUNK + LINK, GROWTH_AT[FIRST[2]] - 4 * CHUNK + LINK, GROWTH_AT[FIRST[3]] - 4 * CHUNK + LINK]
+        WO_AT = [GROWTH_AT[0, 0] + 2048 - LINK, GROWTH_AT[0, 1] + 2048 - LINK, GROWTH_AT[FIRST[1]] + 2048 - LINK]
+        H_AT = {2: WO_AT[2] + 1024 - LINK, 0: 9 * SLOT, 3: 9 * SLOT + 1024, 5: 9 * SLOT + 3072}
+        H_AT[1] = H_AT[2] + 1024 - LINK
+        H_AT[4] = H_AT[3] + 1024 - LINK
 
-        G00 = GROWTH
-        WO_HEAD = G00 + 2048 - 64
-        H2 = WO_HEAD + 2048 - 64
-        H4 = H2 + 1024 - 64
-        WO_TAIL = H4 + 1024 - 64
-        G11 = WO_TAIL + 1024 - 64
-        FREE = LATE
-        H_AT = (H2 + 64, FREE + 8192, H2, FREE + 9216, H4, FREE + 10240)
-        GROWTH_AT = (G00, FREE, FREE + 2048, G11, FREE + 4096, FREE + 6144, FREE + 12288, FREE + 14336)
-        CODES_AT = (GROWTH_AT[2], GROWTH_AT[4], GROWTH_AT[6])
+        ts_win = kept("ts_win", [P, T // 4], I32)
         v_rows = kept("v_rows", [P, S], U8)
-        v_scales = kept("v_scales", [P, PASSES * S // 4], I32)
-        ts_tile = at("ts_tile", TS, [P, (END - TS) // 4], I32)
-        ts_win = ts_tile[:, 0 : T // 4]
+        v_planes = kept("v_planes", [P, PASSES * S // 4], I32)
         ws_raw = [kept("wes_raw", [P, PASSES * H // 4], I32), kept("wbs_raw", [P, PASSES * H // 4], I32)]
-        nc.sync.dma_start(out=ts_tile[0:32, 0 : T // 4], in_=tab_scales.rearrange("a r t -> r a t").bitcast(I32))
+        nc.sync.dma_start(out=ts_win[0:32, :], in_=tab_scales.rearrange("a r t -> r a t").bitcast(I32))
         nc.gpsimd.memset(ws_raw[1][:], 0)
         nc.gpsimd.memset(ws_raw[0][:], 0)
-        nc.vector.memset(ts_tile[32:64, 0 : T // 4], 0)
-        nc.vector.memset(ts_tile[64:128, 0 : T // 4], 0)
-        nc.vector.memset(v_scales[:], 0)
+        nc.vector.memset(ts_win[32:64, :], 0)
+        nc.vector.memset(ts_win[64:128, :], 0)
+        nc.vector.memset(v_planes[:], 0)
+        wb_raw = kept("wb_raw", [P, PASSES * H // 2], I32)
 
-        def load_scales(w, scales, queue, quadrants):
+        first_row = (4, 0)
+
+        def load_scales(w, scales, quadrants):
             for q in quadrants:
-                queue.dma_start(
-                    out=ws_raw[w][32 * q + 4 * (1 - w) : 32 * q + 4 * (1 - w) + 4, :],
+                row = 32 * q + first_row[w]
+                nc.sync.dma_start(
+                    out=ws_raw[w][row : row + 4, :],
                     in_=scales[:, 4 * q : 4 * q + 4, :].rearrange("a r c -> r a c").bitcast(I32),
                 )
 
-        wb_raw = at("wb_raw", WB, [P, PASSES * H // 2], I32)
-        tw_win = [at("tw_win0", TAB0, [P, T], I32), at("tw_win1", TAB1, [P, T], I32)]
+        tw_win = [kept(f"tw_win{a}", [P, T], I32) for a in range(PASSES)]
 
         def load_table(a):
             nc.sync.dma_start(out=tw_win[a][:], in_=tab_words[a].rearrange("p t i -> p (t i)").bitcast(I32))
 
         load_table(0)
         nc.sync.dma_start(out=wb_raw[:].rearrange("p (a c) -> p a c", a=PASSES), in_=wb_words.rearrange("a p c -> p a c").bitcast(I32))
-        load_scales(1, wb_scales, nc.sync, (0, 2, 1, 3))
+        load_scales(1, wb_scales, (0, 2, 1, 3))
         load_table(1)
-        load_scales(0, we_scales, nc.sync, (0, 2))
+        load_scales(0, we_scales, (0, 2))
 
-        def gather_words(a, lo, hi):
+        nc.vector.tensor_copy(v_rows[:], ts_win[:].bitcast(U8).indirect(offsets[:]))
+        for q in (0, 2, 1, 3):
+            nc.sync.dma_start(out=v_planes[32 * q : 32 * q + 4, :], in_=v_rows[8 * q : 8 * q + 8, :].bitcast(I32))
+        wr_raw = [kept("wr_raw0", [P, 4 * H], F32), kept("wr_raw1", [P, 4 * H], F32)]
+
+        def load_wr(a):
+            nc.sync.dma_start(out=wr_raw[a][:], in_=wr[512 * a : 512 * (a + 1), :].rearrange("(p i) c -> p (i c)", i=4))
+
+        load_wr(0)
+        load_scales(0, we_scales, (1, 3))
+        load_wr(1)
+        we_raw = kept("we_raw", [P, PASSES * H], I32)
+        wo_raw = kept("wo_raw", [P, SLOTS, N], F32)
+        bias = kept("bias", [P, BLOCKS], F32)
+        nc.sync.dma_start(out=we_raw[:].rearrange("p (a c) -> p a c", a=PASSES), in_=we_words.rearrange("a p c i -> p a (c i)").bitcast(I32))
+        for t in range(SLOTS):
+            nc.sync.dma_start(out=wo_raw[:, t, :], in_=wo.rearrange("(g t e) n -> t g e n", t=SLOTS, e=RUN)[t])
+        with nc.allow_non_contiguous_dma(reason="one bias value a partition"):
+            nc.sync.dma_start(out=bias[:], in_=bo.rearrange("(b p) -> p b", p=P))
+
+        def reorder(dst, src, run):
             nc.vector.tensor_copy(
-                v_codes[a][:, lo:hi], tw_win[a][:].bitcast(U32).indirect(offsets[:, lo // 16 : hi // 16])
+                dst.rearrange("p (t x e) -> p t x e", t=SLOTS, e=run),
+                src.rearrange("p (x t e) -> p t x e", t=SLOTS, e=run),
             )
 
-        def cast_wr(a, u, engine_copy):
+        wb_codes = kept("wb_codes", [P, PASSES * H // 2], I32)
+        ws = [kept(f"ws{w}", [P, PASSES * H // 4], I32) for w in range(2)]
+        v_codes = [kept(f"v_codes{a}", [P, S], U32) for a in range(PASSES)]
+
+        def gather_words(a, lo, hi):
+            nc.vector.tensor_copy(v_codes[a][:, lo:hi], tw_win[a][:].bitcast(U32).indirect(offsets[:, lo // 16 : hi // 16]))
+
+        gather_words(0, 0, S)
+        reorder(wb_codes[:], wb_raw[:], RUN // 2)
+        reorder(ws[1][:], ws_raw[1][:], RUN // 4)
+        for c in range(4):
+            gather_words(1, CHUNK * c, CHUNK * (c + 1))
+        reorder(ws[0][:], ws_raw[0][:], RUN // 4)
+
+        def product(dst, codes, scales, a, lo, hi, start, stop):
+            plane = v_planes[:, (S * a + lo) // 4 : (S * a + hi) // 4].bitcast(U8)
+            nc.tensor.matmul_mx(
+                out=dst, lhsT=codes, lhsT_scale=scales,
+                rhs=v_codes[a][:, lo:hi].bitcast(FP8X4), rhs_scale=plane,
+                start=start, stop=stop,
+            )
+
+        def w_scale(w, a, t):
+            first = 64 * t + 32 * a
+            return ws[w][first_row[w] :, first : first + 32].bitcast(U8)
+
+        back = {}
+
+        def background(a, j, first):
+            for t in range(SLOTS):
+                col = 128 * t + 64 * a
+                product(back_acc[j][:, P * t : P * (t + 1)], wb_codes[:, col : col + 64].bitcast(FP4X4), w_scale(1, a, t), a, P * j, P * (j + 1),
+                        start=(first and t == 0), stop=(not first and t == SLOTS - 1))
+
+        def keep_background(j):
+            back[j] = kept(f"back{j}", [P, BANK], F32)
+            nc.scalar.copy(
+                back[j][:].rearrange("p (n t) -> p n t", t=SLOTS),
+                back_acc[j][:].rearrange("p (t n) -> p n t", t=SLOTS),
+            )
+
+        warm = bank("warm", 7)
+        for first in range(0, T, BANK):
+            nc.tensor.matmul_mx(
+                out=warm[:], lhsT=wb_raw[:, 0:64].bitcast(FP4X4), lhsT_scale=v_rows[:, 0:P],
+                rhs=tw_win[0][:, first : first + BANK].bitcast(FP8X4), rhs_scale=v_rows[:, 0:BANK], start=True, stop=True,
+            )
+        back_acc = {j: bank(f"back_acc{j}", index) for index, j in enumerate(COPIED + WAITING)}
+        background(0, COPIED[0], True)
+        for j, ahead in zip(COPIED, COPIED[1:] + (None,)):
+            if ahead is not None:
+                background(0, ahead, True)
+            background(1, j, False)
+            keep_background(j)
+        for j in WAITING:
+            background(0, j, True)
+            background(1, j, False)
+
+        wr_bf = {(a, u): kept(f"wr_bf{a}{u}", [P, 2 * H], BF16) for a in range(PASSES) for u in range(2)}
+        wr_codes = {(a, u): kept(f"wr_codes{a}{u}", [P, 256], U32) for a in range(PASSES) for u in range(2)}
+        wr_scales = [kept(f"wr_scales{a}", [P, H], U8) for a in range(PASSES)]
+
+        def cast_wr(a, first, count, engine_copy):
+            u, s = divmod(first, 2)
             engine_copy(
-                wr_bf[a, u][:].rearrange("p (t g e i) -> p t g e i", t=2, e=RUN, i=4),
-                wr_raw[a][:].rearrange("p (i g t e) -> p t g e i", i=4, t=SLOTS, e=RUN)[:, 2 * u : 2 * u + 2],
+                wr_bf[a, u][:, H * s : H * (s + count)].rearrange("p (t g e i) -> p t g e i", t=count, e=RUN, i=4),
+                wr_raw[a][:].rearrange("p (i g t e) -> p t g e i", i=4, t=SLOTS, e=RUN)[:, first : first + count],
             )
 
         def cast_slot(a, t, engine_copy):
@@ -120,316 +199,203 @@ def tile_list_kmer_locus_enrichment_kernel(
                 in_=wr_bf[a, u][:],
             )
 
-        def reorder(engine, dst, src, run):
-            engine.tensor_copy(
-                dst.rearrange("p (t x e) -> p t x e", t=SLOTS, e=run),
-                src.rearrange("p (x t e) -> p t x e", t=SLOTS, e=run),
-            )
-
-        def product(dst, codes, scales, a, lo, hi, start, stop):
-            plane = v_scales[:, (S * a + lo) // 4 : (S * a + hi) // 4].bitcast(U8)
-            nc.tensor.matmul_mx(
-                out=dst, lhsT=codes, lhsT_scale=scales,
-                rhs=v_codes[a][:, lo:hi].bitcast(FP8X4), rhs_scale=plane,
-                start=start, stop=stop,
-            )
-
-        def w_scale(w, a, t):
-            first = 64 * t + 32 * a
-            return ws[w][4 * (1 - w) :, first : first + 32].bitcast(U8)
-
-        nc.vector.tensor_copy(v_rows[:], ts_win.bitcast(U8).indirect(offsets[:]))
-        for q in (0, 2, 1, 3):
-            nc.sync.dma_start(out=v_scales[32 * q : 32 * q + 4, :], in_=v_rows[8 * q : 8 * q + 8, :].bitcast(I32))
-        wr_raw = [at("wr_raw0", WR0, [P, 4 * H], F32), at("wr_raw1", WR1, [P, 4 * H], F32)]
-        for a in range(PASSES):
-            nc.sync.dma_start(out=wr_raw[a][:], in_=wr[512 * a : 512 * (a + 1), :].rearrange("(p i) c -> p (i c)", i=4))
-            if a == 0:
-                load_scales(0, we_scales, nc.sync, (1, 3))
-        v_codes = [kept("v_codes0", [P, S], U32)]
-        ws = {}
-        for lo, hi in [[0,1024]]:
-            gather_words(0, lo, hi)
-        wb_codes = kept("wb_codes", [P, PASSES * H // 2], I32)
-        ws[1] = kept("ws1", [P, PASSES * H // 4], I32)
-        reorder(nc.vector, wb_codes[:], wb_raw[:], RUN // 2)
-        reorder(nc.vector, ws[1][:], ws_raw[1][:], RUN // 4)
-        v_codes.append(kept("v_codes1", [P, S], U32))
-
-        we_raw = at("we_raw", WE, [P, PASSES * H], I32)
-        wo_raw = at("wo_raw", WO, [P, SLOTS, N], F32)
-        bias = at("bias", BIAS, [P, N // P], F32)
-        nc.sync.dma_start(out=we_raw[:].rearrange("p (a c) -> p a c", a=PASSES), in_=we_words.rearrange("a p c i -> p a (c i)").bitcast(I32))
+        for u in (1, 0):
+            cast_wr(0, 2 * u, 2, nc.vector.tensor_copy)
+        for u in (1, 0):
+            quantise_wr(0, u)
         for t in range(SLOTS):
-            nc.sync.dma_start(out=wo_raw[:, t, :], in_=wo.rearrange("(g t e) n -> t g e n", t=SLOTS, e=RUN)[t])
-        with nc.allow_non_contiguous_dma(reason="one bias value a partition"):
-            nc.sync.dma_start(out=bias[:], in_=bo.rearrange("(b p) -> p b", p=P))
-
-        back_acc = {}
-        back = {}
-
-        def background(a, j):
-            if a == 0:
-                back_acc[j] = bank(f"back_acc{j}", BACK_BANK[j])
-            for t in range(SLOTS):
-                first = 128 * t + 64 * a
-                product(back_acc[j][:, P * t : P * (t + 1)], wb_codes[:, first : first + 64].bitcast(FP4X4), w_scale(1, a, t), a, P * j, P * (j + 1),
-                        start=(a == 0 and t == 0), stop=(a == PASSES - 1 and t == SLOTS - 1))
-
-        def keep_background(j):
-            back[j] = kept(f"back{j}", [P, BANK], F32)
-            nc.scalar.copy(
-                back[j][:].rearrange("p (n t) -> p n t", t=SLOTS),
-                back_acc[j][:].rearrange("p (t n) -> p n t", t=SLOTS),
-            )
-
-        rate = {}
-        growth = {}
-
-        def rate_pass(a, c, u):
-            if a == 0:
-                rate[c, u] = bank(f"rate{c}{u}", RATE_BANK[c] + u)
-            lo = CHUNK * c
-            for s in range(2):
-                cols = slice(P * (2 * u + s), P * (2 * u + s + 1))
-                product(rate[c, u][:, CHUNK * s : CHUNK * (s + 1)], wr_codes[a, u][:, P * s : P * (s + 1)].bitcast(FP8X4), wr_scales[a][:, cols], a, lo, lo + CHUNK,
-                        start=(a == 0 and s == 0), stop=(a == PASSES - 1 and s == 1))
-            if a == PASSES - 1:
-                growth[c, u] = at(f"growth{c}{u}", GROWTH_AT[2 * c + u], [P, CHUNK, 2], F32)
-                nc.scalar.activation(growth[c, u][:], rate[c, u][:].rearrange("p (s n) -> p n s", s=2), ACT.Exp)
-
-        wr_bf = {(1, 1): kept("wr_bf11", [P, 2 * H], BF16)}
-        wr_scales = [kept(f"wr_scales{a}", [P, H], U8) for a in range(PASSES)]
-        wo_codes = kept("wo_codes", [P, N], U32)
-        wo_scales = kept("wo_scales", [P, N], U8)
-
-        def cast_wo(b):
-            nc.scalar.copy(
-                wo_bf[b].rearrange("p (n t) -> p n t", t=SLOTS),
-                wo_raw[:, :, P * b : P * (b + 1)].rearrange("p t n -> p n t"),
-            )
-
-        def quantise_wo(part):
-            cols = (slice(0, 256), slice(256, 384))[part]
-            nc.vector.quantize_mx(out=wo_codes[:, cols].bitcast(FP8X4), scales=wo_scales[:, cols], in_=(wo_head, wo_tail)[part][:])
-
-        signal = {}
-        expo = {}
-        h_bf = {}
-        h_mx = {}
-
-        def exposure(c, u, pieces=((0, CHUNK),)):
-            lo = CHUNK * c
-            if u == 0:
-                signal[c] = ring.tile([P, 2, CHUNK, 2], F32, name="signal", align_bytes=64)
-            acc = bank(f"expo{c}{u}", EXPO_BANK[c] + u)
-            for s in range(2):
-                t = 2 * u + s
-                for a in range(PASSES):
-                    first = 256 * t + 128 * a
-                    product(acc[:, CHUNK * s : CHUNK * (s + 1)], we_codes[:, first : first + 128].bitcast(FP8X4), w_scale(0, a, t), a, lo, lo + CHUNK,
-                            start=(a == 0), stop=(a == PASSES - 1))
-            expo[c, u] = acc
-            for first, width in pieces:
-                grow(c, u, first, width)
-
-        def grow(c, u, first, width):
-            nc.vector.tensor_tensor(
-                signal[c][:, u, first : first + width, :],
-                expo[c, u][:].rearrange("p (s n) -> p n s", s=2)[:, first : first + width],
-                growth[c, u][:, first : first + width],
-                ALU.mult,
-            )
-
-        def correct(c, lo, width, engine):
-            j = 2 * c + lo // P
-            h_bf[j] = at(f"h_bf{j}", H_AT[j], [P, P * SLOTS], BF16)
-            if j in back:
-                taken = back[j][:, SLOTS * (lo % P) : SLOTS * (lo % P + width)].rearrange("p (n u s) -> p n u s", u=2, s=2)
-            else:
-                taken = back_acc[j][:].rearrange("p (u s n) -> p n u s", u=2, s=2)[:, lo % P : lo % P + width]
-            engine.tensor_tensor(
-                h_bf[j][:].rearrange("p (n u s) -> p n u s", u=2, s=2),
-                signal[c][:, :, lo : lo + width, :].rearrange("p u n s -> p n u s"),
-                taken,
-                ALU.subtract,
-            )
-
-        def quantise_h(c, lo, width):
-            codes = at(f"h_codes{c}", CODES_AT[c], [P, width], U32)
-            scales = ring.tile([P, width], U8, name="h_scales", align_bytes=64)
-            for half in (1, 0):
-                cols = slice(P * half, P * (half + 1))
-                nc.vector.quantize_mx(out=codes[:, cols].bitcast(FP8X4), scales=scales[:, cols], in_=h_bf[2 * c + half][:])
-            h_mx[c, lo] = (codes, scales)
-
-        def rate_tile(j):
-            acc = bank(f"rate_tile{j}", 4 + j % 2)
-            for a in range(PASSES):
-                for t in range(SLOTS):
-                    product(acc[:, P * t : P * (t + 1)], wr_codes[a, t // 2][:, P * (t % 2) : P * (t % 2 + 1)].bitcast(FP8X4), wr_scales[a][:, P * t : P * (t + 1)],
-                            a, P * j, P * (j + 1), start=(a == 0 and t == 0), stop=(a == PASSES - 1 and t == SLOTS - 1))
-            growth[j] = at(f"growth{j}", GROWTH_AT[j], [P, P, SLOTS], F32)
-            nc.scalar.activation(growth[j][:], acc[:].rearrange("p (t n) -> p n t", t=SLOTS), ACT.Exp)
-
-        def exposure_tile(j):
-            expo[j] = bank(f"expo_tile{j}", j % 2)
-            for a in range(PASSES):
-                for t in range(SLOTS):
-                    first = 256 * t + 128 * a
-                    product(expo[j][:, P * t : P * (t + 1)], we_codes[:, first : first + 128].bitcast(FP8X4), w_scale(0, a, t),
-                            a, P * j, P * (j + 1), start=(a == 0 and t == 0), stop=(a == PASSES - 1 and t == SLOTS - 1))
-
-        piece_signal = {}
-        piece_bf = {}
-
-        def grow_piece(j, lo, width):
-            piece_signal[j, lo] = kept(f"signal{j}{lo}", [P, width, SLOTS], F32)
-            nc.vector.tensor_tensor(
-                piece_signal[j, lo][:],
-                expo[j][:].rearrange("p (t n) -> p n t", t=SLOTS)[:, lo : lo + width],
-                growth[j][:, lo : lo + width],
-                ALU.mult,
-            )
-
-        def correct_piece(j, lo, width, engine):
-            piece_bf[j, lo] = kept(f"h_bf{j}{lo}", [P, width * SLOTS], BF16)
-            if j in back:
-                taken = back[j][:, SLOTS * lo : SLOTS * (lo + width)].rearrange("p (n t) -> p n t", t=SLOTS)
-            else:
-                taken = back_acc[j][:].rearrange("p (t n) -> p n t", t=SLOTS)[:, lo : lo + width]
-            engine.tensor_tensor(piece_bf[j, lo][:].rearrange("p (n t) -> p n t", t=SLOTS), piece_signal[j, lo][:], taken, ALU.subtract)
-
-        def quantise_piece(j, lo, width):
-            codes = ring.tile([P, width], U32, name="h_codes", align_bytes=64)
-            scales = ring.tile([P, width], U8, name="h_scales", align_bytes=64)
-            nc.vector.quantize_mx(out=codes[:].bitcast(FP8X4), scales=scales[:], in_=piece_bf[j, lo][:])
-            h_mx[j // 2, P * (j % 2) + lo] = (codes, scales)
-
-        def readout(c, lo, width, first_bank, on_vector=False):
-            codes, scales = h_mx[c, lo]
-            blocks = N // P
-            staged = ring.tile([P, blocks, width], F32, name="staged", align_bytes=64)
-            per_bank = min(blocks, BANK // width)
-            accs = [bank(f"sum{c}{lo}{first}", first_bank + first // per_bank) for first in range(0, blocks, per_bank)]
-            sums = [accs[b // per_bank][:, width * (b % per_bank) : width * (b % per_bank + 1)] for b in range(blocks)]
-            for b in range(blocks):
-                nc.tensor.matmul_mx(
-                    out=sums[b], lhsT=wo_codes[:, P * b : P * (b + 1)].bitcast(FP8X4), lhsT_scale=wo_scales[:, P * b : P * (b + 1)],
-                    rhs=codes[:].bitcast(FP8X4), rhs_scale=scales[:], start=True, stop=True,
-                )
-            if on_vector:
-                nc.vector.tensor_tensor(
-                    staged[:],
-                    accs[0][:, 0 : blocks * width].rearrange("p (b j) -> p b j", b=blocks),
-                    bias[:].unsqueeze(2).to_broadcast([P, blocks, width]),
-                    ALU.add,
-                )
-            else:
-                for b in range(blocks):
-                    nc.scalar.activation(staged[:, b, :], sums[b], ACT.Identity, bias=bias[:, b : b + 1])
-            first = CHUNK * c + lo
-            if width == CHUNK:
-                for b in range(blocks):
-                    nc.sync.dma_start(out=out[P * b : P * (b + 1), first : first + width], in_=staged[:, b, :])
-            else:
-                nc.sync.dma_start(out=out[:, first : first + width].rearrange("(b p) j -> p b j", p=P), in_=staged[:])
-
-        for lo, hi in ((0, 256), (256, 512), (512, 768), (768, S)):
-            gather_words(1, lo, hi)
-        ws[0] = kept("ws0", [P, PASSES * H // 4], I32)
-        reorder(nc.vector, ws[0][:], ws_raw[0][:], RUN // 4)
-        wr_bf[0, 0] = kept("wr_bf00", [P, 2 * H], BF16)
-        wr_bf[0, 1] = kept("wr_bf01", [P, 2 * H], BF16)
-        wr_bf[1, 0] = kept("wr_bf10", [P, 2 * H], BF16)
-        cast_wr(0, 1, nc.vector.tensor_copy)
-        cast_wr(0, 0, nc.vector.tensor_copy)
-        background(0,0)
-        background(0,2)
-        background(1,0)
-        keep_background(0)
-        background(0,4)
-        background(1,2)
-        keep_background(2)
-        background(0,6)
-        background(1,4)
-        keep_background(4)
-        background(1,6)
-        keep_background(6)
-        background(0,1)
-        background(1,1)
-        background(0,3)
-        background(1,3)
-        background(0,5)
-        background(1,5)
-        background(0,7)
-        background(1,7)
-        wr_codes = {(a, u): kept(f"wr_codes{a}{u}", [P, 256], U32) for a in range(PASSES) for u in range(2)}
-        quantise_wr(0, 1)
-        quantise_wr(0, 0)
-        cast_slot(1, 0, nc.vector.tensor_copy)
-        cast_slot(1, 1, nc.scalar.copy)
-        cast_slot(1, 2, nc.vector.tensor_copy)
-        cast_slot(1, 3, nc.scalar.copy)
+            cast_slot(1, t, nc.scalar.copy if t % 2 else nc.vector.tensor_copy)
         for u in range(2):
-            rate_pass(0, 0, u)
-        quantise_wr(1, 0)
-        quantise_wr(1, 1)
+            quantise_wr(1, u)
         we_codes = kept("we_codes", [P, PASSES * H], I32)
         for u in range(2):
             nc.vector.tensor_copy(
                 we_codes[:, H * u : H * (u + 1)].rearrange("p (t x e) -> p t x e", t=2, e=RUN),
                 we_raw[:].rearrange("p (x t e) -> p t x e", t=SLOTS, e=RUN)[:, 2 * u : 2 * u + 2],
             )
-        for u in range(2):
-            rate_pass(1, 0, u)
-        for u in range(2):
-            exposure(0, u)
-        for u in range(2):
-            rate_pass(0, 1, u)
-            rate_pass(1, 1, u)
-        wo_head = at("wo_head", WO_HEAD, [P, 2 * P * SLOTS], BF16)
-        wo_bf = {0: wo_head[:, 0:512], 1: wo_head[:, 512:1024]}
-        for b in range(2):
-            cast_wo(b)
-        correct(0, 0, P, nc.gpsimd)
-        correct(0, P, P, nc.vector)
-        exposure(1, 0)
+
+        RATE_BANK = {(0, 0): 0, (0, 1): 1, (1, 1): 2, (1, 0): 1, (2, 0): 0, (2, 1): 1, 6: 0, 7: 1}
+        EXPO_BANK = {(0, 0): 3, (0, 1): 0, (1, 1): 2, (1, 0): 3, (2, 0): 2, (2, 1): 3, 6: 2, 7: 3}
+
+        rate = {}
+        growth = {}
+        expo = {}
+        signal = {}
+        h_bf = {}
+        h_mx = {}
+
+        def rate_pass(a, c, u):
+            if a == 0:
+                rate[c, u] = bank(f"rate{c}{u}", RATE_BANK[c, u])
+            lo = CHUNK * c
+            for s in range(2):
+                cols = slice(P * (2 * u + s), P * (2 * u + s + 1))
+                product(rate[c, u][:, CHUNK * s : CHUNK * (s + 1)], wr_codes[a, u][:, P * s : P * (s + 1)].bitcast(FP8X4), wr_scales[a][:, cols], a, lo, lo + CHUNK,
+                        start=(a == 0 and s == 0), stop=(a == PASSES - 1 and s == 1))
+            if a == PASSES - 1:
+                growth[c, u] = at(f"growth{c}{u}", GROWTH_AT[c, u], [P, CHUNK, 2], F32)
+                nc.scalar.activation(growth[c, u][:], rate[c, u][:].rearrange("p (s n) -> p n s", s=2), ACT.Exp)
+
+        def exposure(c, u):
+            lo = CHUNK * c
+            if c not in signal:
+                signal[c] = kept(f"signal{c}", [P, 2, CHUNK, 2], F32)
+            acc = bank(f"expo{c}{u}", EXPO_BANK[c, u])
+            for s in range(2):
+                t = 2 * u + s
+                for a in range(PASSES):
+                    first = 256 * t + 128 * a
+                    product(acc[:, CHUNK * s : CHUNK * (s + 1)], we_codes[:, first : first + 128].bitcast(FP8X4), w_scale(0, a, t), a, lo, lo + CHUNK,
+                            start=(a == 0), stop=(a == PASSES - 1))
+            nc.vector.tensor_tensor(signal[c][:, u], acc[:].rearrange("p (s n) -> p n s", s=2), growth[c, u][:], ALU.mult)
+
+        def correct(c):
+            for half, engine in ((0, nc.gpsimd), (1, nc.vector)):
+                j = 2 * c + half
+                h_bf[j] = at(f"h_bf{j}", H_AT[j], [P, P * SLOTS], BF16)
+                if j in back:
+                    taken = back[j][:].rearrange("p (n u s) -> p n u s", u=2, s=2)
+                else:
+                    taken = back_acc[j][:].rearrange("p (u s n) -> p n u s", u=2, s=2)
+                engine.tensor_tensor(
+                    h_bf[j][:].rearrange("p (n u s) -> p n u s", u=2, s=2),
+                    signal[c][:, :, P * half : P * (half + 1), :].rearrange("p u n s -> p n u s"),
+                    taken,
+                    ALU.subtract,
+                )
+
+        def quantise_h(c):
+            codes = at(f"h_codes{c}", CODES_AT[c], [P, CHUNK], U32)
+            scales = kept(f"h_scales{c}", [P, CHUNK], U8)
+            for half in (0, 1):
+                cols = slice(P * half, P * (half + 1))
+                nc.vector.quantize_mx(out=codes[:, cols].bitcast(FP8X4), scales=scales[:, cols], in_=h_bf[2 * c + half][:])
+            h_mx[CHUNK * c] = (codes, scales)
+
+        wo_scales = kept("wo_scales", [P, N], U8)
+        wo_codes = {}
+
+        wo_bf = {}
+
+        def cast_wo(b):
+            wo_bf[b] = at(f"wo_bf{b}", WO_AT[b], [P, P, SLOTS], BF16)
+            nc.scalar.copy(wo_bf[b][:], wo_raw[:, :, P * b : P * (b + 1)].rearrange("p t n -> p n t"))
+
+        def quantise_wo(b):
+            wo_codes[b] = at(f"wo_codes{b}", GROWTH_AT[FIRST[1]] + LINK + 4 * P * b, [P, P], U32)
+            nc.vector.quantize_mx(out=wo_codes[b][:].bitcast(FP8X4), scales=wo_scales[:, P * b : P * (b + 1)], in_=wo_bf[b][:].rearrange("p n t -> p (n t)"))
+
+        def rate_tile(j):
+            acc = bank(f"rate_tile{j}", RATE_BANK[j])
+            for a in range(PASSES):
+                for t in range(SLOTS):
+                    product(acc[:, P * t : P * (t + 1)], wr_codes[a, t // 2][:, P * (t % 2) : P * (t % 2 + 1)].bitcast(FP8X4), wr_scales[a][:, P * t : P * (t + 1)],
+                            a, P * j, P * (j + 1), start=(a == 0 and t == 0), stop=(a == PASSES - 1 and t == SLOTS - 1))
+            growth[j] = at(f"growth{j}", GROWTH_AT[3, j % 2], [P, P, SLOTS], F32)
+            nc.scalar.activation(growth[j][:], acc[:].rearrange("p (t n) -> p n t", t=SLOTS), ACT.Exp)
+
+        def exposure_tile(j):
+            expo[j] = bank(f"expo_tile{j}", EXPO_BANK[j])
+            for a in range(PASSES):
+                for t in range(SLOTS):
+                    first = 256 * t + 128 * a
+                    product(expo[j][:, P * t : P * (t + 1)], we_codes[:, first : first + 128].bitcast(FP8X4), w_scale(0, a, t),
+                            a, P * j, P * (j + 1), start=(a == 0 and t == 0), stop=(a == PASSES - 1 and t == SLOTS - 1))
+
+        def grow_piece(j, lo, width):
+            signal[j, lo] = kept(f"signal{j}_{lo}", [P, width, SLOTS], F32)
+            nc.vector.tensor_tensor(
+                signal[j, lo][:],
+                expo[j][:].rearrange("p (t n) -> p n t", t=SLOTS)[:, lo : lo + width],
+                growth[j][:, lo : lo + width],
+                ALU.mult,
+            )
+
+        def correct_piece(j, lo, width):
+            h_bf[j, lo] = kept(f"h_bf{j}_{lo}", [P, width * SLOTS], BF16)
+            if j in back:
+                taken = back[j][:, SLOTS * lo : SLOTS * (lo + width)].rearrange("p (n t) -> p n t", t=SLOTS)
+            else:
+                taken = back_acc[j][:].rearrange("p (t n) -> p n t", t=SLOTS)[:, lo : lo + width]
+            nc.vector.tensor_tensor(h_bf[j, lo][:].rearrange("p (n t) -> p n t", t=SLOTS), signal[j, lo][:], taken, ALU.subtract)
+
+        def quantise_piece(j, lo, width):
+            codes = kept(f"h_codes{j}_{lo}", [P, width], U32)
+            scales = kept(f"h_scales{j}_{lo}", [P, width], U8)
+            nc.vector.quantize_mx(out=codes[:].bitcast(FP8X4), scales=scales[:], in_=h_bf[j, lo][:])
+            h_mx[P * j + lo] = (codes, scales)
+
+        def readout(first, width, banks, on_vector=False):
+            codes, scales = h_mx[first]
+            staged = kept(f"staged{first}", [P, BLOCKS, width], F32)
+            per_bank = min(BLOCKS, BANK // width)
+            accs = [bank(f"sum{first}_{index}", index) for index in banks]
+            sums = [accs[b // per_bank][:, width * (b % per_bank) : width * (b % per_bank + 1)] for b in range(BLOCKS)]
+            for b in range(BLOCKS):
+                nc.tensor.matmul_mx(
+                    out=sums[b], lhsT=wo_codes[b][:].bitcast(FP8X4), lhsT_scale=wo_scales[:, P * b : P * (b + 1)],
+                    rhs=codes[:].bitcast(FP8X4), rhs_scale=scales[:], start=True, stop=True,
+                )
+            if on_vector:
+                nc.vector.tensor_tensor(
+                    staged[:],
+                    accs[0][:, 0 : BLOCKS * width].rearrange("p (b j) -> p b j", b=BLOCKS),
+                    bias[:].unsqueeze(2).to_broadcast([P, BLOCKS, width]),
+                    ALU.add,
+                )
+            else:
+                for b in range(BLOCKS):
+                    nc.scalar.activation(staged[:, b, :], sums[b], ACT.Identity, bias=bias[:, b : b + 1])
+            if width == CHUNK:
+                for b in range(BLOCKS):
+                    nc.sync.dma_start(out=out[P * b : P * (b + 1), first : first + width], in_=staged[:, b, :])
+            else:
+                nc.sync.dma_start(out=out[:, first : first + width].rearrange("(b p) j -> p b j", p=P), in_=staged[:])
+
+        rate_pass(0, 0, 0)
+        rate_pass(0, 0, 1)
+        rate_pass(0, 1, 1)
+        rate_pass(1, 0, 0)
+        rate_pass(1, 0, 1)
+        exposure(0, 0)
+        rate_pass(1, 1, 1)
+        exposure(0, 1)
+        rate_pass(0, 1, 0)
+        rate_pass(1, 1, 0)
+        cast_wo(0)
+        cast_wo(1)
+        correct(0)
         exposure(1, 1)
-        quantise_h(0, 0, CHUNK)
-        rate_pass(0,2,0)
-        rate_pass(1,2,0)
-        rate_pass(0,2,1)
-        rate_pass(1,2,1)
-        wo_tail = at("wo_tail", WO_TAIL, [P, P * SLOTS], BF16)
-        wo_bf[2] = wo_tail[:]
+        exposure(1, 0)
         cast_wo(2)
-        quantise_wo(0)
-        correct(1, 0, P, nc.gpsimd)
-        correct(1, P, P, nc.vector)
+        quantise_h(0)
+        for b in range(BLOCKS):
+            quantise_wo(b)
+        for u in range(2):
+            rate_pass(0, 2, u)
+            rate_pass(1, 2, u)
+        correct(1)
         exposure(2, 0)
         exposure(2, 1)
-        quantise_h(1, 0, CHUNK)
-        quantise_wo(1)
+        quantise_h(1)
         rate_tile(6)
-        rate_tile(7)
-        readout(0, 0, CHUNK, 2)
-        correct(2, 0, P, nc.gpsimd)
-        correct(2, P, P, nc.vector)
+        readout(0, CHUNK, (4, 5))
+        correct(2)
         exposure_tile(6)
+        rate_tile(7)
         exposure_tile(7)
-        readout(1, 0, CHUNK, 4)
         grow_piece(6, 0, P)
-        quantise_h(2, 0, CHUNK)
-        readout(2, 0, CHUNK, 2)
+        readout(CHUNK, CHUNK, (4, 6))
+        correct_piece(6, 0, P)
+        quantise_h(2)
+        readout(2 * CHUNK, CHUNK, (5, 0))
         grow_piece(7, 0, 64)
-        correct_piece(6, 0, P, nc.vector)
-        grow_piece(7, 64, 64)
         quantise_piece(6, 0, P)
-        readout(3, 0, P, 6)
-        correct_piece(7, 0, 64, nc.vector)
-        correct_piece(7, 64, 64, nc.vector)
+        grow_piece(7, 64, 64)
+        readout(6 * P, P, (1,))
+        correct_piece(7, 0, 64)
+        correct_piece(7, 64, 64)
         quantise_piece(7, 0, 64)
-        readout(3, P, 64, 0, on_vector=True)
+        readout(7 * P, 64, (2,), on_vector=True)
         quantise_piece(7, 64, 64)
-        readout(3, P + 64, 64, 4, on_vector=True)
+        readout(7 * P + 64, 64, (3,), on_vector=True)

@@ -17,15 +17,39 @@ ALU = mybir.AluOpType
 ACT = mybir.ActivationFunctionType
 
 P = 128
-PASSES = 2
+PASSES = K // 512
 SLOTS = 4
 RUN = 8
-CHUNK = 256
+CHUNK = 2 * P
+CHUNKS = S // CHUNK
 BANK = 512
 BLOCKS = N // P
-LINK = 64
+PIECE = 64
+WARM_UPS = 5
+EXPO, BACK = 0, 1
+PLANE_START = {EXPO: 4, BACK: 0}
+QUADRANTS = (0, 2, 1, 3)
 COPIED = (0, 2, 4, 7)
 WAITING = (1, 3, 5, 6)
+
+LINK = 64
+ROOM = 8192
+GROWTH_BYTES = 4 * BANK
+BF_BYTES = 2 * BANK
+GROWTH_AT = {(c, u): ROOM * (1 + 2 * c + u) for c in range(CHUNKS) for u in range(2)}
+NEXT_GROWTH = (GROWTH_AT[1, 1], GROWTH_AT[2, 0], GROWTH_AT[3, 0])
+H_CODES_AT = [first - 4 * CHUNK + LINK for first in NEXT_GROWTH]
+WO_CODES_AT = [NEXT_GROWTH[0] + LINK + 4 * P * b for b in range(BLOCKS)]
+WO_BF_AT = (GROWTH_AT[0, 0] + GROWTH_BYTES - LINK, GROWTH_AT[0, 1] + GROWTH_BYTES - LINK, GROWTH_AT[0, 1] - BF_BYTES + LINK)
+FREE_AT = ROOM * (1 + 2 * CHUNKS)
+H_BF_AT = {
+    0: FREE_AT,
+    1: WO_BF_AT[2] - 2 * (BF_BYTES - LINK),
+    2: WO_BF_AT[2] - (BF_BYTES - LINK),
+    3: FREE_AT + BF_BYTES,
+    4: FREE_AT + 2 * BF_BYTES - LINK,
+    5: FREE_AT + 3 * BF_BYTES,
+}
 
 
 def tile_list_kmer_locus_enrichment_kernel(
@@ -49,63 +73,58 @@ def tile_list_kmer_locus_enrichment_kernel(
         offsets = keep.tile([P, S // 16], U16, name="offsets")
         nc.sync.dma_start(offsets[:], offs)
 
-        SLOT = 8192
-        GROWTH_AT = {(c, u): SLOT * (1 + 2 * c + u) for c in range(4) for u in range(2)}
-        FIRST = ((0, 0), (1, 1), (2, 0), (3, 0))
-        CODES_AT = [GROWTH_AT[FIRST[1]] - 4 * CHUNK + LINK, GROWTH_AT[FIRST[2]] - 4 * CHUNK + LINK, GROWTH_AT[FIRST[3]] - 4 * CHUNK + LINK]
-        WO_AT = [GROWTH_AT[0, 0] + 2048 - LINK, GROWTH_AT[0, 1] + 2048 - LINK, GROWTH_AT[FIRST[1]] + 2048 - LINK]
-        H_AT = {2: WO_AT[2] + 1024 - LINK, 0: 9 * SLOT, 3: 9 * SLOT + 1024, 5: 9 * SLOT + 3072}
-        H_AT[1] = H_AT[2] + 1024 - LINK
-        H_AT[4] = H_AT[3] + 1024 - LINK
-
-        ts_win = kept("ts_win", [P, T // 4], I32)
+        scale_window = kept("scale_window", [P, T // 4], I32)
         v_rows = kept("v_rows", [P, S], U8)
         v_planes = kept("v_planes", [P, PASSES * S // 4], I32)
-        ws_raw = [kept("wes_raw", [P, PASSES * H // 4], I32), kept("wbs_raw", [P, PASSES * H // 4], I32)]
-        nc.sync.dma_start(out=ts_win[0:32, :], in_=tab_scales.rearrange("a r t -> r a t").bitcast(I32))
-        nc.gpsimd.memset(ws_raw[1][:], 0)
-        nc.gpsimd.memset(ws_raw[0][:], 0)
-        nc.vector.memset(ts_win[32:64, :], 0)
-        nc.vector.memset(ts_win[64:128, :], 0)
+        w_rows = {w: kept(f"w_rows{w}", [P, PASSES * H // 4], I32) for w in (EXPO, BACK)}
+        nc.sync.dma_start(out=scale_window[0:32, :], in_=tab_scales.rearrange("a r t -> r a t").bitcast(I32))
+        nc.gpsimd.memset(w_rows[BACK][:], 0)
+        nc.gpsimd.memset(w_rows[EXPO][:], 0)
+        nc.vector.memset(scale_window[32:64, :], 0)
+        nc.vector.memset(scale_window[64:128, :], 0)
         nc.vector.memset(v_planes[:], 0)
         wb_raw = kept("wb_raw", [P, PASSES * H // 2], I32)
 
-        first_row = (4, 0)
-
         def load_scales(w, scales, quadrants):
             for q in quadrants:
-                row = 32 * q + first_row[w]
+                row = 32 * q + PLANE_START[w]
                 nc.sync.dma_start(
-                    out=ws_raw[w][row : row + 4, :],
+                    out=w_rows[w][row : row + 4, :],
                     in_=scales[:, 4 * q : 4 * q + 4, :].rearrange("a r c -> r a c").bitcast(I32),
                 )
 
-        tw_win = [kept(f"tw_win{a}", [P, T], I32) for a in range(PASSES)]
+        word_window = [kept(f"word_window{a}", [P, T], I32) for a in range(PASSES)]
 
         def load_table(a):
-            nc.sync.dma_start(out=tw_win[a][:], in_=tab_words[a].rearrange("p t i -> p (t i)").bitcast(I32))
+            nc.sync.dma_start(out=word_window[a][:], in_=tab_words[a].rearrange("p t i -> p (t i)").bitcast(I32))
 
         load_table(0)
-        nc.sync.dma_start(out=wb_raw[:].rearrange("p (a c) -> p a c", a=PASSES), in_=wb_words.rearrange("a p c -> p a c").bitcast(I32))
-        load_scales(1, wb_scales, (0, 2, 1, 3))
+        nc.sync.dma_start(
+            out=wb_raw[:].rearrange("p (a c) -> p a c", a=PASSES), in_=wb_words.rearrange("a p c -> p a c").bitcast(I32)
+        )
+        load_scales(BACK, wb_scales, QUADRANTS)
         load_table(1)
-        load_scales(0, we_scales, (0, 2))
+        load_scales(EXPO, we_scales, QUADRANTS[:2])
 
-        nc.vector.tensor_copy(v_rows[:], ts_win[:].bitcast(U8).indirect(offsets[:]))
-        for q in (0, 2, 1, 3):
+        nc.vector.tensor_copy(v_rows[:], scale_window[:].bitcast(U8).indirect(offsets[:]))
+        for q in QUADRANTS:
             nc.sync.dma_start(out=v_planes[32 * q : 32 * q + 4, :], in_=v_rows[8 * q : 8 * q + 8, :].bitcast(I32))
-        wr_raw = [kept("wr_raw0", [P, 4 * H], F32), kept("wr_raw1", [P, 4 * H], F32)]
+
+        wr_raw = [kept(f"wr_raw{a}", [P, 4 * H], F32) for a in range(PASSES)]
 
         def load_wr(a):
             nc.sync.dma_start(out=wr_raw[a][:], in_=wr[512 * a : 512 * (a + 1), :].rearrange("(p i) c -> p (i c)", i=4))
 
         load_wr(0)
-        load_scales(0, we_scales, (1, 3))
+        load_scales(EXPO, we_scales, QUADRANTS[2:])
         load_wr(1)
         we_raw = kept("we_raw", [P, PASSES * H], I32)
         wo_raw = kept("wo_raw", [P, SLOTS, N], F32)
         bias = kept("bias", [P, BLOCKS], F32)
-        nc.sync.dma_start(out=we_raw[:].rearrange("p (a c) -> p a c", a=PASSES), in_=we_words.rearrange("a p c i -> p a (c i)").bitcast(I32))
+        nc.sync.dma_start(
+            out=we_raw[:].rearrange("p (a c) -> p a c", a=PASSES),
+            in_=we_words.rearrange("a p c i -> p a (c i)").bitcast(I32),
+        )
         for t in range(SLOTS):
             nc.sync.dma_start(out=wo_raw[:, t, :], in_=wo.rearrange("(g t e) n -> t g e n", t=SLOTS, e=RUN)[t])
         with nc.allow_non_contiguous_dma(reason="one bias value a partition"):
@@ -118,93 +137,117 @@ def tile_list_kmer_locus_enrichment_kernel(
             )
 
         wb_codes = kept("wb_codes", [P, PASSES * H // 2], I32)
-        ws = [kept(f"ws{w}", [P, PASSES * H // 4], I32) for w in range(2)]
+        w_planes = {w: kept(f"w_planes{w}", [P, PASSES * H // 4], I32) for w in (EXPO, BACK)}
         v_codes = [kept(f"v_codes{a}", [P, S], U32) for a in range(PASSES)]
 
         def gather_words(a, lo, hi):
-            nc.vector.tensor_copy(v_codes[a][:, lo:hi], tw_win[a][:].bitcast(U32).indirect(offsets[:, lo // 16 : hi // 16]))
+            nc.vector.tensor_copy(
+                v_codes[a][:, lo:hi], word_window[a][:].bitcast(U32).indirect(offsets[:, lo // 16 : hi // 16])
+            )
 
         gather_words(0, 0, S)
         reorder(wb_codes[:], wb_raw[:], RUN // 2)
-        reorder(ws[1][:], ws_raw[1][:], RUN // 4)
-        for c in range(4):
+        reorder(w_planes[BACK][:], w_rows[BACK][:], RUN // 4)
+        for c in range(CHUNKS):
             gather_words(1, CHUNK * c, CHUNK * (c + 1))
-        reorder(ws[0][:], ws_raw[0][:], RUN // 4)
+        reorder(w_planes[EXPO][:], w_rows[EXPO][:], RUN // 4)
 
         def product(dst, codes, scales, a, lo, hi, start, stop):
-            plane = v_planes[:, (S * a + lo) // 4 : (S * a + hi) // 4].bitcast(U8)
             nc.tensor.matmul_mx(
-                out=dst, lhsT=codes, lhsT_scale=scales,
-                rhs=v_codes[a][:, lo:hi].bitcast(FP8X4), rhs_scale=plane,
-                start=start, stop=stop,
+                out=dst,
+                lhsT=codes,
+                lhsT_scale=scales,
+                rhs=v_codes[a][:, lo:hi].bitcast(FP8X4),
+                rhs_scale=v_planes[:, (S * a + lo) // 4 : (S * a + hi) // 4].bitcast(U8),
+                start=start,
+                stop=stop,
             )
 
-        def w_scale(w, a, t):
-            first = 64 * t + 32 * a
-            return ws[w][first_row[w] :, first : first + 32].bitcast(U8)
+        def packed_plane(w, a, t):
+            first = (PASSES * t + a) * P // 4
+            return w_planes[w][PLANE_START[w] :, first : first + P // 4].bitcast(U8)
 
-        back = {}
+        warm = bank("warm", len(COPIED + WAITING) - 1)
+        for n in range(WARM_UPS):
+            first = BANK * n % T
+            nc.tensor.matmul_mx(
+                out=warm[:],
+                lhsT=wb_raw[:, 0 : P // 2].bitcast(FP4X4),
+                lhsT_scale=v_rows[:, 0:P],
+                rhs=word_window[0][:, first : first + BANK].bitcast(FP8X4),
+                rhs_scale=v_rows[:, 0:BANK],
+                start=True,
+                stop=True,
+            )
 
-        def background(a, j, first):
+        back_sum = {j: bank(f"back_sum{j}", index) for index, j in enumerate(COPIED + WAITING)}
+        back_copy = {}
+
+        def background(a, j):
             for t in range(SLOTS):
-                col = 128 * t + 64 * a
-                product(back_acc[j][:, P * t : P * (t + 1)], wb_codes[:, col : col + 64].bitcast(FP4X4), w_scale(1, a, t), a, P * j, P * (j + 1),
-                        start=(first and t == 0), stop=(not first and t == SLOTS - 1))
+                first = (PASSES * t + a) * P // 2
+                product(
+                    back_sum[j][:, P * t : P * (t + 1)],
+                    wb_codes[:, first : first + P // 2].bitcast(FP4X4),
+                    packed_plane(BACK, a, t),
+                    a,
+                    P * j,
+                    P * (j + 1),
+                    start=(a == 0 and t == 0),
+                    stop=(a == PASSES - 1 and t == SLOTS - 1),
+                )
 
-        def keep_background(j):
-            back[j] = kept(f"back{j}", [P, BANK], F32)
-            nc.scalar.copy(
-                back[j][:].rearrange("p (n t) -> p n t", t=SLOTS),
-                back_acc[j][:].rearrange("p (t n) -> p n t", t=SLOTS),
-            )
+        def copy_background(j):
+            back_copy[j] = kept(f"back_copy{j}", [P, P, SLOTS], F32)
+            nc.scalar.copy(back_copy[j][:], back_sum[j][:].rearrange("p (t n) -> p n t", t=SLOTS))
 
-        warm = bank("warm", 7)
-        for first in range(0, T, BANK):
-            nc.tensor.matmul_mx(
-                out=warm[:], lhsT=wb_raw[:, 0:64].bitcast(FP4X4), lhsT_scale=v_rows[:, 0:P],
-                rhs=tw_win[0][:, first : first + BANK].bitcast(FP8X4), rhs_scale=v_rows[:, 0:BANK], start=True, stop=True,
-            )
-        back_acc = {j: bank(f"back_acc{j}", index) for index, j in enumerate(COPIED + WAITING)}
-        background(0, COPIED[0], True)
-        for j, ahead in zip(COPIED, COPIED[1:] + (None,)):
-            if ahead is not None:
-                background(0, ahead, True)
-            background(1, j, False)
-            keep_background(j)
+        def taken(j):
+            if j in COPIED:
+                return back_copy[j][:]
+            return back_sum[j][:].rearrange("p (t n) -> p n t", t=SLOTS)
+
+        background(0, COPIED[0])
+        for index, j in enumerate(COPIED):
+            if index + 1 < len(COPIED):
+                background(0, COPIED[index + 1])
+            background(1, j)
+            copy_background(j)
         for j in WAITING:
-            background(0, j, True)
-            background(1, j, False)
+            for a in range(PASSES):
+                background(a, j)
 
         wr_bf = {(a, u): kept(f"wr_bf{a}{u}", [P, 2 * H], BF16) for a in range(PASSES) for u in range(2)}
-        wr_codes = {(a, u): kept(f"wr_codes{a}{u}", [P, 256], U32) for a in range(PASSES) for u in range(2)}
-        wr_scales = [kept(f"wr_scales{a}", [P, H], U8) for a in range(PASSES)]
+        wr_codes = {(a, u): kept(f"wr_codes{a}{u}", [P, 2 * P], U32) for a in range(PASSES) for u in range(2)}
+        wr_planes = [kept(f"wr_planes{a}", [P, H], U8) for a in range(PASSES)]
 
-        def cast_wr(a, first, count, engine_copy):
-            u, s = divmod(first, 2)
-            engine_copy(
-                wr_bf[a, u][:, H * s : H * (s + count)].rearrange("p (t g e i) -> p t g e i", t=count, e=RUN, i=4),
-                wr_raw[a][:].rearrange("p (i g t e) -> p t g e i", i=4, t=SLOTS, e=RUN)[:, first : first + count],
+        def wr_slots(a):
+            return wr_raw[a][:].rearrange("p (i g t e) -> p t g e i", i=4, t=SLOTS, e=RUN)
+
+        def cast_pair(a, u):
+            nc.vector.tensor_copy(
+                wr_bf[a, u][:].rearrange("p (t g e i) -> p t g e i", t=2, e=RUN, i=4), wr_slots(a)[:, 2 * u : 2 * u + 2]
             )
 
         def cast_slot(a, t, engine_copy):
             engine_copy(
                 wr_bf[a, t // 2][:, H * (t % 2) : H * (t % 2 + 1)].rearrange("p (g e i) -> p g e i", e=RUN, i=4),
-                wr_raw[a][:].rearrange("p (i g t e) -> p t g e i", i=4, t=SLOTS, e=RUN)[:, t],
+                wr_slots(a)[:, t],
             )
 
         def quantise_wr(a, u):
             nc.vector.quantize_mx(
                 out=wr_codes[a, u][:].bitcast(FP8X4),
-                scales=wr_scales[a][:, 256 * u : 256 * (u + 1)],
+                scales=wr_planes[a][:, 2 * P * u : 2 * P * (u + 1)],
                 in_=wr_bf[a, u][:],
             )
 
         for u in (1, 0):
-            cast_wr(0, 2 * u, 2, nc.vector.tensor_copy)
+            cast_pair(0, u)
         for u in (1, 0):
             quantise_wr(0, u)
-        for t in range(SLOTS):
-            cast_slot(1, t, nc.scalar.copy if t % 2 else nc.vector.tensor_copy)
+        cast_pair(1, 0)
+        cast_slot(1, 2, nc.scalar.copy)
+        cast_slot(1, 3, nc.vector.tensor_copy)
         for u in range(2):
             quantise_wr(1, u)
         we_codes = kept("we_codes", [P, PASSES * H], I32)
@@ -214,143 +257,184 @@ def tile_list_kmer_locus_enrichment_kernel(
                 we_raw[:].rearrange("p (x t e) -> p t x e", t=SLOTS, e=RUN)[:, 2 * u : 2 * u + 2],
             )
 
-        RATE_BANK = {(0, 0): 0, (0, 1): 1, (1, 1): 2, (1, 0): 1, (2, 0): 0, (2, 1): 1, 6: 0, 7: 1}
-        EXPO_BANK = {(0, 0): 3, (0, 1): 0, (1, 1): 2, (1, 0): 3, (2, 0): 2, (2, 1): 3, 6: 2, 7: 3}
+        def wr_operand(a, t):
+            codes = wr_codes[a, t // 2][:, P * (t % 2) : P * (t % 2 + 1)].bitcast(FP8X4)
+            return codes, wr_planes[a][:, P * t : P * (t + 1)]
 
-        rate = {}
+        def we_operand(a, t):
+            first = (PASSES * t + a) * P
+            return we_codes[:, first : first + P].bitcast(FP8X4), packed_plane(EXPO, a, t)
+
+        opened = []
+
+        def next_bank(name):
+            opened.append(name)
+            return bank(name, (len(opened) - 1) % len(COPIED))
+
+        rate_sum = {}
+        expo_sum = {}
         growth = {}
-        expo = {}
         signal = {}
         h_bf = {}
         h_mx = {}
+        wo_bf = {}
+        wo_codes = {}
+        wo_plane = kept("wo_plane", [P, N], U8)
 
         def rate_pass(a, c, u):
             if a == 0:
-                rate[c, u] = bank(f"rate{c}{u}", RATE_BANK[c, u])
-            lo = CHUNK * c
+                rate_sum[c, u] = next_bank(f"rate{c}{u}")
             for s in range(2):
-                cols = slice(P * (2 * u + s), P * (2 * u + s + 1))
-                product(rate[c, u][:, CHUNK * s : CHUNK * (s + 1)], wr_codes[a, u][:, P * s : P * (s + 1)].bitcast(FP8X4), wr_scales[a][:, cols], a, lo, lo + CHUNK,
-                        start=(a == 0 and s == 0), stop=(a == PASSES - 1 and s == 1))
+                product(
+                    rate_sum[c, u][:, CHUNK * s : CHUNK * (s + 1)],
+                    *wr_operand(a, 2 * u + s),
+                    a,
+                    CHUNK * c,
+                    CHUNK * (c + 1),
+                    start=(a == 0 and s == 0),
+                    stop=(a == PASSES - 1 and s == 1),
+                )
             if a == PASSES - 1:
                 growth[c, u] = at(f"growth{c}{u}", GROWTH_AT[c, u], [P, CHUNK, 2], F32)
-                nc.scalar.activation(growth[c, u][:], rate[c, u][:].rearrange("p (s n) -> p n s", s=2), ACT.Exp)
+                nc.scalar.activation(growth[c, u][:], rate_sum[c, u][:].rearrange("p (s n) -> p n s", s=2), ACT.Exp)
+
+        def rate(c, u):
+            for a in range(PASSES):
+                rate_pass(a, c, u)
 
         def exposure(c, u):
-            lo = CHUNK * c
             if c not in signal:
                 signal[c] = kept(f"signal{c}", [P, 2, CHUNK, 2], F32)
-            acc = bank(f"expo{c}{u}", EXPO_BANK[c, u])
+            acc = next_bank(f"expo{c}{u}")
             for s in range(2):
-                t = 2 * u + s
                 for a in range(PASSES):
-                    first = 256 * t + 128 * a
-                    product(acc[:, CHUNK * s : CHUNK * (s + 1)], we_codes[:, first : first + 128].bitcast(FP8X4), w_scale(0, a, t), a, lo, lo + CHUNK,
-                            start=(a == 0), stop=(a == PASSES - 1))
+                    product(
+                        acc[:, CHUNK * s : CHUNK * (s + 1)],
+                        *we_operand(a, 2 * u + s),
+                        a,
+                        CHUNK * c,
+                        CHUNK * (c + 1),
+                        start=(a == 0),
+                        stop=(a == PASSES - 1),
+                    )
             nc.vector.tensor_tensor(signal[c][:, u], acc[:].rearrange("p (s n) -> p n s", s=2), growth[c, u][:], ALU.mult)
 
         def correct(c):
-            for half, engine in ((0, nc.gpsimd), (1, nc.vector)):
+            for half, engine in enumerate((nc.gpsimd, nc.vector)):
                 j = 2 * c + half
-                h_bf[j] = at(f"h_bf{j}", H_AT[j], [P, P * SLOTS], BF16)
-                if j in back:
-                    taken = back[j][:].rearrange("p (n u s) -> p n u s", u=2, s=2)
-                else:
-                    taken = back_acc[j][:].rearrange("p (u s n) -> p n u s", u=2, s=2)
+                h_bf[j] = at(f"h_bf{j}", H_BF_AT[j], [P, P * SLOTS], BF16)
                 engine.tensor_tensor(
                     h_bf[j][:].rearrange("p (n u s) -> p n u s", u=2, s=2),
                     signal[c][:, :, P * half : P * (half + 1), :].rearrange("p u n s -> p n u s"),
-                    taken,
+                    taken(j).rearrange("p n (u s) -> p n u s", u=2),
                     ALU.subtract,
                 )
 
-        def quantise_h(c):
-            codes = at(f"h_codes{c}", CODES_AT[c], [P, CHUNK], U32)
-            scales = kept(f"h_scales{c}", [P, CHUNK], U8)
-            for half in (0, 1):
+        def quantise_chunk(c):
+            codes = at(f"h_codes{c}", H_CODES_AT[c], [P, CHUNK], U32)
+            plane = kept(f"h_plane{c}", [P, CHUNK], U8)
+            for half in range(2):
                 cols = slice(P * half, P * (half + 1))
-                nc.vector.quantize_mx(out=codes[:, cols].bitcast(FP8X4), scales=scales[:, cols], in_=h_bf[2 * c + half][:])
-            h_mx[CHUNK * c] = (codes, scales)
-
-        wo_scales = kept("wo_scales", [P, N], U8)
-        wo_codes = {}
-
-        wo_bf = {}
+                nc.vector.quantize_mx(out=codes[:, cols].bitcast(FP8X4), scales=plane[:, cols], in_=h_bf[2 * c + half][:])
+            h_mx[CHUNK * c] = (codes, plane)
 
         def cast_wo(b):
-            wo_bf[b] = at(f"wo_bf{b}", WO_AT[b], [P, P, SLOTS], BF16)
+            wo_bf[b] = at(f"wo_bf{b}", WO_BF_AT[b], [P, P, SLOTS], BF16)
             nc.scalar.copy(wo_bf[b][:], wo_raw[:, :, P * b : P * (b + 1)].rearrange("p t n -> p n t"))
 
         def quantise_wo(b):
-            wo_codes[b] = at(f"wo_codes{b}", GROWTH_AT[FIRST[1]] + LINK + 4 * P * b, [P, P], U32)
-            nc.vector.quantize_mx(out=wo_codes[b][:].bitcast(FP8X4), scales=wo_scales[:, P * b : P * (b + 1)], in_=wo_bf[b][:].rearrange("p n t -> p (n t)"))
+            wo_codes[b] = at(f"wo_codes{b}", WO_CODES_AT[b], [P, P], U32)
+            nc.vector.quantize_mx(
+                out=wo_codes[b][:].bitcast(FP8X4),
+                scales=wo_plane[:, P * b : P * (b + 1)],
+                in_=wo_bf[b][:].rearrange("p n t -> p (n t)"),
+            )
+
+        def tile_sum(name, j, operand):
+            acc = next_bank(f"{name}{j}")
+            for a in range(PASSES):
+                for t in range(SLOTS):
+                    product(
+                        acc[:, P * t : P * (t + 1)],
+                        *operand(a, t),
+                        a,
+                        P * j,
+                        P * (j + 1),
+                        start=(a == 0 and t == 0),
+                        stop=(a == PASSES - 1 and t == SLOTS - 1),
+                    )
+            return acc[:].rearrange("p (t n) -> p n t", t=SLOTS)
 
         def rate_tile(j):
-            acc = bank(f"rate_tile{j}", RATE_BANK[j])
-            for a in range(PASSES):
-                for t in range(SLOTS):
-                    product(acc[:, P * t : P * (t + 1)], wr_codes[a, t // 2][:, P * (t % 2) : P * (t % 2 + 1)].bitcast(FP8X4), wr_scales[a][:, P * t : P * (t + 1)],
-                            a, P * j, P * (j + 1), start=(a == 0 and t == 0), stop=(a == PASSES - 1 and t == SLOTS - 1))
-            growth[j] = at(f"growth{j}", GROWTH_AT[3, j % 2], [P, P, SLOTS], F32)
-            nc.scalar.activation(growth[j][:], acc[:].rearrange("p (t n) -> p n t", t=SLOTS), ACT.Exp)
+            summed = tile_sum("rate_tile", j, wr_operand)
+            growth[j] = at(f"growth_tile{j}", GROWTH_AT[j // 2, j % 2], [P, P, SLOTS], F32)
+            nc.scalar.activation(growth[j][:], summed, ACT.Exp)
 
         def exposure_tile(j):
-            expo[j] = bank(f"expo_tile{j}", EXPO_BANK[j])
-            for a in range(PASSES):
-                for t in range(SLOTS):
-                    first = 256 * t + 128 * a
-                    product(expo[j][:, P * t : P * (t + 1)], we_codes[:, first : first + 128].bitcast(FP8X4), w_scale(0, a, t),
-                            a, P * j, P * (j + 1), start=(a == 0 and t == 0), stop=(a == PASSES - 1 and t == SLOTS - 1))
+            expo_sum[j] = tile_sum("expo_tile", j, we_operand)
 
         def grow_piece(j, lo, width):
             signal[j, lo] = kept(f"signal{j}_{lo}", [P, width, SLOTS], F32)
             nc.vector.tensor_tensor(
-                signal[j, lo][:],
-                expo[j][:].rearrange("p (t n) -> p n t", t=SLOTS)[:, lo : lo + width],
-                growth[j][:, lo : lo + width],
-                ALU.mult,
+                signal[j, lo][:], expo_sum[j][:, lo : lo + width], growth[j][:, lo : lo + width], ALU.mult
             )
 
         def correct_piece(j, lo, width):
             h_bf[j, lo] = kept(f"h_bf{j}_{lo}", [P, width * SLOTS], BF16)
-            if j in back:
-                taken = back[j][:, SLOTS * lo : SLOTS * (lo + width)].rearrange("p (n t) -> p n t", t=SLOTS)
-            else:
-                taken = back_acc[j][:].rearrange("p (t n) -> p n t", t=SLOTS)[:, lo : lo + width]
-            nc.vector.tensor_tensor(h_bf[j, lo][:].rearrange("p (n t) -> p n t", t=SLOTS), signal[j, lo][:], taken, ALU.subtract)
+            nc.vector.tensor_tensor(
+                h_bf[j, lo][:].rearrange("p (n t) -> p n t", t=SLOTS),
+                signal[j, lo][:],
+                taken(j)[:, lo : lo + width],
+                ALU.subtract,
+            )
 
         def quantise_piece(j, lo, width):
             codes = kept(f"h_codes{j}_{lo}", [P, width], U32)
-            scales = kept(f"h_scales{j}_{lo}", [P, width], U8)
-            nc.vector.quantize_mx(out=codes[:].bitcast(FP8X4), scales=scales[:], in_=h_bf[j, lo][:])
-            h_mx[P * j + lo] = (codes, scales)
+            plane = kept(f"h_plane{j}_{lo}", [P, width], U8)
+            nc.vector.quantize_mx(out=codes[:].bitcast(FP8X4), scales=plane[:], in_=h_bf[j, lo][:])
+            h_mx[P * j + lo] = (codes, plane)
 
-        def readout(first, width, banks, on_vector=False):
-            codes, scales = h_mx[first]
-            staged = kept(f"staged{first}", [P, BLOCKS, width], F32)
+        def read_out(first, width, banks):
+            codes, plane = h_mx[first]
             per_bank = min(BLOCKS, BANK // width)
             accs = [bank(f"sum{first}_{index}", index) for index in banks]
             sums = [accs[b // per_bank][:, width * (b % per_bank) : width * (b % per_bank + 1)] for b in range(BLOCKS)]
             for b in range(BLOCKS):
                 nc.tensor.matmul_mx(
-                    out=sums[b], lhsT=wo_codes[b][:].bitcast(FP8X4), lhsT_scale=wo_scales[:, P * b : P * (b + 1)],
-                    rhs=codes[:].bitcast(FP8X4), rhs_scale=scales[:], start=True, stop=True,
+                    out=sums[b],
+                    lhsT=wo_codes[b][:].bitcast(FP8X4),
+                    lhsT_scale=wo_plane[:, P * b : P * (b + 1)],
+                    rhs=codes[:].bitcast(FP8X4),
+                    rhs_scale=plane[:],
+                    start=True,
+                    stop=True,
                 )
-            if on_vector:
-                nc.vector.tensor_tensor(
-                    staged[:],
-                    accs[0][:, 0 : BLOCKS * width].rearrange("p (b j) -> p b j", b=BLOCKS),
-                    bias[:].unsqueeze(2).to_broadcast([P, BLOCKS, width]),
-                    ALU.add,
-                )
-            else:
-                for b in range(BLOCKS):
-                    nc.scalar.activation(staged[:, b, :], sums[b], ACT.Identity, bias=bias[:, b : b + 1])
-            if width == CHUNK:
-                for b in range(BLOCKS):
-                    nc.sync.dma_start(out=out[P * b : P * (b + 1), first : first + width], in_=staged[:, b, :])
-            else:
-                nc.sync.dma_start(out=out[:, first : first + width].rearrange("(b p) j -> p b j", p=P), in_=staged[:])
+            return accs, sums
+
+        def store_blocks(first, staged):
+            width = staged.shape[2]
+            nc.sync.dma_start(out=out[:, first : first + width].rearrange("(b p) j -> p b j", p=P), in_=staged[:])
+
+        def finish_on_scalar(first, width, banks):
+            staged = kept(f"staged{first}", [P, BLOCKS, width], F32)
+            sums = read_out(first, width, banks)[1]
+            for b in range(BLOCKS):
+                nc.scalar.activation(staged[:, b, :], sums[b], ACT.Identity, bias=bias[:, b : b + 1])
+            return staged
+
+        def finish_chunk(c, banks):
+            staged = finish_on_scalar(CHUNK * c, CHUNK, banks)
+            for b in range(BLOCKS):
+                nc.sync.dma_start(out=out[P * b : P * (b + 1), CHUNK * c : CHUNK * (c + 1)], in_=staged[:, b, :])
+
+        def finish_piece(j, lo, staged, index):
+            acc = read_out(P * j + lo, PIECE, (index,))[0][0]
+            nc.vector.tensor_tensor(
+                staged[:, :, lo : lo + PIECE],
+                acc[:, 0 : BLOCKS * PIECE].rearrange("p (b j) -> p b j", b=BLOCKS),
+                bias[:].unsqueeze(2).to_broadcast([P, BLOCKS, PIECE]),
+                ALU.add,
+            )
 
         rate_pass(0, 0, 0)
         rate_pass(0, 0, 1)
@@ -360,42 +444,43 @@ def tile_list_kmer_locus_enrichment_kernel(
         exposure(0, 0)
         rate_pass(1, 1, 1)
         exposure(0, 1)
-        rate_pass(0, 1, 0)
-        rate_pass(1, 1, 0)
+        rate(1, 0)
         cast_wo(0)
         cast_wo(1)
         correct(0)
         exposure(1, 1)
         exposure(1, 0)
         cast_wo(2)
-        quantise_h(0)
+        quantise_chunk(0)
         for b in range(BLOCKS):
             quantise_wo(b)
         for u in range(2):
-            rate_pass(0, 2, u)
-            rate_pass(1, 2, u)
+            rate(2, u)
         correct(1)
-        exposure(2, 0)
-        exposure(2, 1)
-        quantise_h(1)
-        rate_tile(6)
-        readout(0, CHUNK, (4, 5))
+        for u in range(2):
+            exposure(2, u)
+        quantise_chunk(1)
+
+        before_last, last = 2 * CHUNKS - 2, 2 * CHUNKS - 1
+        rate_tile(before_last)
+        finish_chunk(0, (4, 5))
         correct(2)
-        exposure_tile(6)
-        rate_tile(7)
-        exposure_tile(7)
-        grow_piece(6, 0, P)
-        readout(CHUNK, CHUNK, (4, 6))
-        correct_piece(6, 0, P)
-        quantise_h(2)
-        readout(2 * CHUNK, CHUNK, (5, 0))
-        grow_piece(7, 0, 64)
-        quantise_piece(6, 0, P)
-        grow_piece(7, 64, 64)
-        readout(6 * P, P, (1,))
-        correct_piece(7, 0, 64)
-        correct_piece(7, 64, 64)
-        quantise_piece(7, 0, 64)
-        readout(7 * P, 64, (2,), on_vector=True)
-        quantise_piece(7, 64, 64)
-        readout(7 * P + 64, 64, (3,), on_vector=True)
+        exposure_tile(before_last)
+        rate_tile(last)
+        exposure_tile(last)
+        grow_piece(before_last, 0, P)
+        finish_chunk(1, (4, 6))
+        correct_piece(before_last, 0, P)
+        quantise_chunk(2)
+        finish_chunk(2, (5, 0))
+        grow_piece(last, 0, PIECE)
+        quantise_piece(before_last, 0, P)
+        grow_piece(last, PIECE, PIECE)
+        store_blocks(P * before_last, finish_on_scalar(P * before_last, P, (1,)))
+        for lo in (0, PIECE):
+            correct_piece(last, lo, PIECE)
+        staged_last = kept("staged_last", [P, BLOCKS, P], F32)
+        for index, lo in ((2, 0), (3, PIECE)):
+            quantise_piece(last, lo, PIECE)
+            finish_piece(last, lo, staged_last, index)
+        store_blocks(P * last, staged_last)

@@ -29,8 +29,9 @@ WARM_UPS = 5
 EXPO, BACK = 0, 1
 PLANE_START = {EXPO: 4, BACK: 0}
 QUADRANTS = (0, 2, 1, 3)
-COPIED = (0, 2, 4, 7)
+COPIED = (0, 2, 4)
 WAITING = (1, 3, 5, 6)
+TURN_BANKS = 4
 
 LINK = 64
 ROOM = 8192
@@ -167,7 +168,7 @@ def tile_list_kmer_locus_enrichment_kernel(
             first = (PASSES * t + a) * P // 4
             return w_planes[w][PLANE_START[w] :, first : first + P // 4].bitcast(U8)
 
-        warm = bank("warm", len(COPIED + WAITING) - 1)
+        warm = bank("warm", TURN_BANKS - 1)
         for n in range(WARM_UPS):
             first = BANK * n % T
             nc.tensor.matmul_mx(
@@ -180,7 +181,8 @@ def tile_list_kmer_locus_enrichment_kernel(
                 stop=True,
             )
 
-        back_sum = {j: bank(f"back_sum{j}", index) for index, j in enumerate(COPIED + WAITING)}
+        back_sum = {j: bank(f"back_sum{j}", index) for index, j in enumerate(COPIED)}
+        back_sum.update({j: bank(f"back_sum{j}", TURN_BANKS + index) for index, j in enumerate(WAITING)})
         back_copy = {}
 
         def background(a, j):
@@ -269,7 +271,7 @@ def tile_list_kmer_locus_enrichment_kernel(
 
         def next_bank(name):
             opened.append(name)
-            return bank(name, (len(opened) - 1) % len(COPIED))
+            return bank(name, (len(opened) - 1) % TURN_BANKS)
 
         rate_sum = {}
         expo_sum = {}
@@ -470,9 +472,12 @@ def tile_list_kmer_locus_enrichment_kernel(
         exposure_tile(last)
         grow_piece(before_last, 0, P)
         finish_chunk(1, (4, 6))
+        back_sum[last] = bank("back_sum_last", 0)
+        for a in range(PASSES):
+            background(a, last)
         correct_piece(before_last, 0, P)
         quantise_chunk(2)
-        finish_chunk(2, (5, 0))
+        finish_chunk(2, (5, 2))
         grow_piece(last, 0, PIECE)
         quantise_piece(before_last, 0, P)
         grow_piece(last, PIECE, PIECE)
@@ -480,7 +485,7 @@ def tile_list_kmer_locus_enrichment_kernel(
         for lo in (0, PIECE):
             correct_piece(last, lo, PIECE)
         staged_last = kept("staged_last", [P, BLOCKS, P], F32)
-        for index, lo in ((2, 0), (3, PIECE)):
+        for index, lo in ((7, 0), (3, PIECE)):
             quantise_piece(last, lo, PIECE)
             finish_piece(last, lo, staged_last, index)
         store_blocks(P * last, staged_last)

@@ -25,7 +25,6 @@ CHUNKS = S // CHUNK
 BANK = 512
 BLOCKS = N // P
 PIECE = 64
-WARM_UPS = 5
 EXPO, BACK = 0, 1
 PLANE_START = {EXPO: 4, BACK: 0}
 QUADRANTS = (0, 2, 1, 3)
@@ -167,19 +166,6 @@ def tile_list_kmer_locus_enrichment_kernel(
         def packed_plane(w, a, t):
             first = (PASSES * t + a) * P // 4
             return w_planes[w][PLANE_START[w] :, first : first + P // 4].bitcast(U8)
-
-        warm = bank("warm", TURN_BANKS - 1)
-        for n in range(WARM_UPS):
-            first = BANK * n % T
-            nc.tensor.matmul_mx(
-                out=warm[:],
-                lhsT=wb_raw[:, 0 : P // 2].bitcast(FP4X4),
-                lhsT_scale=v_rows[:, 0:P],
-                rhs=word_window[0][:, first : first + BANK].bitcast(FP8X4),
-                rhs_scale=v_rows[:, 0:BANK],
-                start=True,
-                stop=True,
-            )
 
         back_sum = {j: bank(f"back_sum{j}", index) for index, j in enumerate(COPIED)}
         back_sum.update({j: bank(f"back_sum{j}", TURN_BANKS + index) for index, j in enumerate(WAITING)})

@@ -30,6 +30,7 @@ PLANE_START = {EXPO: 4, BACK: 0}
 QUADRANTS = (0, 2, 1, 3)
 COPIED = (0, 2, 4)
 WAITING = (1, 3, 5, 6)
+HALF = S // 2
 TURN_BANKS = 4
 
 LINK = 64
@@ -37,19 +38,24 @@ ROOM = 8192
 GROWTH_BYTES = 4 * BANK
 BF_BYTES = 2 * BANK
 GROWTH_AT = {(c, u): ROOM * (1 + 2 * c + u) for c in range(CHUNKS) for u in range(2)}
+FREE_AT = ROOM * (1 + 2 * CHUNKS)
+BACK_COPY_AT = {}
 NEXT_GROWTH = (GROWTH_AT[1, 1], GROWTH_AT[2, 0], GROWTH_AT[3, 0])
 H_CODES_AT = [first - 4 * CHUNK + LINK for first in NEXT_GROWTH]
 WO_CODES_AT = [NEXT_GROWTH[0] + LINK + 4 * P * b for b in range(BLOCKS)]
 WO_BF_AT = (GROWTH_AT[0, 0] + GROWTH_BYTES - LINK, GROWTH_AT[0, 1] + GROWTH_BYTES - LINK, GROWTH_AT[0, 1] - BF_BYTES + LINK)
-FREE_AT = ROOM * (1 + 2 * CHUNKS)
 H_BF_AT = {
     0: FREE_AT,
     1: WO_BF_AT[2] - 2 * (BF_BYTES - LINK),
     2: WO_BF_AT[2] - (BF_BYTES - LINK),
     3: FREE_AT + BF_BYTES,
-    4: FREE_AT + 2 * BF_BYTES - LINK,
+    4: WO_BF_AT[2] - (BF_BYTES - LINK) + LINK,
     5: FREE_AT + 3 * BF_BYTES,
+    6: FREE_AT + 4 * BF_BYTES,
+    7: FREE_AT + 3 * ROOM,
 }
+PIECES_AT = FREE_AT + 4 * ROOM
+STAGED6_AT = PIECES_AT + 16 * CHUNK - LINK
 
 
 def tile_list_kmer_locus_enrichment_kernel(
@@ -186,7 +192,10 @@ def tile_list_kmer_locus_enrichment_kernel(
                 )
 
         def copy_background(j):
-            back_copy[j] = kept(f"back_copy{j}", [P, P, SLOTS], F32)
+            if j in BACK_COPY_AT:
+                back_copy[j] = at(f"back_copy{j}", BACK_COPY_AT[j], [P, P, SLOTS], F32)
+            else:
+                back_copy[j] = kept(f"back_copy{j}", [P, P, SLOTS], F32)
             nc.scalar.copy(back_copy[j][:], back_sum[j][:].rearrange("p (t n) -> p n t", t=SLOTS))
 
         def taken(j):
@@ -253,12 +262,6 @@ def tile_list_kmer_locus_enrichment_kernel(
             first = (PASSES * t + a) * P
             return we_codes[:, first : first + P].bitcast(FP8X4), packed_plane(EXPO, a, t)
 
-        opened = []
-
-        def next_bank(name):
-            opened.append(name)
-            return bank(name, (len(opened) - 1) % TURN_BANKS)
-
         rate_sum = {}
         expo_sum = {}
         growth = {}
@@ -269,9 +272,9 @@ def tile_list_kmer_locus_enrichment_kernel(
         wo_codes = {}
         wo_plane = kept("wo_plane", [P, N], U8)
 
-        def rate_pass(a, c, u):
+        def rate_pass(a, c, u, index=None):
             if a == 0:
-                rate_sum[c, u] = next_bank(f"rate{c}{u}")
+                rate_sum[c, u] = bank(f"rate{c}{u}", index)
             for s in range(2):
                 product(
                     rate_sum[c, u][:, CHUNK * s : CHUNK * (s + 1)],
@@ -286,14 +289,14 @@ def tile_list_kmer_locus_enrichment_kernel(
                 growth[c, u] = at(f"growth{c}{u}", GROWTH_AT[c, u], [P, CHUNK, 2], F32)
                 nc.scalar.activation(growth[c, u][:], rate_sum[c, u][:].rearrange("p (s n) -> p n s", s=2), ACT.Exp)
 
-        def rate(c, u):
+        def rate(c, u, index):
             for a in range(PASSES):
-                rate_pass(a, c, u)
+                rate_pass(a, c, u, index)
 
-        def exposure(c, u):
+        def exposure(c, u, index):
             if c not in signal:
                 signal[c] = kept(f"signal{c}", [P, 2, CHUNK, 2], F32)
-            acc = next_bank(f"expo{c}{u}")
+            acc = expo_sum[c, u] = bank(f"expo{c}{u}", index)
             for s in range(2):
                 for a in range(PASSES):
                     product(
@@ -305,10 +308,14 @@ def tile_list_kmer_locus_enrichment_kernel(
                         start=(a == 0),
                         stop=(a == PASSES - 1),
                     )
-            nc.vector.tensor_tensor(signal[c][:, u], acc[:].rearrange("p (s n) -> p n s", s=2), growth[c, u][:], ALU.mult)
 
-        def correct(c):
-            for half, engine in enumerate((nc.gpsimd, nc.vector)):
+        def grow(c, u, lo=0, hi=CHUNK):
+            summed = expo_sum[c, u][:].rearrange("p (s n) -> p n s", s=2)
+            nc.vector.tensor_tensor(signal[c][:, u, lo:hi], summed[:, lo:hi], growth[c, u][:, lo:hi], ALU.mult)
+
+        def correct(c, halves=(0, 1)):
+            for half in halves:
+                engine = (nc.gpsimd, nc.vector)[half]
                 j = 2 * c + half
                 h_bf[j] = at(f"h_bf{j}", H_BF_AT[j], [P, P * SLOTS], BF16)
                 engine.tensor_tensor(
@@ -326,9 +333,13 @@ def tile_list_kmer_locus_enrichment_kernel(
                 nc.vector.quantize_mx(out=codes[:, cols].bitcast(FP8X4), scales=plane[:, cols], in_=h_bf[2 * c + half][:])
             h_mx[CHUNK * c] = (codes, plane)
 
-        def cast_wo(b):
+        def cast_wo(b, on_gpsimd=False):
             wo_bf[b] = at(f"wo_bf{b}", WO_BF_AT[b], [P, P, SLOTS], BF16)
-            nc.scalar.copy(wo_bf[b][:], wo_raw[:, :, P * b : P * (b + 1)].rearrange("p t n -> p n t"))
+            rows = wo_raw[:, :, P * b : P * (b + 1)].rearrange("p t n -> p n t")
+            if on_gpsimd:
+                nc.gpsimd.tensor_scalar(wo_bf[b][:], rows, 1.0, 0.0, ALU.mult, ALU.add)
+            else:
+                nc.scalar.copy(wo_bf[b][:], rows)
 
         def quantise_wo(b):
             wo_codes[b] = at(f"wo_codes{b}", WO_CODES_AT[b], [P, P], U32)
@@ -338,8 +349,8 @@ def tile_list_kmer_locus_enrichment_kernel(
                 in_=wo_bf[b][:].rearrange("p n t -> p (n t)"),
             )
 
-        def tile_sum(name, j, operand):
-            acc = next_bank(f"{name}{j}")
+        def tile_sum(name, j, operand, index):
+            acc = bank(f"{name}{j}", index)
             for a in range(PASSES):
                 for t in range(SLOTS):
                     product(
@@ -353,24 +364,25 @@ def tile_list_kmer_locus_enrichment_kernel(
                     )
             return acc[:].rearrange("p (t n) -> p n t", t=SLOTS)
 
-        def rate_tile(j):
-            summed = tile_sum("rate_tile", j, wr_operand)
+        def rate_tile(j, index):
+            summed = tile_sum("rate_tile", j, wr_operand, index)
             growth[j] = at(f"growth_tile{j}", GROWTH_AT[j // 2, j % 2], [P, P, SLOTS], F32)
             nc.scalar.activation(growth[j][:], summed, ACT.Exp)
 
-        def exposure_tile(j):
-            expo_sum[j] = tile_sum("expo_tile", j, we_operand)
+        def exposure_tile(j, index):
+            expo_sum[j] = tile_sum("expo_tile", j, we_operand, index)
 
         def grow_piece(j, lo, width):
-            signal[j, lo] = kept(f"signal{j}_{lo}", [P, width, SLOTS], F32)
+            signal[j, lo] = at(f"signal{j}_{lo}", PIECES_AT + 16 * (P * (j % 2) + lo), [P, width, SLOTS], F32)
             nc.vector.tensor_tensor(
                 signal[j, lo][:], expo_sum[j][:, lo : lo + width], growth[j][:, lo : lo + width], ALU.mult
             )
 
         def correct_piece(j, lo, width):
-            h_bf[j, lo] = kept(f"h_bf{j}_{lo}", [P, width * SLOTS], BF16)
+            if lo == 0:
+                h_bf[j] = at(f"h_bf{j}", H_BF_AT[j], [P, P * SLOTS], BF16)
             nc.vector.tensor_tensor(
-                h_bf[j, lo][:].rearrange("p (n t) -> p n t", t=SLOTS),
+                h_bf[j][:, SLOTS * lo : SLOTS * (lo + width)].rearrange("p (n t) -> p n t", t=SLOTS),
                 signal[j, lo][:],
                 taken(j)[:, lo : lo + width],
                 ALU.subtract,
@@ -379,7 +391,7 @@ def tile_list_kmer_locus_enrichment_kernel(
         def quantise_piece(j, lo, width):
             codes = kept(f"h_codes{j}_{lo}", [P, width], U32)
             plane = kept(f"h_plane{j}_{lo}", [P, width], U8)
-            nc.vector.quantize_mx(out=codes[:].bitcast(FP8X4), scales=plane[:], in_=h_bf[j, lo][:])
+            nc.vector.quantize_mx(out=codes[:].bitcast(FP8X4), scales=plane[:], in_=h_bf[j][:, SLOTS * lo : SLOTS * (lo + width)])
             h_mx[P * j + lo] = (codes, plane)
 
         def read_out(first, width, banks):
@@ -410,68 +422,89 @@ def tile_list_kmer_locus_enrichment_kernel(
                 nc.scalar.activation(staged[:, b, :], sums[b], ACT.Identity, bias=bias[:, b : b + 1])
             return staged
 
-        def finish_chunk(c, banks):
-            staged = finish_on_scalar(CHUNK * c, CHUNK, banks)
-            for b in range(BLOCKS):
-                nc.sync.dma_start(out=out[P * b : P * (b + 1), CHUNK * c : CHUNK * (c + 1)], in_=staged[:, b, :])
+        def read_chunk(c, banks):
+            return kept(f"staged{c}", [P, BLOCKS, CHUNK], F32), read_out(CHUNK * c, CHUNK, banks)[1]
 
-        def finish_piece(j, lo, staged, index):
-            acc = read_out(P * j + lo, PIECE, (index,))[0][0]
+        def finish_block(c, read, b):
+            staged, sums = read
+            nc.scalar.activation(staged[:, b, :], sums[b], ACT.Identity, bias=bias[:, b : b + 1])
+            nc.sync.dma_start(out=out[P * b : P * (b + 1), CHUNK * c : CHUNK * (c + 1)], in_=staged[:, b, :])
+
+        def add_bias(acc, width, dst):
             nc.vector.tensor_tensor(
-                staged[:, :, lo : lo + PIECE],
-                acc[:, 0 : BLOCKS * PIECE].rearrange("p (b j) -> p b j", b=BLOCKS),
-                bias[:].unsqueeze(2).to_broadcast([P, BLOCKS, PIECE]),
+                dst,
+                acc[:, 0 : BLOCKS * width].rearrange("p (b j) -> p b j", b=BLOCKS),
+                bias[:].unsqueeze(2).to_broadcast([P, BLOCKS, width]),
                 ALU.add,
             )
 
-        rate_pass(0, 0, 0)
-        rate_pass(0, 0, 1)
-        rate_pass(0, 1, 1)
+        rate_pass(0, 0, 0, 0)
+        rate_pass(0, 0, 1, 1)
+        rate_pass(0, 1, 1, 2)
         rate_pass(1, 0, 0)
         rate_pass(1, 0, 1)
-        exposure(0, 0)
+        exposure(0, 0, 3)
+        grow(0, 0)
         rate_pass(1, 1, 1)
-        exposure(0, 1)
-        rate(1, 0)
+        exposure(0, 1, 0)
+        grow(0, 1, P, CHUNK)
+        grow(0, 1, 0, P)
+        rate(1, 0, 1)
         cast_wo(0)
         cast_wo(1)
         correct(0)
-        exposure(1, 1)
-        exposure(1, 0)
+        exposure(1, 1, 2)
+        grow(1, 1)
+        exposure(1, 0, 3)
+        grow(1, 0)
         cast_wo(2)
         quantise_chunk(0)
         for b in range(BLOCKS):
             quantise_wo(b)
-        for u in range(2):
-            rate(2, u)
+        rate(2, 0, 0)
+        rate(2, 1, 1)
         correct(1)
-        for u in range(2):
-            exposure(2, u)
+        exposure(2, 0, 2)
+        grow(2, 0)
+        exposure(2, 1, 3)
+        grow(2, 1)
         quantise_chunk(1)
 
         before_last, last = 2 * CHUNKS - 2, 2 * CHUNKS - 1
-        rate_tile(before_last)
-        finish_chunk(0, (4, 5))
+        rate_tile(before_last, 0)
+        sums0 = read_chunk(0, (4, 5))
+        for b in range(BLOCKS):
+            finish_block(0, sums0, b)
         correct(2)
-        exposure_tile(before_last)
-        rate_tile(last)
-        exposure_tile(last)
-        grow_piece(before_last, 0, P)
-        finish_chunk(1, (4, 6))
-        back_sum[last] = bank("back_sum_last", 0)
+        exposure_tile(before_last, 1)
+        rate_tile(last, 2)
+        for lo in (0, PIECE):
+            grow_piece(before_last, lo, PIECE)
+        sums1 = read_chunk(1, (0, 6))
+        for b in range(BLOCKS):
+            finish_block(1, sums1, b)
+        exposure_tile(last, 3)
+        back_sum[last] = bank("back_sum_last", 4)
         for a in range(PASSES):
             background(a, last)
-        correct_piece(before_last, 0, P)
+        for lo in (0, PIECE):
+            correct_piece(before_last, lo, PIECE)
         quantise_chunk(2)
-        finish_chunk(2, (5, 2))
+        sums2 = read_chunk(2, (5, 2))
+        for b in range(BLOCKS):
+            finish_block(2, sums2, b)
         grow_piece(last, 0, PIECE)
         quantise_piece(before_last, 0, P)
         grow_piece(last, PIECE, PIECE)
-        store_blocks(P * before_last, finish_on_scalar(P * before_last, P, (1,)))
+        sum6 = read_out(P * before_last, P, (1,))[0][0]
         for lo in (0, PIECE):
             correct_piece(last, lo, PIECE)
         staged_last = kept("staged_last", [P, BLOCKS, P], F32)
-        for index, lo in ((7, 0), (3, PIECE)):
+        for lo in (0, PIECE):
             quantise_piece(last, lo, PIECE)
-            finish_piece(last, lo, staged_last, index)
+        staged6 = at("staged6", STAGED6_AT, [P, BLOCKS, P], F32)
+        add_bias(sum6, P, staged6[:])
+        store_blocks(P * before_last, staged6)
+        for index, lo in ((7, 0), (3, PIECE)):
+            add_bias(read_out(P * last + lo, PIECE, (index,))[0][0], PIECE, staged_last[:, :, lo : lo + PIECE])
         store_blocks(P * last, staged_last)

@@ -43,17 +43,18 @@ BACK_COPY_AT = {}
 NEXT_GROWTH = (GROWTH_AT[1, 1], GROWTH_AT[2, 0], GROWTH_AT[3, 0])
 H_CODES_AT = [first - 4 * CHUNK + LINK for first in NEXT_GROWTH]
 WO_CODES_AT = [NEXT_GROWTH[0] + LINK + 4 * P * b for b in range(BLOCKS)]
-WO_BF_AT = (GROWTH_AT[0, 0] + GROWTH_BYTES - LINK, GROWTH_AT[0, 1] + GROWTH_BYTES - LINK, GROWTH_AT[0, 1] - BF_BYTES + LINK)
+WO_BF_AT = (FREE_AT + 2 * ROOM, GROWTH_AT[0, 1] - BF_BYTES + LINK, GROWTH_AT[0, 1] + GROWTH_BYTES - LINK)
 H_BF_AT = {
     0: FREE_AT,
-    1: WO_BF_AT[2] - 2 * (BF_BYTES - LINK),
-    2: WO_BF_AT[2] - (BF_BYTES - LINK),
+    1: WO_BF_AT[1] - 2 * (BF_BYTES - LINK),
+    2: WO_BF_AT[1] - (BF_BYTES - LINK),
     3: FREE_AT + BF_BYTES,
-    4: WO_BF_AT[2] - (BF_BYTES - LINK) + LINK,
+    4: WO_BF_AT[1] - (BF_BYTES - LINK) + LINK,
     5: FREE_AT + 3 * BF_BYTES,
     6: FREE_AT + 4 * BF_BYTES,
     7: FREE_AT + 3 * ROOM,
 }
+H_CHUNK_AT = {0: FREE_AT + 5 * BF_BYTES, 2: H_BF_AT[2] - BF_BYTES}
 PIECES_AT = FREE_AT + 4 * ROOM
 STAGED6_AT = PIECES_AT + 16 * CHUNK - LINK
 
@@ -151,7 +152,8 @@ def tile_list_kmer_locus_enrichment_kernel(
                 v_codes[a][:, lo:hi], word_window[a][:].bitcast(U32).indirect(offsets[:, lo // 16 : hi // 16])
             )
 
-        gather_words(0, 0, S)
+        gather_words(0, 0, CHUNK)
+        gather_words(0, CHUNK, S)
         reorder(wb_codes[:], wb_raw[:], RUN // 2)
         reorder(w_planes[BACK][:], w_rows[BACK][:], RUN // 4)
         for c in range(CHUNKS):
@@ -167,6 +169,18 @@ def tile_list_kmer_locus_enrichment_kernel(
                 rhs_scale=v_planes[:, (S * a + lo) // 4 : (S * a + hi) // 4].bitcast(U8),
                 start=start,
                 stop=stop,
+            )
+
+        warm = bank("warm", 3)
+        for repeat in range(5):
+            nc.tensor.matmul_mx(
+                out=warm[:],
+                lhsT=v_codes[0][:, 0:P].bitcast(FP8X4),
+                lhsT_scale=v_rows[:, 0:P],
+                rhs=word_window[0][:, 0:BANK].bitcast(FP8X4),
+                rhs_scale=v_rows[:, 0:BANK],
+                start=True,
+                stop=True,
             )
 
         def packed_plane(w, a, t):
@@ -267,6 +281,7 @@ def tile_list_kmer_locus_enrichment_kernel(
         growth = {}
         signal = {}
         h_bf = {}
+        h_chunk = {}
         h_mx = {}
         wo_bf = {}
         wo_codes = {}
@@ -317,9 +332,14 @@ def tile_list_kmer_locus_enrichment_kernel(
             for half in halves:
                 engine = (nc.gpsimd, nc.vector)[half]
                 j = 2 * c + half
-                h_bf[j] = at(f"h_bf{j}", H_BF_AT[j], [P, P * SLOTS], BF16)
+                if c == 1:
+                    h_bf[j] = at(f"h_bf{j}", H_BF_AT[j], [P, P * SLOTS], BF16)[:]
+                else:
+                    if half == 0:
+                        h_chunk[c] = at(f"h_chunk{c}", H_CHUNK_AT[c], [P, CHUNK * SLOTS], BF16)
+                    h_bf[j] = h_chunk[c][:, BANK * half : BANK * (half + 1)]
                 engine.tensor_tensor(
-                    h_bf[j][:].rearrange("p (n u s) -> p n u s", u=2, s=2),
+                    h_bf[j].rearrange("p (n u s) -> p n u s", u=2, s=2),
                     signal[c][:, :, P * half : P * (half + 1), :].rearrange("p u n s -> p n u s"),
                     taken(j).rearrange("p n (u s) -> p n u s", u=2),
                     ALU.subtract,
@@ -328,9 +348,12 @@ def tile_list_kmer_locus_enrichment_kernel(
         def quantise_chunk(c):
             codes = at(f"h_codes{c}", H_CODES_AT[c], [P, CHUNK], U32)
             plane = kept(f"h_plane{c}", [P, CHUNK], U8)
-            for half in range(2):
-                cols = slice(P * half, P * (half + 1))
-                nc.vector.quantize_mx(out=codes[:, cols].bitcast(FP8X4), scales=plane[:, cols], in_=h_bf[2 * c + half][:])
+            if c == 1:
+                for half in range(2):
+                    cols = slice(P * half, P * (half + 1))
+                    nc.vector.quantize_mx(out=codes[:, cols].bitcast(FP8X4), scales=plane[:, cols], in_=h_bf[2 * c + half])
+            else:
+                nc.vector.quantize_mx(out=codes[:].bitcast(FP8X4), scales=plane[:], in_=h_chunk[c][:])
             h_mx[CHUNK * c] = (codes, plane)
 
         def cast_wo(b, on_gpsimd=False):
@@ -450,7 +473,7 @@ def tile_list_kmer_locus_enrichment_kernel(
         grow(0, 1, P, CHUNK)
         grow(0, 1, 0, P)
         rate(1, 0, 1)
-        cast_wo(0)
+        cast_wo(0, on_gpsimd=True)
         cast_wo(1)
         correct(0)
         exposure(1, 1, 2)

@@ -28,7 +28,7 @@ PIECE = 64
 EXPO, BACK = 0, 1
 PLANE_START = {EXPO: 4, BACK: 0}
 QUADRANTS = (0, 2, 1, 3)
-COPIED = (0, 2, 4)
+COPIED = (0, 2, 4, 7)
 WAITING = (1, 3, 5, 6)
 HALF = S // 2
 TURN_BANKS = 4
@@ -507,9 +507,6 @@ def tile_list_kmer_locus_enrichment_kernel(
         for b in range(BLOCKS):
             finish_block(1, sums1, b)
         exposure_tile(last, 3)
-        back_sum[last] = bank("back_sum_last", 4)
-        for a in range(PASSES):
-            background(a, last)
         for lo in (0, PIECE):
             correct_piece(before_last, lo, PIECE)
         quantise_chunk(2)

@@ -74,13 +74,16 @@ def tile_list_kmer_locus_enrichment_kernel(
         def kept(name, shape, dtype):
             return keep.tile(shape, dtype, name=name, align_bytes=64)
 
+        def streamed(name, shape, dtype):
+            return keep.tile(shape, dtype, name=name, align_bytes=256)
+
         def at(name, offset, shape, dtype):
             return placed.tile(shape, dtype, name=name, offset=offset, align_bytes=64)
 
         offsets = keep.tile([P, S // 16], U16, name="offsets")
         nc.sync.dma_start(offsets[:], offs)
 
-        scale_window = kept("scale_window", [P, T // 4], I32)
+        scale_window = streamed("scale_window", [P, T // 4], I32)
         v_rows = kept("v_rows", [P, S], U8)
         v_planes = kept("v_planes", [P, PASSES * S // 4], I32)
         w_rows = {w: kept(f"w_rows{w}", [P, PASSES * H // 4], I32) for w in (EXPO, BACK)}
@@ -90,7 +93,7 @@ def tile_list_kmer_locus_enrichment_kernel(
         nc.vector.memset(scale_window[32:64, :], 0)
         nc.vector.memset(scale_window[64:128, :], 0)
         nc.vector.memset(v_planes[:], 0)
-        wb_raw = kept("wb_raw", [P, PASSES * H // 2], I32)
+        wb_raw = streamed("wb_raw", [P, PASSES * H // 2], I32)
 
         def load_scales(w, scales, quadrants):
             for q in quadrants:
@@ -100,7 +103,7 @@ def tile_list_kmer_locus_enrichment_kernel(
                     in_=scales[:, 4 * q : 4 * q + 4, :].rearrange("a r c -> r a c").bitcast(I32),
                 )
 
-        word_window = [kept(f"word_window{a}", [P, T], I32) for a in range(PASSES)]
+        word_window = [streamed(f"word_window{a}", [P, T], I32) for a in range(PASSES)]
 
         def load_table(a):
             nc.sync.dma_start(out=word_window[a][:], in_=tab_words[a].rearrange("p t i -> p (t i)").bitcast(I32))
@@ -117,7 +120,7 @@ def tile_list_kmer_locus_enrichment_kernel(
         for q in QUADRANTS:
             nc.sync.dma_start(out=v_planes[32 * q : 32 * q + 4, :], in_=v_rows[8 * q : 8 * q + 8, :].bitcast(I32))
 
-        wr_raw = [kept(f"wr_raw{a}", [P, 4 * H], F32) for a in range(PASSES)]
+        wr_raw = [streamed(f"wr_raw{a}", [P, 4 * H], F32) for a in range(PASSES)]
 
         def load_wr(a):
             nc.sync.dma_start(out=wr_raw[a][:], in_=wr[512 * a : 512 * (a + 1), :].rearrange("(p i) c -> p (i c)", i=4))
@@ -125,8 +128,8 @@ def tile_list_kmer_locus_enrichment_kernel(
         load_wr(0)
         load_scales(EXPO, we_scales, QUADRANTS[2:])
         load_wr(1)
-        we_raw = kept("we_raw", [P, PASSES * H], I32)
-        wo_raw = kept("wo_raw", [P, SLOTS, N], F32)
+        we_raw = streamed("we_raw", [P, PASSES * H], I32)
+        wo_raw = streamed("wo_raw", [P, SLOTS, N], F32)
         bias = kept("bias", [P, BLOCKS], F32)
         nc.sync.dma_start(
             out=we_raw[:].rearrange("p (a c) -> p a c", a=PASSES),
@@ -446,7 +449,7 @@ def tile_list_kmer_locus_enrichment_kernel(
             return staged
 
         def read_chunk(c, banks):
-            return kept(f"staged{c}", [P, BLOCKS, CHUNK], F32), read_out(CHUNK * c, CHUNK, banks)[1]
+            return streamed(f"staged{c}", [P, BLOCKS, CHUNK], F32), read_out(CHUNK * c, CHUNK, banks)[1]
 
         def finish_block(c, read, b):
             staged, sums = read
@@ -519,7 +522,7 @@ def tile_list_kmer_locus_enrichment_kernel(
         sum6 = read_out(P * before_last, P, (1,))[0][0]
         for lo in (0, PIECE):
             correct_piece(last, lo, PIECE)
-        staged_last = kept("staged_last", [P, BLOCKS, P], F32)
+        staged_last = streamed("staged_last", [P, BLOCKS, P], F32)
         for lo in (0, PIECE):
             quantise_piece(last, lo, PIECE)
         staged6 = at("staged6", STAGED6_AT, [P, BLOCKS, P], F32)

@@ -141,9 +141,9 @@ def tile_list_kmer_locus_enrichment_kernel(
             nc.sync.dma_start(out=bias[:], in_=bo.rearrange("(b p) -> p b", p=P))
 
         def reorder(dst, src, run):
-            nc.vector.tensor_copy(
-                dst.rearrange("p (t x e) -> p t x e", t=SLOTS, e=run),
-                src.rearrange("p (x t e) -> p t x e", t=SLOTS, e=run),
+            nc.scalar.copy(
+                dst.bitcast(U32).rearrange("p (t x e) -> p t x e", t=SLOTS, e=run),
+                src.bitcast(U32).rearrange("p (x t e) -> p t x e", t=SLOTS, e=run),
             )
 
         wb_codes = kept("wb_codes", [P, PASSES * H // 2], I32)
@@ -259,17 +259,28 @@ def tile_list_kmer_locus_enrichment_kernel(
             cast_pair(0, u)
         for u in (1, 0):
             quantise_wr(0, u)
-        cast_pair(1, 0)
-        cast_slot(1, 2, nc.scalar.copy)
-        cast_slot(1, 3, nc.vector.tensor_copy)
-        for u in range(2):
-            quantise_wr(1, u)
         we_codes = kept("we_codes", [P, PASSES * H], I32)
-        for u in range(2):
+
+        def quantise_slot(t):
+            nc.vector.quantize_mx(
+                out=wr_codes[1, t // 2][:, P * (t % 2) : P * (t % 2 + 1)].bitcast(FP8X4),
+                scales=wr_planes[1][:, P * t : P * (t + 1)],
+                in_=wr_bf[1, t // 2][:, H * (t % 2) : H * (t % 2 + 1)],
+            )
+
+        def reorder_we(u):
             nc.vector.tensor_copy(
                 we_codes[:, H * u : H * (u + 1)].rearrange("p (t x e) -> p t x e", t=2, e=RUN),
                 we_raw[:].rearrange("p (x t e) -> p t x e", t=SLOTS, e=RUN)[:, 2 * u : 2 * u + 2],
             )
+
+        for t in range(SLOTS):
+            cast_slot(1, t, nc.vector.tensor_copy if t < 2 else nc.scalar.copy)
+        for t in range(SLOTS - 1):
+            quantise_slot(t)
+        reorder_we(0)
+        quantise_slot(SLOTS - 1)
+        reorder_we(1)
 
         def wr_operand(a, t):
             codes = wr_codes[a, t // 2][:, P * (t % 2) : P * (t % 2 + 1)].bitcast(FP8X4)

@@ -28,8 +28,10 @@ PIECE = 64
 EXPO, BACK = 0, 1
 PLANE_START = {EXPO: 4, BACK: 0}
 QUADRANTS = (0, 2, 1, 3)
-COPIED = (0, 2, 4, 7)
-WAITING = (1, 3, 5, 6)
+SPANS = (1, 5)
+ON_GPSIMD = (1, 2, 5)
+WAITING = (0, 3, 4, 7)
+BEFORE_LAST, LAST = 7, 6
 HALF = S // 2
 TURN_BANKS = 4
 
@@ -39,7 +41,6 @@ GROWTH_BYTES = 4 * BANK
 BF_BYTES = 2 * BANK
 GROWTH_AT = {(c, u): ROOM * (1 + 2 * c + u) for c in range(CHUNKS) for u in range(2)}
 FREE_AT = ROOM * (1 + 2 * CHUNKS)
-BACK_COPY_AT = {}
 NEXT_GROWTH = (GROWTH_AT[1, 1], GROWTH_AT[2, 0], GROWTH_AT[3, 0])
 H_CODES_AT = [first - 4 * CHUNK + LINK for first in NEXT_GROWTH]
 WO_CODES_AT = [NEXT_GROWTH[0] + LINK + 4 * P * b for b in range(BLOCKS)]
@@ -159,8 +160,8 @@ def tile_list_kmer_locus_enrichment_kernel(
         gather_words(0, CHUNK, S)
         reorder(wb_codes[:], wb_raw[:], RUN // 2)
         reorder(w_planes[BACK][:], w_rows[BACK][:], RUN // 4)
-        for c in range(CHUNKS):
-            gather_words(1, CHUNK * c, CHUNK * (c + 1))
+        for first, tiles in ((0, 3), (5, 3), (3, 2)):
+            gather_words(1, P * first, P * (first + tiles))
         reorder(w_planes[EXPO][:], w_rows[EXPO][:], RUN // 4)
 
         def product(dst, codes, scales, a, lo, hi, start, stop):
@@ -190,45 +191,39 @@ def tile_list_kmer_locus_enrichment_kernel(
             first = (PASSES * t + a) * P // 4
             return w_planes[w][PLANE_START[w] :, first : first + P // 4].bitcast(U8)
 
-        back_sum = {j: bank(f"back_sum{j}", index) for index, j in enumerate(COPIED)}
-        back_sum.update({j: bank(f"back_sum{j}", TURN_BANKS + index) for index, j in enumerate(WAITING)})
-        back_copy = {}
+        back_sum = {j: bank(f"back_sum{j}", TURN_BANKS + index) for index, j in enumerate(WAITING)}
+        span_sum = {(j, u): bank(f"span_sum{j}{u}", 2 * k + u) for k, j in enumerate(SPANS) for u in range(2)}
+        span_copy = {j: kept(f"span_copy{j}", [P, 2, CHUNK, 2], F32) for j in SPANS}
 
-        def background(a, j):
-            for t in range(SLOTS):
-                first = (PASSES * t + a) * P // 2
-                product(
-                    back_sum[j][:, P * t : P * (t + 1)],
-                    wb_codes[:, first : first + P // 2].bitcast(FP4X4),
-                    packed_plane(BACK, a, t),
-                    a,
-                    P * j,
-                    P * (j + 1),
-                    start=(a == 0 and t == 0),
-                    stop=(a == PASSES - 1 and t == SLOTS - 1),
-                )
+        def back_pass(dst, a, t, lo, hi, start, stop):
+            first = (PASSES * t + a) * P // 2
+            product(dst, wb_codes[:, first : first + P // 2].bitcast(FP4X4), packed_plane(BACK, a, t), a, lo, hi, start, stop)
 
-        def copy_background(j):
-            if j in BACK_COPY_AT:
-                back_copy[j] = at(f"back_copy{j}", BACK_COPY_AT[j], [P, P, SLOTS], F32)
-            else:
-                back_copy[j] = kept(f"back_copy{j}", [P, P, SLOTS], F32)
-            nc.scalar.copy(back_copy[j][:], back_sum[j][:].rearrange("p (t n) -> p n t", t=SLOTS))
+        def span_pass(a, j, u):
+            for s in range(2):
+                dst = span_sum[j, u][:, CHUNK * s : CHUNK * (s + 1)]
+                back_pass(dst, a, 2 * u + s, P * j, P * j + CHUNK, a == 0 and s == 0, a == PASSES - 1 and s == 1)
+            if a == PASSES - 1:
+                nc.scalar.copy(span_copy[j][:, u], span_sum[j, u][:].rearrange("p (s n) -> p n s", s=2))
+
+        def background(j):
+            for a in range(PASSES):
+                for t in range(SLOTS):
+                    dst = back_sum[j][:, P * t : P * (t + 1)]
+                    back_pass(dst, a, t, P * j, P * (j + 1), a == 0 and t == 0, a == PASSES - 1 and t == SLOTS - 1)
 
         def taken(j):
-            if j in COPIED:
-                return back_copy[j][:]
-            return back_sum[j][:].rearrange("p (t n) -> p n t", t=SLOTS)
+            if j in WAITING:
+                return back_sum[j][:].rearrange("p (u s n) -> p n u s", u=2, s=2)
+            first = max(k for k in SPANS if k <= j)
+            return span_copy[first][:, :, P * (j - first) : P * (j - first + 1), :].rearrange("p u n s -> p n u s")
 
-        background(0, COPIED[0])
-        for index, j in enumerate(COPIED):
-            if index + 1 < len(COPIED):
-                background(0, COPIED[index + 1])
-            background(1, j)
-            copy_background(j)
-        for j in WAITING:
-            for a in range(PASSES):
-                background(a, j)
+        for a in range(PASSES):
+            for j in SPANS:
+                for u in range(2):
+                    span_pass(a, j, u)
+        for j in (0, 7, 3, 4):
+            background(j)
 
         wr_bf = {(a, u): kept(f"wr_bf{a}{u}", [P, 2 * H], BF16) for a in range(PASSES) for u in range(2)}
         wr_codes = {(a, u): kept(f"wr_codes{a}{u}", [P, 2 * P], U32) for a in range(PASSES) for u in range(2)}
@@ -342,20 +337,20 @@ def tile_list_kmer_locus_enrichment_kernel(
             summed = expo_sum[c, u][:].rearrange("p (s n) -> p n s", s=2)
             nc.vector.tensor_tensor(signal[c][:, u, lo:hi], summed[:, lo:hi], growth[c, u][:, lo:hi], ALU.mult)
 
-        def correct(c, halves=(0, 1)):
-            for half in halves:
-                engine = (nc.gpsimd, nc.vector)[half]
-                j = 2 * c + half
+        def correct(c):
+            for j in sorted((2 * c, 2 * c + 1), key=lambda tile: tile not in ON_GPSIMD):
+                engine = nc.gpsimd if j in ON_GPSIMD else nc.vector
+                half = j % 2
                 if c == 1:
                     h_bf[j] = at(f"h_bf{j}", H_BF_AT[j], [P, P * SLOTS], BF16)[:]
                 else:
-                    if half == 0:
+                    if c not in h_chunk:
                         h_chunk[c] = at(f"h_chunk{c}", H_CHUNK_AT[c], [P, CHUNK * SLOTS], BF16)
                     h_bf[j] = h_chunk[c][:, BANK * half : BANK * (half + 1)]
                 engine.tensor_tensor(
                     h_bf[j].rearrange("p (n u s) -> p n u s", u=2, s=2),
                     signal[c][:, :, P * half : P * (half + 1), :].rearrange("p u n s -> p n u s"),
-                    taken(j).rearrange("p n (u s) -> p n u s", u=2),
+                    taken(j),
                     ALU.subtract,
                 )
 
@@ -403,14 +398,14 @@ def tile_list_kmer_locus_enrichment_kernel(
 
         def rate_tile(j, index):
             summed = tile_sum("rate_tile", j, wr_operand, index)
-            growth[j] = at(f"growth_tile{j}", GROWTH_AT[j // 2, j % 2], [P, P, SLOTS], F32)
+            growth[j] = at(f"growth_tile{j}", GROWTH_AT[j // 2, int(j == LAST)], [P, P, SLOTS], F32)
             nc.scalar.activation(growth[j][:], summed, ACT.Exp)
 
         def exposure_tile(j, index):
             expo_sum[j] = tile_sum("expo_tile", j, we_operand, index)
 
         def grow_piece(j, lo, width):
-            signal[j, lo] = at(f"signal{j}_{lo}", PIECES_AT + 16 * (P * (j % 2) + lo), [P, width, SLOTS], F32)
+            signal[j, lo] = at(f"signal{j}_{lo}", PIECES_AT + 16 * (P * (j == LAST) + lo), [P, width, SLOTS], F32)
             nc.vector.tensor_tensor(
                 signal[j, lo][:], expo_sum[j][:, lo : lo + width], growth[j][:, lo : lo + width], ALU.mult
             )
@@ -419,8 +414,8 @@ def tile_list_kmer_locus_enrichment_kernel(
             if lo == 0:
                 h_bf[j] = at(f"h_bf{j}", H_BF_AT[j], [P, P * SLOTS], BF16)
             nc.vector.tensor_tensor(
-                h_bf[j][:, SLOTS * lo : SLOTS * (lo + width)].rearrange("p (n t) -> p n t", t=SLOTS),
-                signal[j, lo][:],
+                h_bf[j][:, SLOTS * lo : SLOTS * (lo + width)].rearrange("p (n u s) -> p n u s", u=2, s=2),
+                signal[j, lo][:].rearrange("p n (u s) -> p n u s", u=2),
                 taken(j)[:, lo : lo + width],
                 ALU.subtract,
             )
@@ -484,8 +479,8 @@ def tile_list_kmer_locus_enrichment_kernel(
         grow(0, 0)
         rate_pass(1, 1, 1)
         exposure(0, 1, 0)
-        grow(0, 1, P, CHUNK)
         grow(0, 1, 0, P)
+        grow(0, 1, P, CHUNK)
         rate(1, 0, 1)
         cast_wo(0, on_gpsimd=True)
         cast_wo(1)
@@ -507,7 +502,7 @@ def tile_list_kmer_locus_enrichment_kernel(
         grow(2, 1)
         quantise_chunk(1)
 
-        before_last, last = 2 * CHUNKS - 2, 2 * CHUNKS - 1
+        before_last, last = BEFORE_LAST, LAST
         rate_tile(before_last, 0)
         sums0 = read_chunk(0, (4, 5))
         for b in range(BLOCKS):

@@ -28,10 +28,10 @@ PIECE = 64
 EXPO, BACK = 0, 1
 PLANE_START = {EXPO: 4, BACK: 0}
 QUADRANTS = (0, 2, 1, 3)
-SPANS = (1, 5)
+SPAN = 1
 ON_GPSIMD = (1, 2, 5)
-WAITING = (0, 3, 4, 7)
-BEFORE_LAST, LAST = 7, 6
+WAITING = (0, 3, 4, 6)
+BEFORE_LAST, LAST = 6, 7
 HALF = S // 2
 TURN_BANKS = 4
 
@@ -160,7 +160,7 @@ def tile_list_kmer_locus_enrichment_kernel(
         gather_words(0, CHUNK, S)
         reorder(wb_codes[:], wb_raw[:], RUN // 2)
         reorder(w_planes[BACK][:], w_rows[BACK][:], RUN // 4)
-        for first, tiles in ((0, 3), (5, 3), (3, 2)):
+        for first, tiles in ((0, 3), (3, 3), (6, 2)):
             gather_words(1, P * first, P * (first + tiles))
         reorder(w_planes[EXPO][:], w_rows[EXPO][:], RUN // 4)
 
@@ -192,19 +192,21 @@ def tile_list_kmer_locus_enrichment_kernel(
             return w_planes[w][PLANE_START[w] :, first : first + P // 4].bitcast(U8)
 
         back_sum = {j: bank(f"back_sum{j}", TURN_BANKS + index) for index, j in enumerate(WAITING)}
-        span_sum = {(j, u): bank(f"span_sum{j}{u}", 2 * k + u) for k, j in enumerate(SPANS) for u in range(2)}
-        span_copy = {j: kept(f"span_copy{j}", [P, 2, CHUNK, 2], F32) for j in SPANS}
+        back_sum[5] = bank("back_sum5", 2)
+        span_sum = [bank(f"span_sum{u}", u) for u in range(2)]
+        span_copy = kept("span_copy", [P, 2, CHUNK, 2], F32)
+        tile_copy = kept("tile_copy", [P, P, SLOTS], F32)
 
         def back_pass(dst, a, t, lo, hi, start, stop):
             first = (PASSES * t + a) * P // 2
             product(dst, wb_codes[:, first : first + P // 2].bitcast(FP4X4), packed_plane(BACK, a, t), a, lo, hi, start, stop)
 
-        def span_pass(a, j, u):
+        def span_pass(a, u):
             for s in range(2):
-                dst = span_sum[j, u][:, CHUNK * s : CHUNK * (s + 1)]
-                back_pass(dst, a, 2 * u + s, P * j, P * j + CHUNK, a == 0 and s == 0, a == PASSES - 1 and s == 1)
+                dst = span_sum[u][:, CHUNK * s : CHUNK * (s + 1)]
+                back_pass(dst, a, 2 * u + s, P * SPAN, P * SPAN + CHUNK, a == 0 and s == 0, a == PASSES - 1 and s == 1)
             if a == PASSES - 1:
-                nc.scalar.copy(span_copy[j][:, u], span_sum[j, u][:].rearrange("p (s n) -> p n s", s=2))
+                nc.scalar.copy(span_copy[:, u], span_sum[u][:].rearrange("p (s n) -> p n s", s=2))
 
         def background(j):
             for a in range(PASSES):
@@ -213,16 +215,19 @@ def tile_list_kmer_locus_enrichment_kernel(
                     back_pass(dst, a, t, P * j, P * (j + 1), a == 0 and t == 0, a == PASSES - 1 and t == SLOTS - 1)
 
         def taken(j):
-            if j in WAITING:
-                return back_sum[j][:].rearrange("p (u s n) -> p n u s", u=2, s=2)
-            first = max(k for k in SPANS if k <= j)
-            return span_copy[first][:, :, P * (j - first) : P * (j - first + 1), :].rearrange("p u n s -> p n u s")
+            if j in (SPAN, SPAN + 1):
+                return span_copy[:, :, P * (j - SPAN) : P * (j - SPAN + 1), :].rearrange("p u n s -> p n u s")
+            if j == 5:
+                return tile_copy[:].rearrange("p n (u s) -> p n u s", u=2)
+            return back_sum[j][:].rearrange("p (u s n) -> p n u s", u=2, s=2)
 
         for a in range(PASSES):
-            for j in SPANS:
-                for u in range(2):
-                    span_pass(a, j, u)
-        for j in (0, 7, 3, 4):
+            for u in range(2):
+                span_pass(a, u)
+        background(0)
+        background(5)
+        nc.scalar.copy(tile_copy[:], back_sum[5][:].rearrange("p (t n) -> p n t", t=SLOTS))
+        for j in WAITING[1:]:
             background(j)
 
         wr_bf = {(a, u): kept(f"wr_bf{a}{u}", [P, 2 * H], BF16) for a in range(PASSES) for u in range(2)}
@@ -516,6 +521,8 @@ def tile_list_kmer_locus_enrichment_kernel(
         for b in range(BLOCKS):
             finish_block(1, sums1, b)
         exposure_tile(last, 3)
+        back_sum[last] = bank("back_sum_last", 4)
+        background(last)
         for lo in (0, PIECE):
             correct_piece(before_last, lo, PIECE)
         quantise_chunk(2)

from contextlib import ExitStack

import concourse.mybir as mybir

K, T, S, H, N = 1024, 2048, 1024, 512, 384
FLOPS = 3 * 2 * K * H * S + 2 * H * N * S

F32 = mybir.dt.float32
BF16 = mybir.dt.bfloat16
I32 = mybir.dt.int32
U32 = mybir.dt.uint32
U16 = mybir.dt.uint16
U8 = mybir.dt.uint8
FP8X4 = mybir.dt.float8_e4m3fn_x4
FP4X4 = mybir.dt.float4_e2m1fn_x4
ALU = mybir.AluOpType
ACT = mybir.ActivationFunctionType

P = 128
PASSES = K // 512
SLOTS = 4
RUN = 8
CHUNK = 2 * P
CHUNKS = S // CHUNK
BANK = 512
BLOCKS = N // P
PIECE = 64
EXPO, BACK = 0, 1
PLANE_START = {EXPO: 4, BACK: 0}
QUADRANTS = (0, 2, 1, 3)
SPAN = 1
ON_GPSIMD = (1, 2, 5)
WAITING = (0, 3, 4, 6)
BEFORE_LAST, LAST = 6, 7
HALF = S // 2
TURN_BANKS = 4

LINK = 64
ROOM = 8192
GROWTH_BYTES = 4 * BANK
BF_BYTES = 2 * BANK
GROWTH_AT = {(c, u): ROOM * (1 + 2 * c + u) for c in range(CHUNKS) for u in range(2)}
FREE_AT = ROOM * (1 + 2 * CHUNKS)
NEXT_GROWTH = (GROWTH_AT[1, 1], GROWTH_AT[2, 0], GROWTH_AT[3, 0])
H_CODES_AT = [first - 4 * CHUNK + LINK for first in NEXT_GROWTH]
WO_CODES_AT = [NEXT_GROWTH[0] + LINK + 4 * P * b for b in range(BLOCKS)]
WO_BF_AT = (FREE_AT + 2 * ROOM, GROWTH_AT[0, 1] - BF_BYTES + LINK, GROWTH_AT[0, 1] + GROWTH_BYTES - LINK)
H_BF_AT = {
    0: FREE_AT,
    1: WO_BF_AT[1] - 2 * (BF_BYTES - LINK),
    2: WO_BF_AT[1] - (BF_BYTES - LINK),
    3: FREE_AT + BF_BYTES,
    4: WO_BF_AT[1] - (BF_BYTES - LINK) + LINK,
    5: FREE_AT + 3 * BF_BYTES,
    6: FREE_AT + 4 * BF_BYTES,
    7: FREE_AT + 3 * ROOM,
}
H_CHUNK_AT = {0: FREE_AT + 5 * BF_BYTES, 2: H_BF_AT[2] - BF_BYTES}
PIECES_AT = FREE_AT + 4 * ROOM
STAGED6_AT = PIECES_AT + 16 * CHUNK - LINK


def tile_list_kmer_locus_enrichment_kernel(
    tc, tab_words, tab_scales, offs, wr, we_words, we_scales, wb_words, wb_scales, wo, bo, out
):
    nc = tc.nc
    with ExitStack() as ctx:
        keep = ctx.enter_context(tc.tile_pool(name="keep", bufs=1))
        placed = ctx.enter_context(tc.tile_pool(name="placed", bufs=1))
        psum = ctx.enter_context(tc.psum_pool(name="psum", bufs=1))

        def bank(name, index):
            return psum.tile([P, BANK], F32, name=name, offset=4 * BANK * index)

        def kept(name, shape, dtype):
            return keep.tile(shape, dtype, name=name, align_bytes=64)

        def streamed(name, shape, dtype):
            return keep.tile(shape, dtype, name=name, align_bytes=256)

        def at(name, offset, shape, dtype):
            return placed.tile(shape, dtype, name=name, offset=offset, align_bytes=64)

        offsets = keep.tile([P, S // 16], U16, name="offsets")
        nc.sync.dma_start(offsets[:], offs)

        scale_window = streamed("scale_window", [P, T // 4], I32)
        v_rows = kept("v_rows", [P, S], U8)
        v_planes = kept("v_planes", [P, PASSES * S // 4], I32)
        w_rows = {w: kept(f"w_rows{w}", [P, PASSES * H // 4], I32) for w in (EXPO, BACK)}
        nc.sync.dma_start(out=scale_window[0:32, :], in_=tab_scales.rearrange("a r t -> r a t").bitcast(I32))
        nc.gpsimd.memset(w_rows[BACK][:], 0)
        nc.gpsimd.memset(w_rows[EXPO][:], 0)
        nc.vector.memset(scale_window[32:64, :], 0)
        nc.vector.memset(scale_window[64:128, :], 0)
        nc.vector.memset(v_planes[:], 0)
        wb_raw = streamed("wb_raw", [P, PASSES * H // 2], I32)

        def load_scales(w, scales, quadrants):
            for q in quadrants:
                row = 32 * q + PLANE_START[w]
                nc.sync.dma_start(
                    out=w_rows[w][row : row + 4, :],
                    in_=scales[:, 4 * q : 4 * q + 4, :].rearrange("a r c -> r a c").bitcast(I32),
                )

        word_window = [streamed(f"word_window{a}", [P, T], I32) for a in range(PASSES)]

        def load_table(a):
            nc.sync.dma_start(out=word_window[a][:], in_=tab_words[a].rearrange("p t i -> p (t i)").bitcast(I32))

        load_table(0)
        nc.sync.dma_start(
            out=wb_raw[:].rearrange("p (a c) -> p a c", a=PASSES), in_=wb_words.rearrange("a p c -> p a c").bitcast(I32)
        )
        load_scales(BACK, wb_scales, QUADRANTS)
        load_table(1)
        load_scales(EXPO, we_scales, QUADRANTS[:2])

        nc.vector.tensor_copy(v_rows[:], scale_window[:].bitcast(U8).indirect(offsets[:]))
        for q in QUADRANTS:
            nc.sync.dma_start(out=v_planes[32 * q : 32 * q + 4, :], in_=v_rows[8 * q : 8 * q + 8, :].bitcast(I32))

        wr_raw = [streamed(f"wr_raw{a}", [P, 4 * H], F32) for a in range(PASSES)]

        def load_wr(a):
            nc.sync.dma_start(out=wr_raw[a][:], in_=wr[512 * a : 512 * (a + 1), :].rearrange("(p i) c -> p (i c)", i=4))

        load_wr(0)
        load_scales(EXPO, we_scales, QUADRANTS[2:])
        load_wr(1)
        we_raw = streamed("we_raw", [P, PASSES * H], I32)
        wo_raw = streamed("wo_raw", [P, SLOTS, N], F32)
        bias = kept("bias", [P, BLOCKS], F32)
        nc.sync.dma_start(
            out=we_raw[:].rearrange("p (a c) -> p a c", a=PASSES),
            in_=we_words.rearrange("a p c i -> p a (c i)").bitcast(I32),
        )
        for t in range(SLOTS):
            nc.sync.dma_start(out=wo_raw[:, t, :], in_=wo.rearrange("(g t e) n -> t g e n", t=SLOTS, e=RUN)[t])
        with nc.allow_non_contiguous_dma(reason="one bias value a partition"):
            nc.sync.dma_start(out=bias[:], in_=bo.rearrange("(b p) -> p b", p=P))

        def reorder(dst, src, run):
            nc.scalar.copy(
                dst.bitcast(U32).rearrange("p (t x e) -> p t x e", t=SLOTS, e=run),
                src.bitcast(U32).rearrange("p (x t e) -> p t x e", t=SLOTS, e=run),
            )

        wb_codes = kept("wb_codes", [P, PASSES * H // 2], I32)
        w_planes = {w: kept(f"w_planes{w}", [P, PASSES * H // 4], I32) for w in (EXPO, BACK)}
        v_codes = [kept(f"v_codes{a}", [P, S], U32) for a in range(PASSES)]

        def gather_words(a, lo, hi):
            nc.vector.tensor_copy(
                v_codes[a][:, lo:hi], word_window[a][:].bitcast(U32).indirect(offsets[:, lo // 16 : hi // 16])
            )

        gather_words(0, 0, CHUNK)
        gather_words(0, CHUNK, S)
        reorder(wb_codes[:], wb_raw[:], RUN // 2)
        reorder(w_planes[BACK][:], w_rows[BACK][:], RUN // 4)
        for first, tiles in ((0, 3), (3, 3), (6, 2)):
            gather_words(1, P * first, P * (first + tiles))
        reorder(w_planes[EXPO][:], w_rows[EXPO][:], RUN // 4)

        def product(dst, codes, scales, a, lo, hi, start, stop):
            nc.tensor.matmul_mx(
                out=dst,
                lhsT=codes,
                lhsT_scale=scales,
                rhs=v_codes[a][:, lo:hi].bitcast(FP8X4),
                rhs_scale=v_planes[:, (S * a + lo) // 4 : (S * a + hi) // 4].bitcast(U8),
                start=start,
                stop=stop,
            )

        warm = bank("warm", 3)
        for repeat in range(5):
            nc.tensor.matmul_mx(
                out=warm[:],
                lhsT=v_codes[0][:, 0:P].bitcast(FP8X4),
                lhsT_scale=v_rows[:, 0:P],
                rhs=word_window[0][:, 0:BANK].bitcast(FP8X4),
                rhs_scale=v_rows[:, 0:BANK],
                start=True,
                stop=True,
            )

        def packed_plane(w, a, t):
            first = (PASSES * t + a) * P // 4
            return w_planes[w][PLANE_START[w] :, first : first + P // 4].bitcast(U8)

        back_sum = {j: bank(f"back_sum{j}", TURN_BANKS + index) for index, j in enumerate(WAITING)}
        back_sum[5] = bank("back_sum5", 2)
        span_sum = [bank(f"span_sum{u}", u) for u in range(2)]
        span_copy = kept("span_copy", [P, 2, CHUNK, 2], F32)
        tile_copy = kept("tile_copy", [P, P, SLOTS], F32)

        def back_pass(dst, a, t, lo, hi, start, stop):
            first = (PASSES * t + a) * P // 2
            product(dst, wb_codes[:, first : first + P // 2].bitcast(FP4X4), packed_plane(BACK, a, t), a, lo, hi, start, stop)

        def span_pass(a, u):
            for s in range(2):
                dst = span_sum[u][:, CHUNK * s : CHUNK * (s + 1)]
                back_pass(dst, a, 2 * u + s, P * SPAN, P * SPAN + CHUNK, a == 0 and s == 0, a == PASSES - 1 and s == 1)
            if a == PASSES - 1:
                nc.scalar.copy(span_copy[:, u], span_sum[u][:].rearrange("p (s n) -> p n s", s=2))

        def background(j):
            for a in range(PASSES):
                for t in range(SLOTS):
                    dst = back_sum[j][:, P * t : P * (t + 1)]
                    back_pass(dst, a, t, P * j, P * (j + 1), a == 0 and t == 0, a == PASSES - 1 and t == SLOTS - 1)

        def taken(j):
            if j in (SPAN, SPAN + 1):
                return span_copy[:, :, P * (j - SPAN) : P * (j - SPAN + 1), :].rearrange("p u n s -> p n u s")
            if j == 5:
                return tile_copy[:].rearrange("p n (u s) -> p n u s", u=2)
            return back_sum[j][:].rearrange("p (u s n) -> p n u s", u=2, s=2)

        for a in range(PASSES):
            for u in range(2):
                span_pass(a, u)
        background(0)
        background(5)
        nc.scalar.copy(tile_copy[:], back_sum[5][:].rearrange("p (t n) -> p n t", t=SLOTS))
        for j in WAITING[1:]:
            background(j)

        wr_bf = {(a, u): kept(f"wr_bf{a}{u}", [P, 2 * H], BF16) for a in range(PASSES) for u in range(2)}
        wr_codes = {(a, u): kept(f"wr_codes{a}{u}", [P, 2 * P], U32) for a in range(PASSES) for u in range(2)}
        wr_planes = [kept(f"wr_planes{a}", [P, H], U8) for a in range(PASSES)]

        def wr_slots(a):
            return wr_raw[a][:].rearrange("p (i g t e) -> p t g e i", i=4, t=SLOTS, e=RUN)

        def cast_pair(a, u):
            nc.vector.tensor_copy(
                wr_bf[a, u][:].rearrange("p (t g e i) -> p t g e i", t=2, e=RUN, i=4), wr_slots(a)[:, 2 * u : 2 * u + 2]
            )

        def cast_slot(a, t, engine_copy):
            engine_copy(
                wr_bf[a, t // 2][:, H * (t % 2) : H * (t % 2 + 1)].rearrange("p (g e i) -> p g e i", e=RUN, i=4),
                wr_slots(a)[:, t],
            )

        def quantise_wr(a, u):
            nc.vector.quantize_mx(
                out=wr_codes[a, u][:].bitcast(FP8X4),
                scales=wr_planes[a][:, 2 * P * u : 2 * P * (u + 1)],
                in_=wr_bf[a, u][:],
            )

        for u in (1, 0):
            cast_pair(0, u)
        for u in (1, 0):
            quantise_wr(0, u)
        we_codes = kept("we_codes", [P, PASSES * H], I32)

        def quantise_slot(t):
            nc.vector.quantize_mx(
                out=wr_codes[1, t // 2][:, P * (t % 2) : P * (t % 2 + 1)].bitcast(FP8X4),
                scales=wr_planes[1][:, P * t : P * (t + 1)],
                in_=wr_bf[1, t // 2][:, H * (t % 2) : H * (t % 2 + 1)],
            )

        def reorder_we(u):
            nc.vector.tensor_copy(
                we_codes[:, H * u : H * (u + 1)].rearrange("p (t x e) -> p t x e", t=2, e=RUN),
                we_raw[:].rearrange("p (x t e) -> p t x e", t=SLOTS, e=RUN)[:, 2 * u : 2 * u + 2],
            )

        for t in range(SLOTS):
            cast_slot(1, t, nc.vector.tensor_copy if t < 2 else nc.scalar.copy)
        for t in range(SLOTS - 1):
            quantise_slot(t)
        reorder_we(0)
        quantise_slot(SLOTS - 1)
        reorder_we(1)

        def wr_operand(a, t):
            codes = wr_codes[a, t // 2][:, P * (t % 2) : P * (t % 2 + 1)].bitcast(FP8X4)
            return codes, wr_planes[a][:, P * t : P * (t + 1)]

        def we_operand(a, t):
            first = (PASSES * t + a) * P
            return we_codes[:, first : first + P].bitcast(FP8X4), packed_plane(EXPO, a, t)

        rate_sum = {}
        expo_sum = {}
        growth = {}
        signal = {}
        h_bf = {}
        h_chunk = {}
        h_mx = {}
        wo_bf = {}
        wo_codes = {}
        wo_plane = kept("wo_plane", [P, N], U8)

        def rate_pass(a, c, u, index=None):
            if a == 0:
                rate_sum[c, u] = bank(f"rate{c}{u}", index)
            for s in range(2):
                product(
                    rate_sum[c, u][:, CHUNK * s : CHUNK * (s + 1)],
                    *wr_operand(a, 2 * u + s),
                    a,
                    CHUNK * c,
                    CHUNK * (c + 1),
                    start=(a == 0 and s == 0),
                    stop=(a == PASSES - 1 and s == 1),
                )
            if a == PASSES - 1:
                growth[c, u] = at(f"growth{c}{u}", GROWTH_AT[c, u], [P, CHUNK, 2], F32)
                nc.scalar.activation(growth[c, u][:], rate_sum[c, u][:].rearrange("p (s n) -> p n s", s=2), ACT.Exp)

        def rate(c, u, index):
            for a in range(PASSES):
                rate_pass(a, c, u, index)

        def exposure(c, u, index):
            if c not in signal:
                signal[c] = kept(f"signal{c}", [P, 2, CHUNK, 2], F32)
            acc = expo_sum[c, u] = bank(f"expo{c}{u}", index)
            for s in range(2):
                for a in range(PASSES):
                    product(
                        acc[:, CHUNK * s : CHUNK * (s + 1)],
                        *we_operand(a, 2 * u + s),
                        a,
                        CHUNK * c,
                        CHUNK * (c + 1),
                        start=(a == 0),
                        stop=(a == PASSES - 1),
                    )

        def grow(c, u, lo=0, hi=CHUNK):
            summed = expo_sum[c, u][:].rearrange("p (s n) -> p n s", s=2)
            nc.vector.tensor_tensor(signal[c][:, u, lo:hi], summed[:, lo:hi], growth[c, u][:, lo:hi], ALU.mult)

        def correct(c):
            for j in sorted((2 * c, 2 * c + 1), key=lambda tile: tile not in ON_GPSIMD):
                engine = nc.gpsimd if j in ON_GPSIMD else nc.vector
                half = j % 2
                if c == 1:
                    h_bf[j] = at(f"h_bf{j}", H_BF_AT[j], [P, P * SLOTS], BF16)[:]
                else:
                    if c not in h_chunk:
                        h_chunk[c] = at(f"h_chunk{c}", H_CHUNK_AT[c], [P, CHUNK * SLOTS], BF16)
                    h_bf[j] = h_chunk[c][:, BANK * half : BANK * (half + 1)]
                engine.tensor_tensor(
                    h_bf[j].rearrange("p (n u s) -> p n u s", u=2, s=2),
                    signal[c][:, :, P * half : P * (half + 1), :].rearrange("p u n s -> p n u s"),
                    taken(j),
                    ALU.subtract,
                )

        def quantise_chunk(c):
            codes = at(f"h_codes{c}", H_CODES_AT[c], [P, CHUNK], U32)
            plane = kept(f"h_plane{c}", [P, CHUNK], U8)
            if c == 1:
                for half in range(2):
                    cols = slice(P * half, P * (half + 1))
                    nc.vector.quantize_mx(out=codes[:, cols].bitcast(FP8X4), scales=plane[:, cols], in_=h_bf[2 * c + half])
            else:
                nc.vector.quantize_mx(out=codes[:].bitcast(FP8X4), scales=plane[:], in_=h_chunk[c][:])
            h_mx[CHUNK * c] = (codes, plane)

        def cast_wo(b, on_gpsimd=False):
            wo_bf[b] = at(f"wo_bf{b}", WO_BF_AT[b], [P, P, SLOTS], BF16)
            rows = wo_raw[:, :, P * b : P * (b + 1)].rearrange("p t n -> p n t")
            if on_gpsimd:
                nc.gpsimd.tensor_scalar(wo_bf[b][:], rows, 1.0, 0.0, ALU.mult, ALU.add)
            else:
                nc.scalar.copy(wo_bf[b][:], rows)

        def quantise_wo(b):
            wo_codes[b] = at(f"wo_codes{b}", WO_CODES_AT[b], [P, P], U32)
            nc.vector.quantize_mx(
                out=wo_codes[b][:].bitcast(FP8X4),
                scales=wo_plane[:, P * b : P * (b + 1)],
                in_=wo_bf[b][:].rearrange("p n t -> p (n t)"),
            )

        def tile_sum(name, j, operand, index):
            acc = bank(f"{name}{j}", index)
            for a in range(PASSES):
                for t in range(SLOTS):
                    product(
                        acc[:, P * t : P * (t + 1)],
                        *operand(a, t),
                        a,
                        P * j,
                        P * (j + 1),
                        start=(a == 0 and t == 0),
                        stop=(a == PASSES - 1 and t == SLOTS - 1),
                    )
            return acc[:].rearrange("p (t n) -> p n t", t=SLOTS)

        def rate_tile(j, index):
            summed = tile_sum("rate_tile", j, wr_operand, index)
            growth[j] = at(f"growth_tile{j}", GROWTH_AT[j // 2, int(j == LAST)], [P, P, SLOTS], F32)
            nc.scalar.activation(growth[j][:], summed, ACT.Exp)

        def exposure_tile(j, index):
            expo_sum[j] = tile_sum("expo_tile", j, we_operand, index)

        def grow_piece(j, lo, width):
            signal[j, lo] = at(f"signal{j}_{lo}", PIECES_AT + 16 * (P * (j == LAST) + lo), [P, width, SLOTS], F32)
            nc.vector.tensor_tensor(
                signal[j, lo][:], expo_sum[j][:, lo : lo + width], growth[j][:, lo : lo + width], ALU.mult
            )

        def correct_piece(j, lo, width):
            if lo == 0:
                h_bf[j] = at(f"h_bf{j}", H_BF_AT[j], [P, P * SLOTS], BF16)
            nc.vector.tensor_tensor(
                h_bf[j][:, SLOTS * lo : SLOTS * (lo + width)].rearrange("p (n u s) -> p n u s", u=2, s=2),
                signal[j, lo][:].rearrange("p n (u s) -> p n u s", u=2),
                taken(j)[:, lo : lo + width],
                ALU.subtract,
            )

        def quantise_piece(j, lo, width):
            codes = kept(f"h_codes{j}_{lo}", [P, width], U32)
            plane = kept(f"h_plane{j}_{lo}", [P, width], U8)
            nc.vector.quantize_mx(out=codes[:].bitcast(FP8X4), scales=plane[:], in_=h_bf[j][:, SLOTS * lo : SLOTS * (lo + width)])
            h_mx[P * j + lo] = (codes, plane)

        def read_out(first, width, banks):
            codes, plane = h_mx[first]
            per_bank = min(BLOCKS, BANK // width)
            accs = [bank(f"sum{first}_{index}", index) for index in banks]
            sums = [accs[b // per_bank][:, width * (b % per_bank) : width * (b % per_bank + 1)] for b in range(BLOCKS)]
            for b in range(BLOCKS):
                nc.tensor.matmul_mx(
                    out=sums[b],
                    lhsT=wo_codes[b][:].bitcast(FP8X4),
                    lhsT_scale=wo_plane[:, P * b : P * (b + 1)],
                    rhs=codes[:].bitcast(FP8X4),
                    rhs_scale=plane[:],
                    start=True,
                    stop=True,
                )
            return accs, sums

        def store_blocks(first, staged):
            width = staged.shape[2]
            nc.sync.dma_start(out=out[:, first : first + width].rearrange("(b p) j -> p b j", p=P), in_=staged[:])

        def finish_on_scalar(first, width, banks):
            staged = kept(f"staged{first}", [P, BLOCKS, width], F32)
            sums = read_out(first, width, banks)[1]
            for b in range(BLOCKS):
                nc.scalar.activation(staged[:, b, :], sums[b], ACT.Identity, bias=bias[:, b : b + 1])
            return staged

        def read_chunk(c, banks):
            return streamed(f"staged{c}", [P, BLOCKS, CHUNK], F32), read_out(CHUNK * c, CHUNK, banks)[1]

        def finish_block(c, read, b):
            staged, sums = read
            nc.scalar.activation(staged[:, b, :], sums[b], ACT.Identity, bias=bias[:, b : b + 1])
            nc.sync.dma_start(out=out[P * b : P * (b + 1), CHUNK * c : CHUNK * (c + 1)], in_=staged[:, b, :])

        def add_bias(acc, width, dst):
            nc.vector.tensor_tensor(
                dst,
                acc[:, 0 : BLOCKS * width].rearrange("p (b j) -> p b j", b=BLOCKS),
                bias[:].unsqueeze(2).to_broadcast([P, BLOCKS, width]),
                ALU.add,
            )

        rate_pass(0, 0, 0, 0)
        rate_pass(0, 0, 1, 1)
        rate_pass(0, 1, 1, 2)
        rate_pass(1, 0, 0)
        rate_pass(1, 0, 1)
        exposure(0, 0, 3)
        grow(0, 0)
        rate_pass(1, 1, 1)
        exposure(0, 1, 0)
        grow(0, 1, 0, P)
        grow(0, 1, P, CHUNK)
        rate(1, 0, 1)
        cast_wo(0, on_gpsimd=True)
        cast_wo(1)
        correct(0)
        exposure(1, 1, 2)
        grow(1, 1)
        exposure(1, 0, 3)
        grow(1, 0)
        cast_wo(2)
        quantise_chunk(0)
        for b in range(BLOCKS):
            quantise_wo(b)
        rate(2, 0, 0)
        rate(2, 1, 1)
        correct(1)
        exposure(2, 0, 2)
        grow(2, 0)
        exposure(2, 1, 3)
        grow(2, 1)
        quantise_chunk(1)

        before_last, last = BEFORE_LAST, LAST
        rate_tile(before_last, 0)
        sums0 = read_chunk(0, (4, 5))
        for b in range(BLOCKS):
            finish_block(0, sums0, b)
        correct(2)
        exposure_tile(before_last, 1)
        rate_tile(last, 2)
        for lo in (0, PIECE):
            grow_piece(before_last, lo, PIECE)
        sums1 = read_chunk(1, (0, 6))
        for b in range(BLOCKS):
            finish_block(1, sums1, b)
        exposure_tile(last, 3)
        back_sum[last] = bank("back_sum_last", 4)
        background(last)
        for lo in (0, PIECE):
            correct_piece(before_last, lo, PIECE)
        quantise_chunk(2)
        sums2 = read_chunk(2, (5, 2))
        for b in range(BLOCKS):
            finish_block(2, sums2, b)
        grow_piece(last, 0, PIECE)
        quantise_piece(before_last, 0, P)
        grow_piece(last, PIECE, PIECE)
        sum6 = read_out(P * before_last, P, (1,))[0][0]
        for lo in (0, PIECE):
            correct_piece(last, lo, PIECE)
        staged_last = streamed("staged_last", [P, BLOCKS, P], F32)
        for lo in (0, PIECE):
            quantise_piece(last, lo, PIECE)
        staged6 = at("staged6", STAGED6_AT, [P, BLOCKS, P], F32)
        add_bias(sum6, P, staged6[:])
        store_blocks(P * before_last, staged6)
        for index, lo in ((7, 0), (3, PIECE)):
            add_bias(read_out(P * last + lo, PIECE, (index,))[0][0], PIECE, staged_last[:, :, lo : lo + PIECE])
        store_blocks(P * last, staged_last)
